import numpy as np, ml_dtypes
CORES = [242,247,114,119]
N = 4
BF = ml_dtypes.bfloat16
V, K, H, G, W, Q, RO = 768, 1, 768, 512, 2304, 4, 3
AL = 0.125
def parts(rng):
    nm = np.where(rng.random((N, 8, V, 16)) < 0.4, rng.integers(0, V, (N, 8, V, 16)), rng.integers(0, W, (N, 8, V, 16)))
    dl = rng.integers(0, 1024, (N, 8, V, 16)); ph = rng.integers(0, 1024, (N, 8, V)); rb = rng.integers(0, 1024, (N, 8, V))
    lo = np.exp2(rng.random((N, 8, V, 1)) + 3.0 * rng.random((N, 8, V, 16)) - 1.0)
    fa = 0.875 + 0.125 * rng.random((N, 8, V, 16))
    return nm, dl, ph, rb, lo, fa
def turn(x):
    return np.ascontiguousarray(x.transpose(0, 1, 3, 2)).reshape(N, 128, V)
def pack(nm, dl, ph, rb, lo, fa):
    return {"loud": turn(np.clip(lo, 0.5, 8.0)).astype(BF), "fade": turn(np.clip(fa, 0.875, 1.0)).astype(BF), "ph0": ph.astype(np.int32), "rb": rb.astype(np.int32),
            "nb": turn(nm + 4096 * dl).astype(np.int32)}
def setup_inputs(rng):
    return pack(*parts(rng))
def newl(way, l, x, f):
    if way == 1: l, x, f = l.astype(np.float64), x.astype(np.float64), f.astype(np.float64)
    if way == 2: return (np.float32(1.0 - AL) * l + np.float32(AL) * x) * f
    if way == 3: return l * f + (np.float32(AL) * (x - l)) * f
    v = (l + np.float32(AL) * (x - l)) * f
    if way == 4: v = (np.rint(v.astype(np.float64) * 2.0 ** 21) * 2.0 ** -21).astype(np.float32)
    return v
def rivals(rng):
    n = 2 ** 18
    def some(low, high):
        return (low + (high - low) * rng.random(n)).astype(BF).astype(np.float32)
    z, fz, y, fy, a, fa = some(0.5, 1.0), some(0.875, 1.0), some(0.5, 1.0), some(0.875, 1.0), some(4.5, 7.5), some(0.875, 1.0)
    val = []
    for way in range(5):
        z1 = newl(way, z, z, fz) if K > 1 else z
        val.append(newl(way, newl(way, a, y, fa), newl(way, y, z1, fy), fa))
    o = np.argsort(val[0]); i, j = o[:-1], o[1:]; same = val[0][i] == val[0][j]; kinds = []
    for way in range(1, 5):
        w = val[way]
        m = same & (w[i] != w[j]); b, c = i[m], j[m]; up = w[b] < w[c]
        kinds.append((np.where(up, b, c), np.where(up, c, b)))
        m = ~same & (w[j] <= w[i]); kinds.append((i[m], j[m]))
    kinds = [p for p in kinds if len(p[0]) > 0] or [(np.array([0]), np.array([1]))]
    return kinds, z, fz, y, fy, a, fa
def close(rng, nm, dl, ph, rb, lo, fa):
    kinds, z, fz, y, fy, a, ff = rivals(rng)
    ix = np.zeros((N, 8, 32, 16), np.int64)
    for s in range(16):
        first, second = kinds[s % len(kinds)]; c = rng.integers(0, len(first), (N, 8, 16))
        ix[:, :, s] = first[c]; ix[:, :, 16 + s] = second[c]
    d = int(rng.integers(1, N)); e = int(rng.integers(1, N))
    tw = K * np.arange(32); zs = K * (32 + np.arange(32)); ys = K * (np.arange(32) + (64 if K == 1 else 0)) + K - 1
    ju = K * (H - 1 - np.arange(64)) + (RO - 1) % K
    iy = np.roll(ix, (-d, 1), axis=(0, 1)); iz = np.roll(iy, (-e, 1), axis=(0, 1))
    lo[:, :, tw] = a[ix]; fa[:, :, tw] = ff[ix]
    lo[:, :, ys] = y[iy]; fa[:, :, ys] = fy[iy]
    lo[:, :, zs] = z[iz]; fa[:, :, zs] = fz[iz]
    nm[:, :, tw] = (V + (d - 1) * G + ys)[:, None]
    nm[:, :, ys] = (V + (e - 1) * G + zs)[:, None]
    nm[:, :, zs] = zs[:, None]
    st = np.arange(64) % 16; blk = rng.integers(0, N, (N, 8, 64, 1)); cut = rng.integers(2, 16, (N, 8, 64, 1)); k = np.arange(16)
    base = np.where(blk == 0, 0, V + (blk - 1) * G)
    pair = base + np.where(k < cut, tw[st][:, None], tw[16 + st][:, None])
    nm[:, :, ju] = np.where(k == 0, (V + (d - 1) * G + ys[st])[:, None], pair)
    every = np.concatenate([tw, ys, zs, ju]); wait = rng.integers(0, 1024, (N, 8, len(every)))
    dl[:, :, every] = wait[..., None]; rb[:, :, every] = (-wait) & 1023; ph[:, :, every] = int(rng.integers(0, 1024))
def setup_inputs_spread(rng):
    nm, dl, ph, rb, lo, fa = parts(rng)
    nm = np.where(rng.random(nm.shape) < 0.5, nm, np.minimum((W * rng.random(nm.shape) ** 3).astype(np.int64), W - 1))
    dl = np.minimum(np.exp2(10 * rng.random(dl.shape)).astype(np.int64), 1024) - 1
    ph = np.minimum(np.exp2(10 * rng.random(ph.shape)).astype(np.int64), 1023)
    rb = np.minimum((1024 * rng.random(rb.shape) ** 2).astype(np.int64), 1023)
    lo = 2.0 * np.exp2(rng.integers(-1, 2, (N, 8, V, 1))) * np.exp2(2.0 * rng.random(lo.shape) - 1.0)
    fa = np.where(rng.random(fa.shape) < 0.5, fa, 1.0)
    close(rng, nm, dl, ph, rb, lo, fa)
    return pack(nm, dl, ph, rb, lo, fa)
def setup_inputs_ends(rng):
    nm, dl, ph, rb, lo, fa = parts(rng)
    dl = np.where(rng.random(dl.shape) < 0.9, 1023 * rng.integers(0, 2, dl.shape), dl)
    u = rng.random(nm.shape); low, high = u < 0.35, u > 0.65
    nm = np.where(low, 0, np.where(high, W - 1, nm)); dl = np.where(low, 0, np.where(high, 1023, dl))
    ph = np.where(rng.random(ph.shape) < 0.9, 1023 * rng.integers(0, 2, ph.shape), ph); rb = np.where(rng.random(rb.shape) < 0.9, 1023 * rng.integers(0, 2, rb.shape), rb)
    lo = np.where(rng.random(lo.shape) < 0.75, np.where(rng.random(lo.shape) < 0.5, 0.5, 8.0), lo)
    fa = np.where(rng.random(fa.shape) < 0.8, np.where(rng.random(fa.shape) < 0.5, 0.875, 1.0), fa)
    ph[:, ::2, G - 1] = 0
    lad = V - 1 - K * np.arange(16, 0, -1); b = V - 1 - 17 * K
    lo[:, 3::4, lad] = (8.0 - 0.03125 * (15 - np.arange(16)))[:, None]
    ph[:, 3::4, lad] = 0; ph[:, 3::4, V - 1] = 0; ph[:, 3::4, b] = 0; rb[:, 3::4, V - 1] = 1023
    nm[:, 3::4, V - 1] = lad; dl[:, 3::4, V - 1] = 1008 + np.arange(16)
    nm[:, 3::4, b] = lad[15]; dl[:, 3::4, b] = 1023
    return pack(nm, dl, ph, rb, lo, fa)
def setup_inputs_crowd(rng):
    nm, dl, ph, rb, lo, fa = parts(rng)
    place = np.array([0, V - 1, V, W - 1]); one = np.arange(16)[None, None, :] == rng.integers(0, 16, (N, V, 1))
    nm[:, 0] = 0
    nm[:, 1] = np.where(one, nm[:, 1], W - 1)
    nm[:, 2] = rng.choice(place, (N, V, 1))
    nm[:, 3] = rng.choice(place, (N, V, 16)); dl[:, 3] = rng.choice(np.array([0, 1, 512, 1023]), (N, V, 16))
    nm[:, 4] = V - 1; dl[:, 4] = 1023
    nm[:, 5] = np.where(one, nm[:, 5], V - 1); dl[:, 5] = rng.integers(0, 1024, (N, V, 1))
    return pack(nm, dl, ph, rb, lo, fa)
def setup_inputs_bands(rng):
    nm, dl, ph, rb, lo, fa = parts(rng)
    lev = np.argsort(rng.random((N, 8, V, 16)), axis=3); nm = 16 * rng.integers(0, W // 16, (N, 8, V, 16)) + lev
    for g in (1, 4, 7): nm[:, g] = nm[:, g] % V
    way = rng.integers(0, 3, (N, 8, V, 1)); dl = np.where(way == 0, 64 * lev, np.where(way == 1, 64 * (15 - lev), rng.integers(0, 1024, (N, 8, V, 1))))
    ph[:] = rng.integers(0, 1024); o = rng.permutation(16); rise = 0.5 + 0.4375 * (np.arange(V) % 16)
    for g in range(8):
        n = (16, 16, Q, Q, Q, Q - 1, Q - 1, Q - 1)[g]
        lo[:, g] = 2.0
        for b in o[:n]: lo[:, g, :, b] = rise
    fa[:, 2:] = 1.0
    return pack(nm, dl, ph, rb, lo, fa)
def setup_inputs_calm(rng):
    nm, dl, ph, rb, lo, fa = parts(rng)
    for g in (1, 3): nm[:, g] = nm[:, g] % V
    d8 = np.array([8, 1023, 512, 3, 0, 1, 1023, 16])[None, :, None]; step = np.array([1, 0, 0, -1, 1, 1, 0, 1])[None, :, None]
    ph = rng.integers(0, 4, (N, 8, V)); ph[:, 0] = 0; ph[:, 4] = rng.integers(0, 2, (N, V)); ph[:, 2:4] = 1023 - rng.integers(0, 2, (N, 2, V))
    rb = (step * (rng.random((N, 8, V)) < 0.25) - d8) & 1023
    return pack(nm, np.zeros_like(dl) + d8[..., None], ph, rb, lo, fa)
def check_ranges(d):
    bad = []
    for k, lo, hi in (("loud", 0.5, 8.0), ("fade", 0.875, 1.0), ("ph0", 0, 1023), ("rb", 0, 1023), ("nb", 0, 4096 * 1023 + W - 1)):
        x = np.asarray(d[k], np.float64)
        if not (np.min(x) >= lo and np.max(x) <= hi): bad.append("range of " + k)
    if np.max(np.asarray(d["nb"]).astype(np.int64) & 4095) >= W: bad.append("a name in nb")
    return bad
def reference(loud, fade, ph0, rb, nb):
    L = np.ascontiguousarray(loud.astype(np.float32).reshape(N, 8, 16, V).transpose(0, 1, 3, 2))
    fd = np.ascontiguousarray(fade.astype(np.float32).reshape(N, 8, 16, V).transpose(0, 1, 3, 2))
    lst = np.ascontiguousarray(nb.astype(np.int64).reshape(N, 8, 16, V).transpose(0, 1, 3, 2))
    p = ph0.astype(np.int64); add = rb.astype(np.int64); E = np.zeros((N, 8, V, 16), np.float64)
    gi = np.arange(8)[:, None, None]; kk = np.arange(16)
    for t in range(RO):
        c = slice(t % K, V, K)
        L2, p2, lst2 = L.copy(), p.copy(), lst.copy()
        for r in range(N):
            wl = np.concatenate([L[r]] + [np.roll(L[(r - d) % N][:, :G], -1, axis=0) for d in range(1, N)], axis=1)
            wp = np.concatenate([p[r]] + [np.roll(p[(r - d) % N][:, :G], -1, axis=0) for d in range(1, N)], axis=1)
            mine = lst[r][:, c]
            nm = mine & 4095; a = (wp[gi, nm] + (mine >> 12) - p[r][:, c][:, :, None]) & 1023
            o = np.argsort(16 * a + kk, axis=2)
            nm = np.take_along_axis(nm, o, 2); a = np.take_along_axis(a, o, 2)
            x = wl[gi, nm]
            top = np.maximum.accumulate(x, axis=2); m = np.zeros_like(x); m[:, :, 1:] = top[:, :, :-1]
            free = np.count_nonzero(x > m, axis=3) >= Q
            xf = x[free].astype(np.float64); z = np.zeros(x.shape, np.float64)
            z[free] = xf * np.reciprocal(1.0 + np.exp(m[free].astype(np.float64) - xf))
            E[r][:, c] += np.add.reduce(z, axis=2)
            p2[r][:, c] = (p[r][:, c] + np.maximum.reduce(np.where(free, a, 0), axis=2) + add[r][:, c]) & 1023
            if t < RO - 1:
                own = L[r][:, c]; L2[r][:, c] = (own + np.float32(AL) * (top[:, :, 15] - own)) * fd[r][:, c]
            if t < RO - K:
                first = nm[:, :, 0]; got = lst[r][gi[:, :, 0], np.minimum(first, V - 1)]
                hid = np.zeros(free.shape, bool); np.put_along_axis(hid, o, ~free, 2)
                lst2[r][:, c] = np.where(hid & (first < V)[:, :, None], got, mine)
        L, p, lst = L2, p2, lst2
    return {"ye": np.ascontiguousarray(E.transpose(0, 1, 3, 2)).reshape(N, 128, V).astype(np.float32), "yp": np.asarray(p, np.float32)}

def check_inputs(d):
    bad = list(check_ranges(d))
    if not bad:
        for name, y in reference(**d).items():
            for q in range(N):
                v = np.abs(np.asarray(y[q], np.float64)); s = np.sqrt(np.mean(v * v))
                if v.max() > 6 * s or s < 2.0 ** 2: bad.append('%s of rank %d is uneven or too small' % (name, q))
    return bad

@@ -1,0 +1,826 @@
+import math
+import numpy as np
+from concourse.bass import DstId, RemoteDMATransfer
+from concourse.mybir import AluOpType, ActivationFunctionType
+
+ALU, ACTF = AluOpType, ActivationFunctionType
+V, GH, NR, RO = 768, 512, 4, 3
+CW, NCH = 24, 2
+U = 16 * CW
+PAD = 8
+WW = PAD + V + 3 * GH
+WP = PAD + V + 2 * GH + V
+f32, bf, i32, u16 = "float32", "bfloat16", "int32", "uint16"
+
+SCRATCH = {
+    "nbT": ("sbuf", [128, 16, 48], i32), "nbN": ("sbuf", [128, V], i32),
+    "lT0": ("sbuf", [128, 16, 48], f32), "lT1": ("sbuf", [128, 16, 48], f32),
+    "lN0": ("sbuf", [128, V], f32), "lN1": ("sbuf", [128, V], f32),
+    "W0": ("sbuf", [128, WW], bf), "W1": ("sbuf", [128, WW], f32), "W2": ("sbuf", [128, WW], f32),
+    "Ls0": ("sbuf", [128, GH], bf), "Ls1": ("sbuf", [128, GH], f32), "Ls2": ("sbuf", [128, GH], f32),
+    "fad": ("sbuf", [128, V], bf), "Wp": ("sbuf", [128, WP], bf),
+    "Yb": ("sbuf", [128, RO, 192], bf), "land": ("sbuf", [128, 3 * RO, 96], bf),
+    "ph": ("sbuf", [128, 48], i32), "phb": ("sbuf", [128, 96], bf), "rbi": ("sbuf", [128, 48], i32),
+    "pr": ("sbuf", [128, 48], i32), "ti": ("sbuf", [128, 48], i32), "tj": ("sbuf", [128, 48], i32),
+    "kmx": ("sbuf", [128, 48], i32), "phf": ("sbuf", [128, 48], f32),
+    "G": ("sbuf", [128, 3 * 4 * U], bf), "xw": ("sbuf", [128, 3 * 4 * U], f32), "sg": ("sbuf", [128, 3 * 4 * U], bf),
+    "dw": ("sbuf", [128, NCH * 16 * U], f32),
+    "nmc": ("sbuf", [128, V], f32), "off1": ("sbuf", [128, V], u16), "hi2": ("sbuf", [128, V], bf),
+    "Rr": ("sbuf", [128, U], f32), "a15": ("sbuf", [128, 16, CW], f32), "S": ("sbuf", [128, 32, CW], f32),
+    "K": ("sbuf", [128, 32, CW], i32), "lo": ("sbuf", [128, U], i32), "kk": ("sbuf", [128, U], i32),
+    "kf": ("sbuf", [128, U], f32), "pw": ("sbuf", [128, V], bf), "pwb": ("sbuf", [128, V], bf),
+    "Bs": ("sbuf", [128, 48], f32), "bit": ("sbuf", [128, U], bf),
+    "nm8": ("sbuf", [128, V], f32), "off": ("sbuf", [128, V], u16), "off2": ("sbuf", [128, V], u16),
+    "tt": ("sbuf", [128, U], f32), "km": ("sbuf", [128, U], f32), "km2": ("sbuf", [128, U], f32),
+    "qq": ("sbuf", [128, U], bf), "Fi": ("sbuf", [128, 48], i32), "Fc": ("sbuf", [128, 48], i32),
+    "keep": ("sbuf", [128, 16, 48], i32), "fo": ("sbuf", [128, 48], u16),
+    "gp": ("sbuf", [128, V], f32), "gn": ("sbuf", [128, V], f32), "gT": ("sbuf", [128, 16, 48], f32),
+    "Xp": ("sbuf", [128, V], f32), "t1": ("sbuf", [128, V], f32),
+    "Ea": ("sbuf", [128, NCH * 4 * U], f32), "xb": ("sbuf", [128, 3 * 4 * U], bf), "Mb": ("sbuf", [128, 4 * U], bf),
+    "tb": ("sbuf", [128, U], bf),
+    "idv": ("sbuf", [128, 128], f32), "idb": ("sbuf", [128, 128], bf), "mb": ("sbuf", [128, 23, 128], bf),
+    "ng": ("sbuf", [128, U], bf), "mf": ("sbuf", [128, 4, 128], f32), "Sel": ("sbuf", [128, 16, 128], bf), "Ys": ("sbuf", [128, 8, 128], bf),
+    "yv": ("sbuf", [128, 128], f32), "rep": ("sbuf", [128, CW], u16),
+    "yy": ("sbuf", [128, U], f32), "rpf": ("sbuf", [128, 2 * CW], f32), "gv": ("sbuf", [128, 8], f32),
+    "ga": ("sbuf", [128, 8], f32), "gb": ("sbuf", [128, 8], bf), "pc": ("sbuf", [128, 8], i32),
+    "pf": ("sbuf", [128, 8], f32), "pmi": ("sbuf", [128, 48], i32), "nat": ("sbuf", [128, 48], u16),
+    "mv": ("sbuf", [128, 96], f32), "msk": ("sbuf", [128, 192], f32), "kc": ("sbuf", [128, U], bf),
+    "ones": ("sbuf", [128, U], bf),
+    "pM": ("psum", [128, 1024], f32), "pC": ("psum", [128, 1024], f32), "p1": ("psum", [128, 16, 32], f32),
+    "p2": ("psum", [128, 16, 32], f32), "pX": ("psum", [128, 512], f32), "pT": ("psum", [128, 512], f32),
+}
+EXT = {"loud": [128, V], "fade": [128, V], "ph0": [8, V], "rb": [8, V], "nb": [128, V], "ye": [128, V], "yp": [8, V]}
+ENGS = ("pe", "dve", "act", "pool", "sp")
+NSEM = 110
+SEMAPHORES = ["e_" + e for e in ENGS[:4]] + ["b%d" % i for i in range(NSEM)]
+
+SORT_P = "111111110101010100000111111100000000001111111100000000000000000"
+SORT_V = "000000001111111100001111111100001111110000000011110000001111111"
+
+
+def batcher(n):
+    st, p = [], 1
+    while p < n:
+        k = p
+        while k >= 1:
+            s = []
+            for j in range(k % p, n - k, 2 * k):
+                for i in range(min(k, n - j - k)):
+                    if (i + j) // (2 * p) == (i + j + k) // (2 * p):
+                        s.append((i + j, i + j + k))
+            st.append(s)
+            k //= 2
+        p *= 2
+    return st
+
+
+def runs(items):
+    rem, out = sorted(items), []
+    while rem:
+        best = [rem[0]]
+        for x in rem:
+            for y in rem:
+                if y <= x:
+                    continue
+                d = tuple(b - a for a, b in zip(x, y))
+                if min(d) <= 0:
+                    continue
+                run = [x, y]
+                while tuple(a + b for a, b in zip(run[-1], d)) in rem:
+                    run.append(tuple(a + b for a, b in zip(run[-1], d)))
+                if len(run) > len(best):
+                    best = run
+        out.append(best)
+        for z in best:
+            rem.remove(z)
+    return out
+
+
+def sort_steps():
+    comps = [(si, l, h) for si, s in enumerate(batcher(16)) for l, h in s]
+    b, v = [int(x) for x in SORT_P], [int(x) for x in SORT_V]
+    nxt, last = {}, {}
+    for c in range(len(comps) - 1, -1, -1):
+        for w in comps[c][1:]:
+            nxt[(c, w)] = last.get(w)
+            last[w] = c
+
+    def loc(c, w):
+        if c is None:
+            return ("K", w)
+        return ("P", w) if (w == comps[c][1]) == (b[c] == 0) else ("S", 16 * v[c] + w)
+    steps = []
+    for si in range(10):
+        for phs in (0, 1):
+            gr = {}
+            for c, (s, l, h) in enumerate(comps):
+                if s == si:
+                    pw, sw = (l, h) if b[c] == 0 else (h, l)
+                    w = sw if phs == 0 else pw
+                    o = loc(nxt[(c, w)], w)
+                    gr.setdefault((w == l, o[0]), []).append((pw, loc(c, sw)[1], o[1]))
+            for key, it in gr.items():
+                for r in runs(it):
+                    steps.append((key[0], key[1], r))
+    init = [loc(last[w], w) for w in range(16)]
+    first = [(sp, r) for sp in "PS" for r in runs([(w, x[1]) for w, x in enumerate(init) if x[0] == sp])]
+    return first, steps
+
+
+def prog(vals):
+    step = vals[1] - vals[0] if len(vals) > 1 else 1
+    return slice(vals[0], vals[-1] + 1, step)
+
+
+OPT = {"dl": True, "R": True, "r": True, "z": 4, "look": 0.1, "ki": True, "o2": False, "la": True, "df": True,
+       "g0": (1, 3, 5), "d0": False, "gt": (), "f": ((), (), ()), "np": (1, 2)}
+AL = slice(None)
+CY = 0.83e-3
+PAR = {"G": 1.56, "ov": 0.05, "hop": 0.12, "same": 0.06, "pe": 0.8, "dma": 2.0, "far": 1.0, "b2": 1.0}
+
+
+def shape_of(name):
+    return SCRATCH[name][1] if name in SCRATCH else EXT[name]
+
+
+def A(name, *idx):
+    return (name, idx if idx else (AL,))
+
+
+def C(name, a, b, step=1):
+    return (name, (AL, slice(a, b, step)))
+
+
+def IND(win, offs):
+    return ("*", win, offs)
+
+
+def cells(ap):
+    name, idx = ap
+    if name in EXT:
+        return np.zeros(1, np.int64)
+    sh = shape_of(name)[1:]
+    return np.arange(int(np.prod(sh))).reshape(sh)[tuple(idx[1:])].reshape(-1)
+
+
+def build():
+    ops, GC, OV = [], PAR["G"], PAR["ov"]
+    lastw, readers, bank, pebank = {}, {}, {}, {}
+
+    def add(eng, kind, args, outs, ins, cost, lat=0.0, batch=None, extra=()):
+        n = len(ops)
+        raw, war = set(extra), set()
+        rd = []
+        for a in ins:
+            rd += [a[1], a[2]] if a[0] == "*" else [a]
+        for a in rd + list(outs):
+            if a[0] not in lastw:
+                size = 1 if a[0] in EXT else int(np.prod(shape_of(a[0])[1:]))
+                lastw[a[0]] = np.full(size, -1, np.int64)
+                readers[a[0]] = {}
+        for a in rd:
+            c = cells(a)
+            raw.update(int(x) for x in np.unique(lastw[a[0]][c]) if x >= 0)
+        for a in outs:
+            c = cells(a)
+            m = np.zeros(len(lastw[a[0]]), bool)
+            m[c] = True
+            war.update(int(x) for x in np.unique(lastw[a[0]][c]) if x >= 0)
+            for r in list(readers[a[0]]):
+                rc = readers[a[0]][r]
+                hit = m[rc]
+                if hit.any():
+                    war.add(r)
+                    if hit.all():
+                        del readers[a[0]][r]
+                    else:
+                        readers[a[0]][r] = rc[~hit]
+        for a in rd:
+            c = cells(a)
+            old = readers[a[0]].get(n)
+            readers[a[0]][n] = c if old is None else np.concatenate([old, c])
+        for a in outs:
+            lastw[a[0]][cells(a)] = n
+        bks = set()
+        for a in rd + list(outs):
+            if a[0] in SCRATCH and SCRATCH[a[0]][0] == "psum":
+                bks.update((a[0], int(x)) for x in np.unique(cells(a) // 512))
+        for bk in bks:
+            cur = bank.get(bk)
+            if cur is None or cur[0] != eng:
+                bank[bk] = [eng, [n], cur[1] if cur else []]
+            else:
+                cur[1].append(n)
+            war.update(bank[bk][2])
+            if eng == "pe":
+                if bk in pebank:
+                    war.add(pebank[bk])
+                pebank[bk] = n
+        if batch is not None:
+            raw = set(x for x in raw if ops[x]["batch"] != batch)
+            war = set(x for x in war if ops[x]["batch"] != batch)
+        ops.append(dict(eng=eng, kind=kind, args=args, raw=raw, war=war - raw - {n}, cost=cost, lat=lat, batch=batch))
+        return n
+
+    def size(ap):
+        return len(cells(ap))
+
+    def isps(a):
+        return a[0] in SCRATCH and SCRATCH[a[0]][0] == "psum"
+
+    def two(a):
+        return SCRATCH[a[0]][2] in (bf, u16)
+
+    def tt(out, a, b, op):
+        n = size(out)
+        cyc = n * GC if a[0] == "*" else (n if isps(a) or isps(b) else (PAR["b2"] if two(out) and two(a) and two(b) else 2) * n)
+        return add("dve", "tt", (out, a, b, op), [out], [a, b], OV + max(64, cyc) * CY)
+
+    def ts(out, a, s1, s2, op0, op1=None):
+        n = size(out)
+        ins = [a] + [s for s in (s1, s2) if isinstance(s, tuple)]
+        cyc = n * GC if a[0] == "*" else (n / 2 if two(out) and two(a) else n)
+        return add("dve", "ts", (out, a, s1, s2, op0, op1), [out], ins, OV + max(64, cyc) * CY)
+
+    def cp(out, a):
+        n = size(out)
+        cyc = n * GC if a[0] == "*" else (n / 2 if two(out) and two(a) else n)
+        return add("dve", "cp", (out, a), [out], [a], OV + max(64, cyc) * CY)
+
+    def ms(out, val):
+        n = size(out)
+        return add("dve", "ms", (out, val), [out], [], OV + max(64, n / 2 if two(out) else n) * CY)
+
+    def act(out, a, fn, scale=1.0, bias=0.0):
+        n = size(out)
+        return add("act", "act", (out, a, fn, scale, bias), [out], [a], 1.3 * OV + max(64, n * GC if a[0] == "*" else n) * CY)
+
+    def mm(out, l, r, start, stop):
+        n = max(64, size(r)) * (4 if SCRATCH[r[0]][2] == f32 else 1)
+        return add("pe", "mm", (out, l, r, start, stop), [out], [l, r], 0.01 + n * CY * PAR["pe"])
+
+    def iota(out, pat, base, cm):
+        return add("pool", "iota", (out, pat, base, cm), [out], [], 0.13 + 2 * size(out) * CY)
+
+    nb = [0]
+
+    def newb():
+        nb[0] += 1
+        return nb[0] - 1
+
+    def dma(eng, out, a, batch=None, acc=False, kb=1.0):
+        b = newb() if batch is None else batch
+        ins = [a, out] if acc else [a]
+        return add(eng, "dma", (out, a, acc), [out], ins, 1.0 if eng == "pool" else 0.12, PAR["dma"] + 0.22 * kb * (2 if acc else 1), b)
+
+    def exchange(src, dsts, lat):
+        s = add("pool", "send", (src, dsts, newb()), [], [src], 1.0, lat * PAR["far"], newb())
+        return add(None, "recv", (), dsts, [], 0.0, 0.5, ops[s]["args"][2], extra=[s])
+
+    ge, lt, eq = ALU.is_ge, ALU.is_lt, ALU.is_equal
+    mul, plus, sub, mx, mn = ALU.mult, ALU.add, ALU.subtract, ALU.max, ALU.min
+    band, shr = ALU.bitwise_and, ALU.arith_shift_right
+    Wn = ["W0", "W1", "W2"]
+
+    dma("sp", A("ph"), A("ph0"))
+    b = newb()
+    dma("sp", A("Ls0", slice(0, 112), AL), A("loud", slice(16, 128), slice(0, GH)), b)
+    dma("act", A("Ls0", slice(112, 128), AL), A("loud", slice(0, 16), slice(0, GH)), b)
+    b = newb()
+    for k in range(16):
+        dma("sp" if k % 2 else "act", A("nbT", AL, k, AL), A("nb", slice(k, 128, 16), AL), b)
+    dma("sp", C("W0", PAD, PAD + V), A("loud"))
+    dma("sp", A("rbi"), A("rb"))
+    dma("sp", A("nbN"), A("nb"))
+    dma("sp", A("fad"), A("fade"))
+    iota(A("yv"), [[-16, 8], [-1000, 2], [-2, 8]], 0, 1)
+    iota(C("pc", 0, 1), [[0, 1]], 0, 1)
+    iota(A("mv"), [[1, 96]], 0, 0)
+    iota(A("gv"), [[-16, 8]], 0, 1)
+    iota(A("idv"), [[1, 128]], 0, -1)
+    iota(A("kc"), [[2048, 16], [0, CW]], -16384, 0)
+    iota(A("pmi"), [[1, 16], [256, 3]], 0, 0)
+    iota(C("rpf", 0, CW), [[0, 8], [16, 3]], 0, 0)
+    for il in range(2):
+        for pt in range(2):
+            ts(A("Ys", AL, 2 * il + pt, AL), A("yv"), float(il - 1000 * pt), None, eq)
+            ya = C("xw", 128 * (2 * il + pt), 128 * (2 * il + pt + 1))
+            act(ya, A("yv"), ACTF.Abs, 1.0, float(48 - il + 1000 * pt))
+            ts(A("Ys", AL, 4 + 2 * il + pt, AL), ya, 64.0, None, eq)
+    ts(C("pc", 2, 3), C("pc", 0, 1), 7, None, band)
+    ts(C("pc", 4, 5), C("pc", 0, 1), 15, None, band)
+    ts(C("pf", 0, 1), C("pc", 2, 3), 96.0, None, mul)
+    ts(C("pf", 2, 3), C("pc", 4, 5), 16.0, None, mul)
+    ts(C("pf", 4, 5), C("pc", 4, 5), 7.0, 0.5, eq, mul)
+    cp(C("pf", 6, 7), C("pc", 4, 5))
+    ts(C("rpf", 0, CW), C("rpf", 0, CW), C("pf", 6, 7), None, plus)
+    ts(C("rpf", CW, 2 * CW), C("rpf", 0, CW), 24.0, -24.0, ge, mul)
+    tt(C("rpf", 0, CW), C("rpf", 0, CW), C("rpf", CW, 2 * CW), plus)
+    cp(A("rep"), C("rpf", 0, CW))
+    ms(C("msk", 0, 96), 1.0)
+    ts(C("msk", 96, 192), A("mv"), C("pf", 0, 1), float(GH), plus, lt)
+    ts(A("nat"), A("pmi"), C("pf", 2, 3), None, plus)
+    ms(A("Wp"), 1.0)
+    ts(A("Wp"), A("Wp"), C("pf", 4, 5), None, mul)
+    for w in Wn:
+        ms(C(w, 0, PAD), 0.0)
+    ms(A("ones"), 1.0)
+    ts(A("ga"), A("gv"), 0.0, 2.0 ** 25, ge, mul)
+    ts(A("gv"), A("gv"), 15.5, None, lt)
+    tt(A("gb"), A("ga"), A("gv"), mul)
+    ms(A("Sel"), 0.0)
+    for i in range(16):
+        act(A("Sel", AL, i, slice(i, 128, 16)), A("gb"), ACTF.Copy)
+    ts(A("idb"), A("idv"), 0.0, None, eq)
+    for j, w in enumerate([2.0 ** k for k in range(16)] + [-2.0 ** 15, 1152.0, 9 * 2.0 ** 25, 2.0 ** -9, 576.0, -576.0, -1.0]):
+        act(A("mb", AL, j, AL), A("idb"), ACTF.Copy, w)
+    for j, w in enumerate([8.0, -7.0, 1.0, -1.0]):
+        act(A("mf", AL, j, AL), A("idb"), ACTF.Copy, w)
+    LOFF = -float(512 * 4096 + 1144)
+    for ch in range(NCH):
+        cs = slice(ch * CW, (ch + 1) * CW)
+        ts(A("lT0", AL, AL, cs), A("nbT", AL, AL, cs), LOFF, None, plus)
+    ts(A("lN0"), A("nbN"), LOFF, None, plus)
+    ts(A("rbi"), A("rbi"), 512.0, None, plus)
+
+    def mat(j):
+        return A("mb", AL, j, AL)
+
+    def ghosts(w):
+        return [C(w, PAD + V + d * GH, PAD + V + (d + 1) * GH) for d in range(3)]
+
+    def times_out(t):
+        ts(A("ti"), A("ph"), 31, None, band)
+        cp(C("phb", 48, 96), A("ti"))
+        tt(C("phb", 0, 48), A("ph"), A("ti"), sub)
+        for sh in (1, 0):
+            for il in range(2):
+                for pt in range(2):
+                    o = 96 * sh + 48 * il
+                    mm(C("pX", o, o + 48), A("Ys", AL, 4 * sh + 2 * il + pt, AL), C("phb", 48 * pt, 48 * pt + 48), pt == 0, pt == 1)
+        tt(A("Yb", AL, t, AL), C("pX", 0, 192), A("msk"), mul)
+        exchange(A("Yb", AL, t, slice(96, 192)), [A("land", AL, 3 * t + d, AL) for d in range(3)], 3.0)
+        bt = newb()
+        dma("sp", A("Wp", slice(0, 128, 8), slice(PAD, PAD + V)), A("Yb", AL, t, slice(0, 96)), bt)
+        for d in range(3):
+            o = PAD + V + d * GH
+            dma("sp", A("Wp", slice(d + 1, 128, 8), slice(o, o + V)), A("land", AL, 3 * t + d, AL), bt)
+        tt(A("pr"), A("ph"), A("rbi"), plus)
+
+    first, steps = sort_steps()
+    slot = {"G": 0, "xw": 0, "sg": 0, "xb": 0}
+
+    def roll(name):
+        slot[name] = (slot[name] + 1) % 3
+        return slot[name] * 4 * U
+
+    def rint(out, a, c, onact):
+        if onact:
+            act(out, a, ACTF.Identity, 1.0, c)
+            act(out, out, ACTF.Identity, 1.0, -c)
+        else:
+            ts(out, a, c, c, plus, sub)
+
+    def names(t, ch):
+        lT = "lT%d" % (t % 2)
+        cs, o = slice(ch * CW, (ch + 1) * CW), ch * U
+        P2 = A("p%d" % (ch + 1), AL, AL, slice(0, CW))
+        rint(P2, A(lT, AL, AL, cs), 1.5 * 2.0 ** 35, OPT["dl"])
+        tt(C("nmc", o, o + U), A(lT, AL, AL, cs), P2, sub)
+        ts(C("off1", o, o + U), C("nmc", o, o + U), 1152.0, None, plus)
+        act(C("hi2", o, o + U), C("nmc", o, o + U), ACTF.Sign, 1.0, -7.5)
+        mm(P2, A("mf", AL, 1, AL), C("nmc", o, o + U), True, False)
+        mm(P2, mat(0), A("kc"), False, False)
+        mm(P2, mat(21), C("hi2", o, o + U), False, True)
+        f = U + ch * CW
+        for k in range(16):
+            mm(C("pX", f, f + CW), mat(k), C("hi2", o + k * CW, o + (k + 1) * CW), k == 0, k == 15)
+        ts(C("Bs", ch * CW, (ch + 1) * CW), C("pX", f, f + CW), -65535.5, -2.0 ** 10, plus, mul)
+
+    def arrival(t, ch):
+        lT = "lT%d" % (t % 2)
+        cs, o, pc = slice(ch * CW, (ch + 1) * CW), ch * U, ch * 512
+        mm(C("pC", pc, pc + U), mat(20), A("ones"), True, False)
+        for k in range(16):
+            for pt in range(2):
+                mm(C("pC", pc + k * CW, pc + (k + 1) * CW), mat(16), C("phb", 48 * pt + ch * CW, 48 * pt + (ch + 1) * CW), False, False)
+        mm(C("pC", pc, pc + U), A("mf", AL, 0, AL), A(lT, AL, AL, cs), False, False)
+        for j in range(4):
+            s = roll("G")
+            src = IND(C("Wp", 0, WW), C("off1", o + 4 * j * CW, o + 4 * (j + 1) * CW))
+            if t == 0 and 4 * ch + j in OPT["g0"]:
+                ts(C("G", s, s + 4 * U), src, 2.0 ** -10, None, mul)
+            else:
+                act(C("G", s, s + 4 * U), src, ACTF.Copy, 2.0 ** -10)
+            for i in range(16):
+                mm(C("pC", pc + 4 * j * CW, pc + 4 * (j + 1) * CW), A("Sel", AL, i, AL), C("G", s + i, s + 4 * U, 16), False, j == 3 and i == 15)
+
+    def keys(t, ch):
+        o, pc, pp = ch * U, ch * 512, "p%d" % (ch + 1)
+        rint(A("Rr"), C("pC", pc, pc + U), 1.5 * 2.0 ** 48, OPT["R"])
+        tt(A("a15"), C("pC", pc, pc + U), A("Rr"), sub)
+        for sp, r in first:
+            w, z = prog([x[0] for x in r]), prog([x[1] for x in r])
+            dst = A(pp, AL, z, slice(0, CW)) if sp == "P" else A("S", AL, z, AL)
+            tt(dst, A(pp, AL, w, slice(0, CW)), A("a15", AL, w, AL), plus)
+        for ismin, sp, r in steps:
+            pw, sw, ow = [[x[j] for x in r] for j in range(3)]
+            if sp == "P":
+                dst = A(pp, AL, prog(ow), slice(0, CW))
+            elif sp == "S":
+                dst = A("S", AL, prog(ow), AL)
+            else:
+                dst = A("K", AL, prog([16 * ch + x for x in ow]), AL)
+            tt(dst, A(pp, AL, prog(pw), slice(0, CW)), A("S", AL, prog(sw), AL), mn if ismin else mx)
+        Kc = A("K", AL, slice(16 * ch, 16 * ch + 16), AL)
+        ts(A("kk"), Kc, 11, 15, shr, band)
+        if not OPT["ki"]:
+            cp(A("kf"), A("kk"))
+        act(C("pw", o, o + U), A("kk" if OPT["ki"] else "kf"), ACTF.Sigmoid, -math.log(2.0), -12 * math.log(2.0))
+        ts(A("lo"), Kc, 2047, None, band)
+        tt(A("yy"), IND(C("Bs", ch * CW, (ch + 1) * CW), A("rep")), C("pw", o, o + U), mul)
+        rint(C("pT", 0, U), A("yy"), 1.5 * 2.0 ** 23, OPT["r"])
+        tt(A("bit"), C("pT", 0, U), A("yy"), lt)
+        mm(C("pX", 0, U), mat(17), A("bit"), True, True)
+        tt(C("nm8", o, o + U), A("lo"), C("pX", 0, U), plus)
+        cp(C("off", o, o + U), C("nm8", o, o + U))
+        if t < RO - 1:
+            act(C("pwb", o, o + U), C("pw", o, o + U), ACTF.Copy, 2.0 ** 36)
+            ts(C("fo", ch * CW, (ch + 1) * CW), C("nm8", o, o + CW), float(PAD + V - 1), -float(PAD), mn, plus)
+            ts(C("Fc", ch * CW, (ch + 1) * CW), C("nm8", o, o + CW), float(PAD + V), 65535.0, ge, mul)
+
+    def masking(t, ch):
+        o, dd, pc = ch * U, ch * 16 * U, ch * 512
+        win = C(Wn[t], 0, WW)
+        mm(C("pC", pc, pc + U), mat(18), A("ones"), True, False)
+        short = t == 0 and OPT["d0"]
+        for j in range(4 if short else 0):
+            xs, ss = roll("xb"), roll("sg")
+            act(C("xb", xs, xs + 4 * U), IND(win, C("off", o + 4 * j * CW, o + 4 * (j + 1) * CW)), ACTF.Copy)
+            for s in range(4 * j, 4 * j + 4):
+                x = C("xb", xs + (s % 4) * U, xs + (s % 4 + 1) * U)
+                if s == 0:
+                    act(C("dw", dd, dd + U), x, ACTF.Sigmoid)
+                    M = x
+                    continue
+                M2 = C("Mb", (s % 4) * U, (s % 4 + 1) * U) if s < 15 else C("Xp", o, o + U)
+                tt(M2, x, M, mx)
+                pd = C("pM", 512 * (s % 2), 512 * (s % 2) + U)
+                mm(pd, mat(0), x, True, False)
+                mm(pd, mat(22), M, False, True)
+                sgn = C("sg", ss + (s % 4) * U, ss + (s % 4 + 1) * U)
+                if s in OPT["gt"]:
+                    tt(A("tb"), x, M, ALU.is_gt)
+                    ts(sgn, A("tb"), 2.0, -1.0, mul, plus)
+                else:
+                    act(sgn, pd, ACTF.Sign, 1.0, -2.0 ** -26)
+                act(C("dw", dd + s * U, dd + (s + 1) * U), pd, ACTF.Sigmoid)
+                M = M2
+            s0 = max(1, 4 * j)
+            for i in range(16):
+                mm(C("pC", pc + s0 * CW, pc + (4 * j + 4) * CW), A("Sel", AL, i, AL), C("sg", ss + (s0 % 4) * U + i, ss + 4 * U, 16), False, j == 3 and i == 15)
+        if not short:
+            act(C("dw", dd, dd + U), IND(win, C("off", o, o + CW)), ACTF.Copy)
+        M = C("dw", dd, dd + U)
+        for s0, s1 in () if short else ((1, 4), (4, 8), (8, 12), (12, 16)):
+            n = s1 - s0
+            xs = roll("xw")
+            act(C("xw", xs, xs + n * U), IND(win, C("off", o + s0 * CW, o + s1 * CW)), ACTF.Copy)
+            for s in range(s0, s1):
+                x = C("xw", xs + (s - s0) * U, xs + (s - s0 + 1) * U)
+                M2 = None
+                if s < 15:
+                    M2 = C("pM", 512 * (s % 2), 512 * (s % 2) + U)
+                elif t < RO - 1:
+                    M2 = C("Xp", o, o + U)
+                if M2 is not None:
+                    tt(M2, x, M, mx)
+                tt(C("dw", dd + s * U, dd + (s + 1) * U), x, M, sub)
+                M = M2
+            ss = roll("sg")
+            act(C("sg", ss, ss + n * U), C("dw", dd + s0 * U, dd + s1 * U), ACTF.Sign, 1.0, -2.0 ** -26)
+            for i in range(16):
+                mm(C("pC", pc + s0 * CW, pc + s1 * CW), A("Sel", AL, i, AL), C("sg", ss + i, ss + n * U, 16), False, s1 == 16 and i == 15)
+        cnt = C("pC", pc, pc + U)
+        tt(A("km"), A("K", AL, slice(16 * ch, 16 * ch + 16), AL), cnt, mn)
+        tt(C("km2", 0, 192), C("km", 0, 192), C("km", 192, 384), mx)
+        tt(C("km2", 192, 288), C("km2", 0, 96), C("km2", 96, 192), mx)
+        tt(C("km2", 288, 336), C("km2", 192, 240), C("km2", 240, 288), mx)
+        tt(C("kmx", ch * CW, (ch + 1) * CW), C("km2", 288, 312), C("km2", 312, 336), mx)
+        if t < RO - 1:
+            tt(A("qq"), C("pwb", o, o + U), cnt, mn)
+            f = 432 + ch * CW
+            for s in range(16):
+                mm(C("pX", f, f + CW), mat(19), C("qq", s * CW, (s + 1) * CW), s == 0, s == 15)
+            cp(C("Fi", ch * CW, (ch + 1) * CW), C("pX", f, f + CW))
+        if OPT["o2"]:
+            act(A("ng"), cnt, ACTF.Relu, -2.0 ** -10)
+            mm(C("pT", 0, U), A("mf", AL, 2, AL), C("nm8", o, o + U), True, False)
+            mm(C("pT", 0, U), mat(16), A("ng"), False, True)
+            cp(C("off2", o, o + U), C("pT", 0, U))
+        else:
+            tt(A("tt"), C("nm8", o, o + U), cnt, mn)
+            cp(C("off2", o, o + U), A("tt"))
+
+    def hearing(t, ch):
+        o, dd = ch * U, ch * 16 * U
+        n = OPT["z"]
+        for j in range(4):
+            z = C("dw", dd + 4 * j * U, dd + 4 * (j + 1) * U)
+            win = C(Wn[t], 0, WW)
+            if 4 * ch + j in OPT["f"][t]:
+                xs = roll("xw")
+                act(C("xw", xs, xs + 4 * U), IND(win, C("off2", o + 4 * j * CW, o + 4 * (j + 1) * CW)), ACTF.Copy)
+                for s in range(4 * j, 4 * j + 4):
+                    zs, pd = C("dw", dd + s * U, dd + (s + 1) * U), C("pM", 512 * (s % 2), 512 * (s % 2) + U)
+                    act(pd, zs, ACTF.Sigmoid)
+                    tt(zs, pd, C("xw", xs + (s % 4) * U, xs + (s % 4 + 1) * U), mul)
+            else:
+                if t > 0 or not OPT["d0"]:
+                    act(z, z, ACTF.Sigmoid)
+                for s in range(4 * j, 4 * j + 4, n):
+                    zs = C("dw", dd + s * U, dd + (s + n) * U)
+                    tt(zs, IND(win, C("off2", o + s * CW, o + (s + n) * CW)), zs, mul)
+            e = ch * 4 * U
+            if t == 0 and j == 0:
+                dma("sp", C("Ea", e, e + 4 * U), z, kb=6)
+            elif t == RO - 1 and j >= 4 - OPT["np"][ch]:
+                for s in range(4 * j, 4 * j + 4):
+                    mm(C(("pT", "pX")[ch], 0, U), A("mf", AL, 2, AL), C("dw", dd + s * U, dd + (s + 1) * U), s == 16 - 4 * OPT["np"][ch], s == 15)
+            else:
+                dma("pool", C("Ea", e, e + 4 * U), z, acc=True, kb=6)
+
+    def fetch(t):
+        act(A("gp"), IND(A("lN%d" % t), A("fo")), ACTF.Copy)
+        act(A("gn"), IND(A("gp"), A("nat")), ACTF.Copy)
+        bt = newb()
+        for k in range(16):
+            dma("sp", A("gT", AL, k, AL), A("gn", slice(k, 128, 16), AL), bt)
+
+    def loudness(t):
+        own, new = Wn[t], Wn[t + 1]
+        if OPT["la"]:
+            act(A("t1"), IND(A("Xp"), A("nat")), ACTF.Copy, 0.125)
+        else:
+            tt(A("t1"), IND(A("Xp"), A("nat")), C(own, PAD, PAD + V), sub)
+        for h in range(2):
+            a, z = h * U, (h + 1) * U
+            tmp = C("pM", 512 * h, 512 * h + U)
+            if OPT["la"]:
+                act(tmp, C(own, PAD + a, PAD + z), ACTF.Copy, 0.125)
+                tt(tmp, C("t1", a, z), tmp, sub)
+            else:
+                ts(tmp, C("t1", a, z), 0.125, None, mul)
+            tt(tmp, tmp, C(own, PAD + a, PAD + z), plus)
+            tt(C(new, PAD + a, PAD + z), tmp, C("fad", a, z), mul)
+        ls = "Ls%d" % (t + 1)
+        bt = newb()
+        dma("sp", A(ls, slice(0, 112), AL), A(new, slice(16, 128), slice(PAD, PAD + GH)), bt, kb=2)
+        dma("sp", A(ls, slice(112, 128), AL), A(new, slice(0, 16), slice(PAD, PAD + GH)), bt, kb=2)
+
+    def lists(t):
+        old, new = "lT%d" % (t % 2), "lT%d" % ((t + 1) % 2)
+        ts(A("Fi"), A("Fi"), 65535, None, band)
+        tt(A("Fi"), A("Fi"), A("Fc"), mx)
+        for k in range(16):
+            ts(A("keep", AL, k, AL), A("Fi"), 15 - k, 1, shr, band)
+        for ch in range(NCH):
+            cs = slice(ch * CW, (ch + 1) * CW)
+            tmp = A("p%d" % (ch + 1), AL, AL, slice(0, CW))
+            if OPT["df"]:
+                mm(tmp, A("mf", AL, 2, AL), A(old, AL, AL, cs), True, False)
+                mm(tmp, A("mf", AL, 3, AL), A("gT", AL, AL, cs), False, True)
+            else:
+                tt(tmp, A(old, AL, AL, cs), A("gT", AL, AL, cs), sub)
+            tt(tmp, tmp, A("keep", AL, AL, cs), mul)
+            tt(A(new, AL, AL, cs), tmp, A("gT", AL, AL, cs), plus)
+        if t + 2 < RO:
+            bt = newb()
+            for k in range(16):
+                dma("sp", A("lN%d" % (t + 1), slice(k, 128, 16), AL), A(new, AL, k, AL), bt)
+
+    times_out(0)
+    exchange(A("Ls0"), ghosts("W0"), 4.0)
+    for t in range(RO):
+        for step in (names, arrival, keys):
+            for ch in range(NCH):
+                step(t, ch)
+        if t < RO - 1:
+            fetch(t)
+        for ch in range(NCH):
+            masking(t, ch)
+        ts(A("tj"), A("kmx"), 15, None, shr)
+        tt(A("tj"), A("tj"), A("pr"), plus)
+        ts(A("ph"), A("tj"), 1023, None, band)
+        if t < RO - 1:
+            times_out(t + 1)
+            lists(t)
+            loudness(t)
+            exchange(A("Ls%d" % (t + 1)), ghosts(Wn[t + 1]), 8.0)
+        else:
+            cp(A("phf"), A("ph"))
+            dma("sp", A("yp"), A("phf"))
+        for ch in range(NCH):
+            hearing(t, ch)
+    for ch in range(NCH):
+        e = ch * 4 * U
+        pm, acc = C("pM", 512 * ch, 512 * ch + U), C(("pT", "pX")[ch], 0, U)
+        tt(pm, C("Ea", e, e + U), C("Ea", e + U, e + 2 * U), plus)
+        tt(pm, pm, C("Ea", e + 2 * U, e + 3 * U), plus)
+        tt(C("t1", ch * U, (ch + 1) * U), pm, C("Ea", e + 3 * U, e + 4 * U), plus)
+        tt(C("gp", ch * U, (ch + 1) * U), acc, C("t1", ch * U, (ch + 1) * U), plus)
+    cp(A("gn"), IND(A("gp"), A("nat")))
+    dma("sp", A("ye"), A("gn"), kb=3)
+    return ops
+
+
+def order(ops, fixed=None):
+    n = len(ops)
+    members = {}
+    for i, o in enumerate(ops):
+        if o["batch"] is not None:
+            members.setdefault(o["batch"], []).append(i)
+    for o in ops:
+        for key in ("raw", "war"):
+            for d in list(o[key]):
+                if ops[d]["batch"] is not None:
+                    o[key].update(members[ops[d]["batch"]])
+        o["deps"] = o["raw"] | o["war"]
+    succ = [[] for _ in ops]
+    for i, o in enumerate(ops):
+        for d in o["deps"]:
+            succ[d].append(i)
+
+    def gap(d, i):
+        if ops[d]["eng"] == ops[i]["eng"] and ops[d]["batch"] is None:
+            return 0.0 if ops[i]["eng"] == "pe" else PAR["same"]
+        return PAR["hop"]
+    left = [len(o["deps"]) for o in ops]
+    topo = [i for i in range(n) if left[i] == 0]
+    for i in topo:
+        for j in succ[i]:
+            left[j] -= 1
+            if left[j] == 0:
+                topo.append(j)
+    assert len(topo) == n
+    pr = [0.0] * n
+    for i in reversed(topo):
+        pr[i] = ops[i]["cost"] + ops[i]["lat"] + max([pr[j] + gap(i, j) for j in succ[i]] + [0.0])
+    left = [len(o["deps"]) for o in ops]
+    ready = {e: [] for e in ENGS + (None,)}
+    rt, fin, free = [0.0] * n, [0.0] * n, {e: 0.0 for e in ENGS}
+    queue = {e: [] for e in ENGS}
+    for i in range(n):
+        if left[i] == 0:
+            ready[ops[i]["eng"]].append(i)
+    done = 0
+    while done < n:
+        if ready[None]:
+            i = ready[None].pop()
+            start = rt[i]
+        else:
+            best = None
+            for e in ENGS:
+                can = ready[e] if fixed is None else [j for j in fixed[e][len(queue[e]):len(queue[e]) + 1] if left[j] == 0]
+                if can:
+                    t0 = max(free[e], min(rt[j] for j in can))
+                    if best is None or t0 < best[0]:
+                        best = (t0, e, can)
+            t0, e, can = best
+            i = max((j for j in can if rt[j] <= t0 + OPT["look"]), key=lambda j: (pr[j], -j))
+            ready[e].remove(i)
+            start = max(t0, rt[i])
+            free[e] = start + ops[i]["cost"]
+            queue[e].append(i)
+        ops[i]["start"] = start
+        fin[i] = start + ops[i]["cost"] + ops[i]["lat"]
+        done += 1
+        for j in succ[i]:
+            rt[j] = max(rt[j], fin[i] + gap(i, j))
+            left[j] -= 1
+            if left[j] == 0:
+                ready[ops[j]["eng"]].append(j)
+    pos = {}
+    for e in ENGS:
+        for p, i in enumerate(queue[e]):
+            pos[i] = p
+    marked, waited = set(), set()
+    for e in ENGS:
+        known, seen = {}, set()
+        for i in queue[e]:
+            o = ops[i]
+            need, o["wb"] = {}, []
+            for d in sorted(o["deps"]):
+                od = ops[d]
+                if od["batch"] is not None:
+                    if od["batch"] not in seen:
+                        seen.add(od["batch"])
+                        waited.add(od["batch"])
+                        o["wb"].append(od["batch"])
+                elif od["eng"] != e or e != "pe":
+                    if pos[d] > known.get(od["eng"], -1) and pos[d] > pos.get(need.get(od["eng"]), -1):
+                        need[od["eng"]] = d
+            for x, d in need.items():
+                known[x] = pos[d]
+                marked.add(d)
+            o["we"] = list(need.values())
+    count = {}
+    for e in ENGS:
+        c = 0
+        for i in queue[e]:
+            if i in marked:
+                c += 1
+                count[i] = c
+    return dict(ops=ops, queue=queue, count=count, members=members, tail=[x for x in members if x not in waited], end=max(fin))
+
+
+PLAN = {}
+
+
+def shares(src, cores, topo):
+    r = cores.index(src)
+    dst = [cores[(r + d) % NR] for d in range(1, NR)]
+    out, used = {}, set()
+    for x in sorted(dst, key=lambda c: len(topo.engines(src, c))):
+        can = [e for e in topo.engines(src, x) if e not in used]
+        alike = [y for y in dst if y not in out and topo.mask(src, y) == topo.mask(src, x)]
+        n = 1
+        while 2 * n <= len(can) // len(alike):
+            n *= 2
+        out[x] = can[:n]
+        used.update(can[:n])
+    return [(x, out[x]) for x in dst]
+
+
+def rank_program(g, core, T, topo):
+    if T.rank_of(core) is None:
+        return
+    if not PLAN:
+        PLAN.update(order(build()))
+    ops, cores = PLAN["ops"], list(T.cores)
+    mine = shares(core, cores, topo)
+    arrive = sum(len(e) for c in cores if c != core for x, e in shares(c, cores, topo) if x == core)
+    Q = {"pe": g.tensor, "dve": g.vector, "act": g.scalar, "pool": g, "sp": g.sync}
+
+    def R(a):
+        if not isinstance(a, tuple):
+            return a
+        if a[0] == "*":
+            return R(a[1]).indirect(R(a[2]))
+        return T[a[0]][a[1] if len(a[1]) > 1 else a[1][0]]
+
+    def total(bt):
+        kind = ops[PLAN["members"][bt][0]]["kind"]
+        if kind == "send":
+            return sum(len(e) for x, e in mine)
+        return arrive if kind == "recv" else 16 * len(PLAN["members"][bt])
+
+    for e in ENGS:
+        q = Q[e]
+        for i in PLAN["queue"][e]:
+            o = ops[i]
+            for d in o["we"]:
+                q.wait_ge(T.sem["e_" + ops[d]["eng"]], PLAN["count"][d])
+            for bt in o["wb"]:
+                q.wait_ge(T.sem["b%d" % bt], total(bt))
+            k, a = o["kind"], o["args"]
+            if k == "send":
+                tr = []
+                for d, (x, eng) in enumerate(mine):
+                    rid, pid = topo.addr(x, core)
+                    tr.append(RemoteDMATransfer(dst_ids=[DstId(rid=rid, pnc=pid)], dma_engine_mask=sum(1 << y for y in eng),
+                                                remote_sem=T.sem["b%d" % a[2]], src=R(a[0]), dst=R(a[1][d])))
+                q.remote_dma_fused(tr, local_sem=T.sem["b%d" % o["batch"]])
+                continue
+            if k == "dma":
+                ins = q.dma_start(R(a[0]), R(a[1]), accum_op=ALU.add) if a[2] else q.dma_start(R(a[0]), R(a[1]))
+                ins.then_inc(T.sem["b%d" % o["batch"]], 16)
+                continue
+            if k == "tt":
+                ins = q.tensor_tensor(R(a[0]), R(a[1]), R(a[2]), a[3])
+            elif k == "ts":
+                if a[5] is None:
+                    ins = q.tensor_scalar(R(a[0]), R(a[1]), R(a[2]), None, a[4])
+                else:
+                    ins = q.tensor_scalar(R(a[0]), R(a[1]), R(a[2]), R(a[3]), a[4], a[5])
+            elif k == "cp":
+                ins = q.tensor_copy(R(a[0]), R(a[1]))
+            elif k == "ms":
+                ins = q.memset(R(a[0]), a[1])
+            elif k == "act":
+                if a[4] != 0.0:
+                    ins = q.activation(R(a[0]), R(a[1]), a[2], bias=a[4], scale=a[3])
+                elif a[3] != 1.0:
+                    ins = q.activation(R(a[0]), R(a[1]), a[2], scale=a[3])
+                else:
+                    ins = q.activation(R(a[0]), R(a[1]), a[2])
+            elif k == "mm":
+                ins = q.matmul(R(a[0]), R(a[1]), R(a[2]), a[3], a[4])
+            elif SCRATCH[a[0][0]][2] == i32:
+                ins = q.iota(R(a[0]), a[1], a[2], a[3])
+            else:
+                ins = q.iota(R(a[0]), a[1], a[2], a[3], allow_small_or_imprecise_dtypes=True)
+            if i in PLAN["count"]:
+                ins.then_inc(T.sem["e_" + e], 1)
+    for bt in PLAN["tail"]:
+        g.wait_ge(T.sem["b%d" % bt], total(bt))

@@ -26,8 +26,8 @@ SCRATCH = {
     "G": ("sbuf", [128, 3 * 4 * U], bf), "xw": ("sbuf", [128, 3 * 4 * U], f32), "sg": ("sbuf", [128, 3 * 4 * U], bf),
     "dw": ("sbuf", [128, NCH * 16 * U], f32),
     "nmc": ("sbuf", [128, V], f32), "off1": ("sbuf", [128, V], u16), "hi2": ("sbuf", [128, V], bf),
-    "Rr": ("sbuf", [128, U], f32), "a15": ("sbuf", [128, 16, CW], f32), "S": ("sbuf", [128, 32, CW], f32),
-    "K": ("sbuf", [128, 32, CW], i32), "lo": ("sbuf", [128, U], i32), "kk": ("sbuf", [128, U], i32),
+    "Rr": ("sbuf", [128, V], f32), "a15": ("sbuf", [128, 16, 48], f32), "S": ("sbuf", [128, 32, 48], f32),
+    "K": ("sbuf", [128, 16, 48], i32), "lo": ("sbuf", [128, U], i32), "kk": ("sbuf", [128, U], i32),
     "kf": ("sbuf", [128, U], f32), "pw": ("sbuf", [128, V], bf), "pwb": ("sbuf", [128, V], bf),
     "Bs": ("sbuf", [128, 48], f32), "bit": ("sbuf", [128, U], bf),
     "nm8": ("sbuf", [128, V], f32), "off": ("sbuf", [128, V], u16), "off2": ("sbuf", [128, V], u16),
@@ -36,8 +36,7 @@ SCRATCH = {
     "keep": ("sbuf", [128, 16, 48], i32), "fo": ("sbuf", [128, 48], u16),
     "gp": ("sbuf", [128, V], f32), "gn": ("sbuf", [128, V], f32), "gT": ("sbuf", [128, 16, 48], f32),
     "Xp": ("sbuf", [128, V], f32), "t1": ("sbuf", [128, V], f32),
-    "Ea": ("sbuf", [128, NCH * 4 * U], f32), "xb": ("sbuf", [128, 3 * 4 * U], bf), "Mb": ("sbuf", [128, 4 * U], bf),
-    "tb": ("sbuf", [128, U], bf),
+    "Ea": ("sbuf", [128, NCH * 4 * U], f32),
     "idv": ("sbuf", [128, 128], f32), "idb": ("sbuf", [128, 128], bf), "mb": ("sbuf", [128, 23, 128], bf),
     "ng": ("sbuf", [128, U], bf), "mf": ("sbuf", [128, 4, 128], f32), "Sel": ("sbuf", [128, 16, 128], bf), "Ys": ("sbuf", [128, 8, 128], bf),
     "yv": ("sbuf", [128, 128], f32), "rep": ("sbuf", [128, CW], u16),
@@ -46,8 +45,8 @@ SCRATCH = {
     "pf": ("sbuf", [128, 8], f32), "pmi": ("sbuf", [128, 48], i32), "nat": ("sbuf", [128, 48], u16),
     "mv": ("sbuf", [128, 96], f32), "msk": ("sbuf", [128, 192], f32), "kc": ("sbuf", [128, U], bf),
     "ones": ("sbuf", [128, U], bf),
-    "pM": ("psum", [128, 1024], f32), "pC": ("psum", [128, 1024], f32), "p1": ("psum", [128, 16, 32], f32),
-    "p2": ("psum", [128, 16, 32], f32), "pX": ("psum", [128, 512], f32), "pT": ("psum", [128, 512], f32),
+    "pM": ("psum", [128, 1024], f32), "pC": ("psum", [128, 1024], f32), "pP": ("psum", [128, 16, 64], f32),
+    "pX": ("psum", [128, 512], f32), "pT": ("psum", [128, 512], f32),
 }
 EXT = {"loud": [128, V], "fade": [128, V], "ph0": [8, V], "rb": [8, V], "nb": [128, V], "ye": [128, V], "yp": [8, V]}
 ENGS = ("pe", "dve", "act", "pool", "sp")
@@ -133,7 +132,10 @@ def prog(vals):
 
 
 OPT = {"dl": True, "R": True, "r": True, "z": 4, "look": 0.1, "ki": True, "o2": False, "la": True, "df": True,
-       "g0": (1, 3, 5), "d0": False, "gt": (), "f": ((), (), ()), "np": (1, 2)}
+       "g0": (1, 3, 5), "d0": False, "gt": (), "f": ((), (), ()), "np": (1, 2),
+       "u0": True, "u1": False, "u2": False, "n8": False, "w": (0, 0, 0), "g1": (), "fill": 0.0, "near": 1e9, "seed": 0, "amp": 0.0, "c0": False}
+OPT.update({"dl": 0, "R": 0, "r": 1, "la": 0, "g0": (0, 2, 5), "f": ((7,), (7,), (3, 7)), "u0": 1, "u1": 1, "u2": 1, "n8": 1,
+            "fill": 0.45, "c0": 1})
 AL = slice(None)
 CY = 0.83e-3
 PAR = {"G": 1.56, "ov": 0.05, "hop": 0.12, "same": 0.06, "pe": 0.8, "dma": 2.0, "far": 1.0, "b2": 1.0}
@@ -340,7 +342,10 @@ def build():
     for ch in range(NCH):
         cs = slice(ch * CW, (ch + 1) * CW)
         ts(A("lT0", AL, AL, cs), A("nbT", AL, AL, cs), LOFF, None, plus)
-    ts(A("lN0"), A("nbN"), LOFF, None, plus)
+    if OPT["c0"]:
+        act(A("lN0"), A("nbN"), ACTF.Identity, 1.0, LOFF)
+    else:
+        ts(A("lN0"), A("nbN"), LOFF, None, plus)
     ts(A("rbi"), A("rbi"), 512.0, None, plus)
 
     def mat(j):
@@ -384,14 +389,19 @@ def build():
     def names(t, ch):
         lT = "lT%d" % (t % 2)
         cs, o = slice(ch * CW, (ch + 1) * CW), ch * U
-        P2 = A("p%d" % (ch + 1), AL, AL, slice(0, CW))
+        P2 = C(("pT", "pX")[ch], 0, U)
         rint(P2, A(lT, AL, AL, cs), 1.5 * 2.0 ** 35, OPT["dl"])
         tt(C("nmc", o, o + U), A(lT, AL, AL, cs), P2, sub)
-        ts(C("off1", o, o + U), C("nmc", o, o + U), 1152.0, None, plus)
+        if OPT["u1"]:
+            act(C("off1", o, o + U), C("nmc", o, o + U), ACTF.Identity, 1.0, 1152.0)
+        else:
+            ts(C("off1", o, o + U), C("nmc", o, o + U), 1152.0, None, plus)
         act(C("hi2", o, o + U), C("nmc", o, o + U), ACTF.Sign, 1.0, -7.5)
-        mm(P2, A("mf", AL, 1, AL), C("nmc", o, o + U), True, False)
-        mm(P2, mat(0), A("kc"), False, False)
-        mm(P2, mat(21), C("hi2", o, o + U), False, True)
+        for h in range(2):
+            ph_, a, z = A("pP", AL, slice(8 * h, 8 * h + 8), cs), h * U // 2, (h + 1) * U // 2
+            mm(ph_, A("mf", AL, 1, AL), C("nmc", o + a, o + z), True, False)
+            mm(ph_, mat(0), C("kc", a, z), False, False)
+            mm(ph_, mat(21), C("hi2", o + a, o + z), False, True)
         f = U + ch * CW
         for k in range(16):
             mm(C("pX", f, f + CW), mat(k), C("hi2", o + k * CW, o + (k + 1) * CW), k == 0, k == 15)
@@ -408,7 +418,7 @@ def build():
         for j in range(4):
             s = roll("G")
             src = IND(C("Wp", 0, WW), C("off1", o + 4 * j * CW, o + 4 * (j + 1) * CW))
-            if t == 0 and 4 * ch + j in OPT["g0"]:
+            if 4 * ch + j in OPT["g0" if t == 0 else "g1"]:
                 ts(C("G", s, s + 4 * U), src, 2.0 ** -10, None, mul)
             else:
                 act(C("G", s, s + 4 * U), src, ACTF.Copy, 2.0 ** -10)
@@ -416,23 +426,22 @@ def build():
                 mm(C("pC", pc + 4 * j * CW, pc + 4 * (j + 1) * CW), A("Sel", AL, i, AL), C("G", s + i, s + 4 * U, 16), False, j == 3 and i == 15)
 
     def keys(t, ch):
-        o, pc, pp = ch * U, ch * 512, "p%d" % (ch + 1)
-        rint(A("Rr"), C("pC", pc, pc + U), 1.5 * 2.0 ** 48, OPT["R"])
-        tt(A("a15"), C("pC", pc, pc + U), A("Rr"), sub)
+        pc, cs = ch * 512, slice(ch * CW, (ch + 1) * CW)
+        rr = C("Rr", ch * U, (ch + 1) * U)
+        rint(rr, C("pC", pc, pc + U), 1.5 * 2.0 ** 48, OPT["R"])
+        tt(A("a15", AL, AL, cs), C("pC", pc, pc + U), rr, sub)
+
+    def sort(cs):
         for sp, r in first:
             w, z = prog([x[0] for x in r]), prog([x[1] for x in r])
-            dst = A(pp, AL, z, slice(0, CW)) if sp == "P" else A("S", AL, z, AL)
-            tt(dst, A(pp, AL, w, slice(0, CW)), A("a15", AL, w, AL), plus)
+            tt(A("pP" if sp == "P" else "S", AL, z, cs), A("pP", AL, w, cs), A("a15", AL, w, cs), plus)
         for ismin, sp, r in steps:
-            pw, sw, ow = [[x[j] for x in r] for j in range(3)]
-            if sp == "P":
-                dst = A(pp, AL, prog(ow), slice(0, CW))
-            elif sp == "S":
-                dst = A("S", AL, prog(ow), AL)
-            else:
-                dst = A("K", AL, prog([16 * ch + x for x in ow]), AL)
-            tt(dst, A(pp, AL, prog(pw), slice(0, CW)), A("S", AL, prog(sw), AL), mn if ismin else mx)
-        Kc = A("K", AL, slice(16 * ch, 16 * ch + 16), AL)
+            pw, sw, ow = [prog([x[j] for x in r]) for j in range(3)]
+            tt(A("pP" if sp == "P" else sp, AL, ow, cs), A("pP", AL, pw, cs), A("S", AL, sw, cs), mn if ismin else mx)
+
+    def places(t, ch):
+        o = ch * U
+        Kc = A("K", AL, AL, slice(ch * CW, (ch + 1) * CW))
         ts(A("kk"), Kc, 11, 15, shr, band)
         if not OPT["ki"]:
             cp(A("kf"), A("kk"))
@@ -441,9 +450,22 @@ def build():
         tt(A("yy"), IND(C("Bs", ch * CW, (ch + 1) * CW), A("rep")), C("pw", o, o + U), mul)
         rint(C("pT", 0, U), A("yy"), 1.5 * 2.0 ** 23, OPT["r"])
         tt(A("bit"), C("pT", 0, U), A("yy"), lt)
-        mm(C("pX", 0, U), mat(17), A("bit"), True, True)
-        tt(C("nm8", o, o + U), A("lo"), C("pX", 0, U), plus)
-        cp(C("off", o, o + U), C("nm8", o, o + U))
+        if OPT["n8"]:
+            act(A("kf"), A("lo"), ACTF.Copy)
+            mm(C("pX", 0, U), A("mf", AL, 2, AL), A("kf"), True, False)
+            mm(C("pX", 0, U), mat(17), A("bit"), False, True)
+            if OPT["u0"]:
+                act(C("off", o, o + U), C("pX", 0, U), ACTF.Copy)
+            else:
+                cp(C("off", o, o + U), C("pX", 0, U))
+            act(C("nm8", o, o + U), C("pX", 0, U), ACTF.Copy)
+        else:
+            mm(C("pX", 0, U), mat(17), A("bit"), True, True)
+            tt(C("nm8", o, o + U), A("lo"), C("pX", 0, U), plus)
+            if OPT["u0"]:
+                act(C("off", o, o + U), C("nm8", o, o + U), ACTF.Copy)
+            else:
+                cp(C("off", o, o + U), C("nm8", o, o + U))
         if t < RO - 1:
             act(C("pwb", o, o + U), C("pw", o, o + U), ACTF.Copy, 2.0 ** 36)
             ts(C("fo", ch * CW, (ch + 1) * CW), C("nm8", o, o + CW), float(PAD + V - 1), -float(PAD), mn, plus)
@@ -502,7 +524,7 @@ def build():
             for i in range(16):
                 mm(C("pC", pc + s0 * CW, pc + s1 * CW), A("Sel", AL, i, AL), C("sg", ss + i, ss + n * U, 16), False, s1 == 16 and i == 15)
         cnt = C("pC", pc, pc + U)
-        tt(A("km"), A("K", AL, slice(16 * ch, 16 * ch + 16), AL), cnt, mn)
+        tt(A("km"), A("K", AL, AL, slice(ch * CW, (ch + 1) * CW)), cnt, mn)
         tt(C("km2", 0, 192), C("km", 0, 192), C("km", 192, 384), mx)
         tt(C("km2", 192, 288), C("km2", 0, 96), C("km2", 96, 192), mx)
         tt(C("km2", 288, 336), C("km2", 192, 240), C("km2", 240, 288), mx)
@@ -517,10 +539,14 @@ def build():
             act(A("ng"), cnt, ACTF.Relu, -2.0 ** -10)
             mm(C("pT", 0, U), A("mf", AL, 2, AL), C("nm8", o, o + U), True, False)
             mm(C("pT", 0, U), mat(16), A("ng"), False, True)
-            cp(C("off2", o, o + U), C("pT", 0, U))
+            src = C("pT", 0, U)
         else:
             tt(A("tt"), C("nm8", o, o + U), cnt, mn)
-            cp(C("off2", o, o + U), A("tt"))
+            src = A("tt")
+        if OPT["u2"]:
+            act(C("off2", o, o + U), src, ACTF.Relu)
+        else:
+            cp(C("off2", o, o + U), src)
 
     def hearing(t, ch):
         o, dd = ch * U, ch * 16 * U
@@ -586,10 +612,12 @@ def build():
             ts(A("keep", AL, k, AL), A("Fi"), 15 - k, 1, shr, band)
         for ch in range(NCH):
             cs = slice(ch * CW, (ch + 1) * CW)
-            tmp = A("p%d" % (ch + 1), AL, AL, slice(0, CW))
+            tmp = A("pP", AL, AL, cs)
             if OPT["df"]:
-                mm(tmp, A("mf", AL, 2, AL), A(old, AL, AL, cs), True, False)
-                mm(tmp, A("mf", AL, 3, AL), A("gT", AL, AL, cs), False, True)
+                for h in range(2):
+                    w = slice(8 * h, 8 * h + 8)
+                    mm(A("pP", AL, w, cs), A("mf", AL, 2, AL), A(old, AL, w, cs), True, False)
+                    mm(A("pP", AL, w, cs), A("mf", AL, 3, AL), A("gT", AL, w, cs), False, True)
             else:
                 tt(tmp, A(old, AL, AL, cs), A("gT", AL, AL, cs), sub)
             tt(tmp, tmp, A("keep", AL, AL, cs), mul)
@@ -605,6 +633,12 @@ def build():
         for step in (names, arrival, keys):
             for ch in range(NCH):
                 step(t, ch)
+        if OPT["w"][t]:
+            sort(slice(0, NCH * CW))
+        for ch in range(NCH):
+            if not OPT["w"][t]:
+                sort(slice(ch * CW, (ch + 1) * CW))
+            places(t, ch)
         if t < RO - 1:
             fetch(t)
         for ch in range(NCH):
@@ -666,6 +700,11 @@ def order(ops, fixed=None):
     pr = [0.0] * n
     for i in reversed(topo):
         pr[i] = ops[i]["cost"] + ops[i]["lat"] + max([pr[j] + gap(i, j) for j in succ[i]] + [0.0])
+    kinds = sorted(set((o["eng"], o["kind"], str(o["args"][0][0])) for o in ops if o["args"]))
+    shift = dict(zip(kinds, OPT["amp"] * np.random.default_rng(OPT["seed"]).standard_normal(len(kinds))))
+    for i, o in enumerate(ops):
+        if o["args"]:
+            pr[i] += float(shift[(o["eng"], o["kind"], str(o["args"][0][0]))])
     left = [len(o["deps"]) for o in ops]
     ready = {e: [] for e in ENGS + (None,)}
     rt, fin, free = [0.0] * n, [0.0] * n, {e: 0.0 for e in ENGS}
@@ -688,6 +727,10 @@ def order(ops, fixed=None):
                         best = (t0, e, can)
             t0, e, can = best
             i = max((j for j in can if rt[j] <= t0 + OPT["look"]), key=lambda j: (pr[j], -j))
+            if rt[i] > t0 + 1e-6:
+                now = [j for j in can if rt[j] <= t0 + 1e-6 and ops[j]["cost"] <= OPT["fill"] and pr[j] >= pr[i] - OPT["near"]]
+                if now:
+                    i = max(now, key=lambda j: (pr[j], -j))
             ready[e].remove(i)
             start = max(t0, rt[i])
             free[e] = start + ops[i]["cost"]

@@ -5,71 +5,78 @@ from concourse.mybir import AluOpType, ActivationFunctionType
 
 ALU, ACTF = AluOpType, ActivationFunctionType
 V, GH, NR, RO = 768, 512, 4, 3
-CW, NCH = 24, 2
-U = 16 * CW
-PAD = 8
-WW = PAD + V + 3 * GH
-WP = PAD + V + 2 * GH + V
-f32, bf, i32, u16 = "float32", "bfloat16", "int32", "uint16"
+PAD = 16
+HI = 2048
+WW = PAD + HI + 2 * GH
+GCOL = (PAD + V, PAD + HI, PAD + HI + GH)
+CH = ((0, 512), (512, 768))
+BL, UN = 128, 64
+NS = 6
+f32, bf, i32, u16, f16 = "float32", "bfloat16", "int32", "uint16", "float16"
+MATS = ["p15", "n15", "n11", "n12", "neg", "m7", "blk", "nblk", "tri", "w1", "w2", "y", "ny", "wb", "r0"]
+ROWS = ["cn", "ca", "cp", "m1", "m2", "cf", "c1", "cb", "co", "ct", "cr", "c0", "g25", "g12", "gp", "g0", "g10"]
+TWO = 6
+
+
+def N(dt, n=V):
+    return ("sbuf", [128, n], dt)
+
 
 SCRATCH = {
-    "nbT": ("sbuf", [128, 16, 48], i32), "nbN": ("sbuf", [128, V], i32),
-    "lT0": ("sbuf", [128, 16, 48], f32), "lT1": ("sbuf", [128, 16, 48], f32),
-    "lN0": ("sbuf", [128, V], f32), "lN1": ("sbuf", [128, V], f32),
-    "W0": ("sbuf", [128, WW], bf), "W1": ("sbuf", [128, WW], f32), "W2": ("sbuf", [128, WW], f32),
-    "Ls0": ("sbuf", [128, GH], bf), "Ls1": ("sbuf", [128, GH], f32), "Ls2": ("sbuf", [128, GH], f32),
-    "fad": ("sbuf", [128, V], bf), "Wp": ("sbuf", [128, WP], bf),
-    "Yb": ("sbuf", [128, RO, 192], bf), "land": ("sbuf", [128, 3 * RO, 96], bf),
-    "ph": ("sbuf", [128, 48], i32), "phb": ("sbuf", [128, 96], bf), "rbi": ("sbuf", [128, 48], i32),
-    "pr": ("sbuf", [128, 48], i32), "ti": ("sbuf", [128, 48], i32), "tj": ("sbuf", [128, 48], i32),
-    "kmx": ("sbuf", [128, 48], i32), "phf": ("sbuf", [128, 48], f32),
-    "G": ("sbuf", [128, 3 * 4 * U], bf), "xw": ("sbuf", [128, 3 * 4 * U], f32), "sg": ("sbuf", [128, 3 * 4 * U], bf),
-    "dw": ("sbuf", [128, NCH * 16 * U], f32),
-    "nmc": ("sbuf", [128, V], f32), "off1": ("sbuf", [128, V], u16), "hi2": ("sbuf", [128, V], bf),
-    "Rr": ("sbuf", [128, V], f32), "a15": ("sbuf", [128, 16, 48], f32), "S": ("sbuf", [128, 32, 48], f32),
-    "K": ("sbuf", [128, 16, 48], i32), "lo": ("sbuf", [128, U], i32), "kk": ("sbuf", [128, U], i32),
-    "kf": ("sbuf", [128, U], f32), "pw": ("sbuf", [128, V], bf), "pwb": ("sbuf", [128, V], bf),
-    "Bs": ("sbuf", [128, 48], f32), "bit": ("sbuf", [128, U], bf),
-    "nm8": ("sbuf", [128, V], f32), "off": ("sbuf", [128, V], u16), "off2": ("sbuf", [128, V], u16),
-    "tt": ("sbuf", [128, U], f32), "km": ("sbuf", [128, U], f32), "km2": ("sbuf", [128, U], f32),
-    "qq": ("sbuf", [128, U], bf), "Fi": ("sbuf", [128, 48], i32), "Fc": ("sbuf", [128, 48], i32),
-    "keep": ("sbuf", [128, 16, 48], i32), "fo": ("sbuf", [128, 48], u16),
-    "gp": ("sbuf", [128, V], f32), "gn": ("sbuf", [128, V], f32), "gT": ("sbuf", [128, 16, 48], f32),
-    "Xp": ("sbuf", [128, V], f32), "t1": ("sbuf", [128, V], f32),
-    "Ea": ("sbuf", [128, NCH * 4 * U], f32),
-    "idv": ("sbuf", [128, 128], f32), "idb": ("sbuf", [128, 128], bf), "mb": ("sbuf", [128, 23, 128], bf),
-    "ng": ("sbuf", [128, U], bf), "mf": ("sbuf", [128, 4, 128], f32), "Sel": ("sbuf", [128, 16, 128], bf), "Ys": ("sbuf", [128, 8, 128], bf),
-    "yv": ("sbuf", [128, 128], f32), "rep": ("sbuf", [128, CW], u16),
-    "yy": ("sbuf", [128, U], f32), "rpf": ("sbuf", [128, 2 * CW], f32), "gv": ("sbuf", [128, 8], f32),
-    "ga": ("sbuf", [128, 8], f32), "gb": ("sbuf", [128, 8], bf), "pc": ("sbuf", [128, 8], i32),
-    "pf": ("sbuf", [128, 8], f32), "pmi": ("sbuf", [128, 48], i32), "nat": ("sbuf", [128, 48], u16),
-    "mv": ("sbuf", [128, 96], f32), "msk": ("sbuf", [128, 192], f32), "kc": ("sbuf", [128, U], bf),
-    "ones": ("sbuf", [128, U], bf),
-    "pM": ("psum", [128, 1024], f32), "pC": ("psum", [128, 1024], f32), "pP": ("psum", [128, 16, 64], f32),
-    "pX": ("psum", [128, 512], f32), "pT": ("psum", [128, 512], f32),
+    "X0": N(f32, 16 * V), "X1": N(f32, 16 * V), "rg": N(bf, 16 * NS * BL), "Xb": N(bf),
+    "W0": N(bf, WW), "W1": N(f32, WW), "W2": N(f32, WW), "Wp": N(bf, WW),
+    "Ls0": N(bf, GH), "Ls1": N(f32, GH), "fad": N(bf),
+    "Yb": ("sbuf", [128, RO, BL], bf), "land": ("sbuf", [128, 3 * RO, BL], bf),
+    "Yi": N(i32, 64), "rbh": N(f16),
+    "ls": N(f32), "lw": N(f32, V + 8), "Z": N(i32), "nbi": N(i32),
+    "dH": N(f16), "nmS": N(f16), "hi": N(bf), "off1": N(u16), "kH": N(bf), "pw": N(bf), "nmH": N(f16),
+    "off": N(u16), "off2": N(u16), "RD": N(f16), "c0": N(f16), "Dp": N(f32), "t1": N(f32),
+    "fo": N(u16, 48), "K": ("sbuf", [128, 48, 16], f32), "S": ("sbuf", [128, 48, 32], f32),
+    "nH": ("sbuf", [128, 48, 16], f16), "aH": ("sbuf", [128, 48, 16], f16),
+    "II": N(bf, 256), "mb": ("sbuf", [128, len(MATS), 128], bf), "Sel": ("sbuf", [128, 16, 128], bf),
+    "m8": ("sbuf", [128, 4, 128], bf), "mf": N(f32, 128), "cv": ("sbuf", [128, len(ROWS), 128], bf),
+    "ones": N(bf, 512), "nones": N(bf, 512), "kc": N(bf, 512), "msk": N(bf, 16 * BL), "c7": N(bf, 16 * UN),
+    "gs": N(bf, 8), "iv": N(f32, 128), "p2": N(bf, 128), "b8": N(bf, 128), "pc": N(i32, 8), "pf": N(f32, 8), "pb": N(bf, 8),
+    "pa": ("psum", [128, 2048], f32), "ps": ("psum", [128, 128, 16], f32),
 }
 EXT = {"loud": [128, V], "fade": [128, V], "ph0": [8, V], "rb": [8, V], "nb": [128, V], "ye": [128, V], "yp": [8, V]}
 ENGS = ("pe", "dve", "act", "pool", "sp")
-NSEM = 110
+NSEM = 60
 SEMAPHORES = ["e_" + e for e in ENGS[:4]] + ["b%d" % i for i in range(NSEM)]
+AL = slice(None)
+CY = 0.83e-3
+PAR = {"G": 1.56, "ov": 0.05, "hop": 0.12, "same": 0.06, "pe": 0.7, "dma": 2.0, "kb": 0.22, "far": 1.0, "b2": 1.0, "f": 1.0}
+CASES = (({}, 228.0), ({"pe": 0.85, "G": 1.15}, 210.0), ({"dma": 3.5, "kb": 0.4, "far": 2.0, "hop": 0.25, "same": 0.12}, 250.0),
+         ({"G": 2.0, "f": 1.3, "pe": 0.55}, 330.0))
+OPT = {"ac": (384, 384, 384), "round": 56.0, "soon": 1, "un": (), "lastu": 32, "flat": 0.2, "rv": (3,), "hw": (6, 6, 6), "give": 0.002, "fa": (), "qa": 0, "ja": (), "bv": 1, "hu": 64, "tu": 128, "lu": 128, "su": (5,), "em": "vddsss",
+       "tc": (1, 1, 1), "cs": ((0, 1, 2), (), ()),
+       "look": 0.1, "fill": 0.45, "pc": ((128,), (128,), (128,)), "mc": ((640,), (640,), (256, 640)),
+       "turns": 40, "moves": 24000, "amp": 3.0, "part": 0.05, "heat": 0.0005, "seed": 10}
+ASG = {"tg": "act", "lg": "act", "sg": "act", "lgm01": "dve", "lgm03": "dve", "tga01": "dve", "tga02": "dve", "tga04": "dve",
+       "sgm04": "dve", "sgm05": "dve", "nH": "any", "s0": "any", "tga11": "dve", "tga21": "dve",
+       "mk": "any", "u": "any", "dH": "dve"}
+BIAS = {}
+STEP = {"tg": (0.0, 2.7, 0), "s0": (0.0, 0.0, 0), "s": (8.0, 8.0, 0), "lg": (16.0, 5.0, 0), "m": (20.0, 4.4, 0), "sg": (26.0, 4.4, 0),
+        "h": (44.0, 4.4, 0), "lg2": (16.0, 6.5, 0), "m2": (20.0, 6.5, 0), "sg2": (24.0, 6.5, 0), "h2": (34.0, 6.5, 0),
+        "lg0": (16.0, 4.0, 0), "m0": (20.0, 4.0, 0), "sg0": (21.0, 4.0, 0), "h0": (60.0, 3.0, 0), "h1": (36.0, 4.4, 0),
+        "xg": (34.0, 6.5, 0)}
 
-SORT_P = "111111110101010100000111111100000000001111111100000000000000000"
-SORT_V = "000000001111111100001111111100001111110000000011110000001111111"
+SORT_P = "000000000000000000001111000011110000111100000011111111111111111"
+SORT_V = "000000001111111100000000111111110000110000010011110000001111111"
 
 
-def batcher(n):
-    st, p = [], 1
-    while p < n:
-        k = p
-        while k >= 1:
-            s = []
-            for j in range(k % p, n - k, 2 * k):
-                for i in range(min(k, n - j - k)):
-                    if (i + j) // (2 * p) == (i + j + k) // (2 * p):
-                        s.append((i + j, i + j + k))
-            st.append(s)
-            k //= 2
-        p *= 2
+def pairwise(n):
+    st, a = [], 1
+    while a < n:
+        st.append([(i, i + a) for i in range(n) if not i & a])
+        a *= 2
+    a, e = a // 4, 1
+    while a > 0:
+        d = e
+        while d > 0:
+            st.append([(b - d * a, b) for b in range((d + 1) * a, n) if (b // a - d - 1) % 2 == 0])
+            d //= 2
+        a, e = a // 2, 2 * e + 1
     return st
 
 
@@ -96,7 +103,7 @@ def runs(items):
 
 
 def sort_steps():
-    comps = [(si, l, h) for si, s in enumerate(batcher(16)) for l, h in s]
+    comps = [(si, l, h) for si, s in enumerate(pairwise(16)) for l, h in s]
     b, v = [int(x) for x in SORT_P], [int(x) for x in SORT_V]
     nxt, last = {}, {}
     for c in range(len(comps) - 1, -1, -1):
@@ -131,16 +138,6 @@ def prog(vals):
     return slice(vals[0], vals[-1] + 1, step)
 
 
-OPT = {"dl": True, "R": True, "r": True, "z": 4, "look": 0.1, "ki": True, "o2": False, "la": True, "df": True,
-       "g0": (1, 3, 5), "d0": False, "gt": (), "f": ((), (), ()), "np": (1, 2),
-       "u0": True, "u1": False, "u2": False, "n8": False, "w": (0, 0, 0), "g1": (), "fill": 0.0, "near": 1e9, "seed": 0, "amp": 0.0, "c0": False}
-OPT.update({"dl": 0, "R": 0, "r": 1, "la": 0, "g0": (0, 2, 5), "f": ((7,), (7,), (3, 7)), "u0": 1, "u1": 1, "u2": 1, "n8": 1,
-            "fill": 0.45, "c0": 1})
-AL = slice(None)
-CY = 0.83e-3
-PAR = {"G": 1.56, "ov": 0.05, "hop": 0.12, "same": 0.06, "pe": 0.8, "dma": 2.0, "far": 1.0, "b2": 1.0}
-
-
 def shape_of(name):
     return SCRATCH[name][1] if name in SCRATCH else EXT[name]
 
@@ -151,6 +148,20 @@ def A(name, *idx):
 
 def C(name, a, b, step=1):
     return (name, (AL, slice(a, b, step)))
+
+
+def B3(name, a, b, last=AL):
+    return (name, (AL, slice(a, b), last))
+
+
+def PS(bank, n, off=0):
+    if bank < 4:
+        return C("pa", 512 * bank + off, 512 * bank + off + n)
+    return B3("ps", 32 * (bank - 4) + off // 16, 32 * (bank - 4) + (off + n) // 16)
+
+
+def Wd(name, v, n, k=None, head=0, tail=0):
+    return C(name, 16 * v + head, 16 * (v + n) - tail) if k is None else C(name, 16 * v + k, 16 * (v + n), 16)
 
 
 def IND(win, offs):
@@ -166,23 +177,22 @@ def cells(ap):
 
 
 def build():
-    ops, GC, OV = [], PAR["G"], PAR["ov"]
+    ops = []
     lastw, readers, bank, pebank = {}, {}, {}, {}
 
-    def add(eng, kind, args, outs, ins, cost, lat=0.0, batch=None, extra=()):
+    def add(eng, kind, args, outs, ins, cyc, lat=0.0, batch=None, extra=(), key=None):
         n = len(ops)
         raw, war = set(extra), set()
         rd = []
         for a in ins:
-            rd += [a[1], a[2]] if a[0] == "*" else [a]
+            rd += [a[1], a[2]] if a[0] == "*" else ([a[2], a[3]] if a[0] == "?" else [a])
         for a in rd + list(outs):
             if a[0] not in lastw:
                 size = 1 if a[0] in EXT else int(np.prod(shape_of(a[0])[1:]))
                 lastw[a[0]] = np.full(size, -1, np.int64)
                 readers[a[0]] = {}
         for a in rd:
-            c = cells(a)
-            raw.update(int(x) for x in np.unique(lastw[a[0]][c]) if x >= 0)
+            raw.update(int(x) for x in np.unique(lastw[a[0]][cells(a)]) if x >= 0)
         for a in outs:
             c = cells(a)
             m = np.zeros(len(lastw[a[0]]), bool)
@@ -203,14 +213,11 @@ def build():
             readers[a[0]][n] = c if old is None else np.concatenate([old, c])
         for a in outs:
             lastw[a[0]][cells(a)] = n
-        bks = set()
-        for a in rd + list(outs):
-            if a[0] in SCRATCH and SCRATCH[a[0]][0] == "psum":
-                bks.update((a[0], int(x)) for x in np.unique(cells(a) // 512))
-        for bk in bks:
+        who = eng if key is None else n
+        for bk in set((a[0], int(x)) for a in rd + list(outs) if a[0] in ("pa", "ps") for x in np.unique(cells(a) // 512)):
             cur = bank.get(bk)
-            if cur is None or cur[0] != eng:
-                bank[bk] = [eng, [n], cur[1] if cur else []]
+            if cur is None or cur[0] != who:
+                bank[bk] = [who, [n], cur[1] if cur else []]
             else:
                 cur[1].append(n)
             war.update(bank[bk][2])
@@ -219,50 +226,54 @@ def build():
                     war.add(pebank[bk])
                 pebank[bk] = n
         if batch is not None:
+            for x in raw | war:
+                if ops[x]["batch"] == batch:
+                    war = war | ops[x]["deps"]
             raw = set(x for x in raw if ops[x]["batch"] != batch)
             war = set(x for x in war if ops[x]["batch"] != batch)
-        ops.append(dict(eng=eng, kind=kind, args=args, raw=raw, war=war - raw - {n}, cost=cost, lat=lat, batch=batch))
+        ops.append(dict(eng=eng, kind=kind, args=args, deps=(raw | war) - {n}, cyc=cyc, lat=lat, batch=batch, key=key, tag=tag[0]))
         return n
+
+    tag = [""]
 
     def size(ap):
         return len(cells(ap))
 
-    def isps(a):
-        return a[0] in SCRATCH and SCRATCH[a[0]][0] == "psum"
+    def two(*aps):
+        return all(SCRATCH[a[0]][2] in (bf, u16, f16) for a in aps)
 
-    def two(a):
-        return SCRATCH[a[0]][2] in (bf, u16)
+    def one(out, a):
+        return (size(out), "g" if a[0] == "*" else ("h" if two(out, a) else "1"))
 
     def tt(out, a, b, op):
-        n = size(out)
-        cyc = n * GC if a[0] == "*" else (n if isps(a) or isps(b) else (PAR["b2"] if two(out) and two(a) and two(b) else 2) * n)
-        return add("dve", "tt", (out, a, b, op), [out], [a, b], OV + max(64, cyc) * CY)
+        w = "g" if a[0] == "*" else ("1" if {"pa", "ps"} & {a[0], b[0]} else ("b" if two(out, a, b) else "2"))
+        return add("dve", "tt", (out, a, b, op), [out], [a, b], (size(out), w))
 
     def ts(out, a, s1, s2, op0, op1=None):
-        n = size(out)
-        ins = [a] + [s for s in (s1, s2) if isinstance(s, tuple)]
-        cyc = n * GC if a[0] == "*" else (n / 2 if two(out) and two(a) else n)
-        return add("dve", "ts", (out, a, s1, s2, op0, op1), [out], ins, OV + max(64, cyc) * CY)
+        return add("dve", "ts", (out, a, s1, s2, op0, op1), [out], [a] + [s for s in (s1, s2) if isinstance(s, tuple)], one(out, a))
 
-    def cp(out, a):
-        n = size(out)
-        cyc = n * GC if a[0] == "*" else (n / 2 if two(out) and two(a) else n)
-        return add("dve", "cp", (out, a), [out], [a], OV + max(64, cyc) * CY)
+    def scan(out, m, x, sums=False):
+        return add("dve", "scan", (out, m, x, sums), [out], [m, x], (size(out), "h" if two(out, m, x) else "1"))
 
     def ms(out, val):
-        n = size(out)
-        return add("dve", "ms", (out, val), [out], [], OV + max(64, n / 2 if two(out) else n) * CY)
+        return add("dve", "ms", (out, val), [out], [], one(out, out))
 
     def act(out, a, fn, scale=1.0, bias=0.0):
-        n = size(out)
-        return add("act", "act", (out, a, fn, scale, bias), [out], [a], 1.3 * OV + max(64, n * GC if a[0] == "*" else n) * CY)
+        return add("act", "act", (out, a, fn, scale, bias), [out], [a], one(out, a))
+
+    def aff(key, eng, out, a, scale=1.0, bias=0.0, fn=None):
+        return add(eng, "aff", (out, a, scale, bias, fn), [out], [a], one(out, a), key=key)
 
     def mm(out, l, r, start, stop):
-        n = max(64, size(r)) * (4 if SCRATCH[r[0]][2] == f32 else 1)
-        return add("pe", "mm", (out, l, r, start, stop), [out], [l, r], 0.01 + n * CY * PAR["pe"])
+        k = l[2] if l[0] == "?" else l
+        n = max(min(64, size(k)), size(r)) * (4 if SCRATCH[r[0]][2] == f32 else 1)
+        return add("pe", "mm", (out, l, r, start, stop), [out], [l, r], (n, "p"))
 
     def iota(out, pat, base, cm):
-        return add("pool", "iota", (out, pat, base, cm), [out], [], 0.13 + 2 * size(out) * CY)
+        return add("pool", "iota", (out, pat, base, cm), [out], [], (2 * size(out) + 160, "q"))
+
+    def sel(out, a, pat, op, fill, base, cm):
+        return add("pool", "sel", (out, a, pat, op, fill, base, cm), [out], [a], (2 * size(out) + 200, "q"))
 
     nb = [0]
 
@@ -270,479 +281,606 @@ def build():
         nb[0] += 1
         return nb[0] - 1
 
-    def dma(eng, out, a, batch=None, acc=False, kb=1.0):
+    landed = []
+
+    def dma(eng, out, a, batch=None, acc=False, kb=1.0, after=()):
         b = newb() if batch is None else batch
-        ins = [a, out] if acc else [a]
-        return add(eng, "dma", (out, a, acc), [out], ins, 1.0 if eng == "pool" else 0.12, PAR["dma"] + 0.22 * kb * (2 if acc else 1), b)
+        return add(eng, "dma", (out, a, acc), [out], [a, out] if acc else [a], (1200 if eng == "pool" else 140, "c"),
+                   ("d", kb * (2 if acc else 1)), b, after)
 
     def exchange(src, dsts, lat):
-        s = add("pool", "send", (src, dsts, newb()), [], [src], 1.0, lat * PAR["far"], newb())
-        return add(None, "recv", (), dsts, [], 0.0, 0.5, ops[s]["args"][2], extra=[s])
+        s = add("pool", "send", (src, dsts, newb()), [], [src], (1200, "c"), ("f", lat), newb())
+        return add(None, "recv", (), dsts, [], (0, "c"), ("c", 0.5), ops[s]["args"][2], extra=[s])
 
-    ge, lt, eq = ALU.is_ge, ALU.is_lt, ALU.is_equal
+    ge, gt, eq, ne = ALU.is_ge, ALU.is_gt, ALU.is_equal, ALU.not_equal
     mul, plus, sub, mx, mn = ALU.mult, ALU.add, ALU.subtract, ALU.max, ALU.min
     band, shr = ALU.bitwise_and, ALU.arith_shift_right
     Wn = ["W0", "W1", "W2"]
+    LN2 = math.log(2.0)
+    P8 = slice(0, 8)
 
-    dma("sp", A("ph"), A("ph0"))
+    def mat(name, rows=AL, cols=AL):
+        return A("mb", rows, MATS.index(name), cols)
+
+    def row(name, part=None, cols=AL):
+        j = ROWS.index(name)
+        return A("cv", (slice(0, 33) if j < TWO else slice(0, 1)) if part is None else slice(part, part + 1), j, cols)
+
+    def const(out, name, start=False, stop=False, neg=False):
+        r = row(name)
+        mm(out, r, A("nones" if neg else "ones", r[1][0], slice(0, size(out))), start, stop)
+
+    def grid(out, name, stop=False):
+        const(out, name)
+        const(out, name, stop=stop, neg=True)
+
+    eye, f1 = C("II", 0, 128), A("mf")
+
     b = newb()
-    dma("sp", A("Ls0", slice(0, 112), AL), A("loud", slice(16, 128), slice(0, GH)), b)
+    dma("sp", A("Yi", slice(0, 112), slice(0, 32)), A("ph0", slice(1, 8), slice(0, GH)), b)
+    dma("act", A("Yi", slice(112, 128), slice(0, 32)), A("ph0", slice(0, 1), slice(0, GH)), b)
+    ms(C("Wp", 0, PAD), 0.0)
+    ms(C("Wp", GCOL[0], GCOL[0] + GH), 0.0)
+    ms(C("Wp", GCOL[1], WW), 0.0)
+    ts(C("Yi", 32, 64), C("Yi", 0, 32), 31, None, band)
+    tt(A("Yb", AL, 0, slice(0, 32)), C("Yi", 0, 32), C("Yi", 32, 64), sub)
+    aff("p0", "dve", A("Yb", AL, 0, slice(32, 64)), C("Yi", 32, 64))
+    exchange(A("Yb", AL, 0, slice(0, 64)), [A("land", AL, d, slice(0, 64)) for d in range(3)], 3.0)
+    b = newb()
+    for d in range(3):
+        for j in range(2):
+            dma(("sp", "act")[j], A("Wp", slice(4 * j, 128, 16), slice(GCOL[d], GCOL[d] + GH)), A("land", AL, d, slice(32 * j, 32 * j + 32)), b)
+    dma("sp", A("Z", P8, AL), A("ph0"))
+    b = newb()
+    dma("act", A("Ls0", slice(0, 112), AL), A("loud", slice(16, 128), slice(0, GH)), b)
     dma("act", A("Ls0", slice(112, 128), AL), A("loud", slice(0, 16), slice(0, GH)), b)
-    b = newb()
-    for k in range(16):
-        dma("sp" if k % 2 else "act", A("nbT", AL, k, AL), A("nb", slice(k, 128, 16), AL), b)
+    dma("sp", A("nbi"), A("nb"), kb=3)
     dma("sp", C("W0", PAD, PAD + V), A("loud"))
-    dma("sp", A("rbi"), A("rb"))
-    dma("sp", A("nbN"), A("nb"))
     dma("sp", A("fad"), A("fade"))
-    iota(A("yv"), [[-16, 8], [-1000, 2], [-2, 8]], 0, 1)
+    ms(A("ones"), 1.0)
+    ms(A("nones", slice(0, 1), AL), -1.0)
+    ms(A("cv", slice(0, 64), slice(0, TWO), AL), 0.0)
+    ms(A("m8", P8, slice(0, 2), AL), 0.0)
+    sel(eye, C("ones", 0, 128), [[-1, 128]], eq, 0.0, 0, 1)
+    aff("mat", "act", C("II", 128, 256), eye)
+    for j, r, w in ((0, 0, -1.0), (0, 4, 1.0), (0, 8, -1.0), (1, 8, 1.0)):
+        aff("mat", "act", A("m8", P8, j, slice(r, 128, 16)), A("II", P8, P8), w)
+    for name, parts in (("cp", ((0, 0, 512.0), (32, 0, -0.5))),
+                        ("gp", ((0, None, 0.0), (0, 0, 1.5 * 2.0 ** 33), (0, 4, 1.5 * 2.0 ** 28), (0, 8, 1.5 * 2.0 ** 28))),
+                        ("cn", ((0, None, 2.0 ** 22), (32, None, 2064.0))), ("c1", ((0, None, -2.0 ** 14),)),
+                        ("g25", ((0, None, 1.5 * 2.0 ** 48),)), ("ca", ((0, None, 1536 * 2.0 ** 15), (32, None, 2.0 ** 15))),
+                        ("cb", ((0, None, 2.0 ** 18),)), ("co", ((0, None, -2944.0), (0, 0, 0.0))),
+                        ("ct", ((0, None, 0.0), (0, 0, 16.0))), ("cr", ((0, None, -2048.0), (0, 0, 16.0))), ("c0", ((0, None, 0.0),)), ("g12", ((0, None, 1.5 * 2.0 ** 35),)),
+                        ("m1", ((0, None, -0.5),)), ("m2", ((0, None, 0.5), (32, None, -2.0 ** -17))),
+                        ("g0", ((0, None, 1.5 * 2.0 ** 23),)), ("cf", ((0, None, 512.0), (32, None, -0.5))),
+                        ("g10", ((0, None, 1.5 * 2.0 ** 33),))):
+        for part, col, val in parts:
+            ms(row(name, part, AL if col is None else slice(col, 128, 16)), val)
+    sel(A("gs"), C("ones", 0, 8), [[-16, 8]], ge, 0.0, 0, 1)
+    sel(A("gs"), A("gs"), [[16, 8]], ge, 0.0, 15, -1)
+    sel(mat("blk"), C("ones", 0, 128), [[-16, 8], [0, 16]], ge, 0.0, 0, 1)
+    sel(mat("blk"), mat("blk"), [[16, 8], [0, 16]], ge, 0.0, 15, -1)
+    iota(A("kc"), [[0, 32], [2048, 16]], 2048, 0)
     iota(C("pc", 0, 1), [[0, 1]], 0, 1)
-    iota(A("mv"), [[1, 96]], 0, 0)
-    iota(A("gv"), [[-16, 8]], 0, 1)
-    iota(A("idv"), [[1, 128]], 0, -1)
-    iota(A("kc"), [[2048, 16], [0, CW]], -16384, 0)
-    iota(A("pmi"), [[1, 16], [256, 3]], 0, 0)
-    iota(C("rpf", 0, CW), [[0, 8], [16, 3]], 0, 0)
-    for il in range(2):
-        for pt in range(2):
-            ts(A("Ys", AL, 2 * il + pt, AL), A("yv"), float(il - 1000 * pt), None, eq)
-            ya = C("xw", 128 * (2 * il + pt), 128 * (2 * il + pt + 1))
-            act(ya, A("yv"), ACTF.Abs, 1.0, float(48 - il + 1000 * pt))
-            ts(A("Ys", AL, 4 + 2 * il + pt, AL), ya, 64.0, None, eq)
-    ts(C("pc", 2, 3), C("pc", 0, 1), 7, None, band)
-    ts(C("pc", 4, 5), C("pc", 0, 1), 15, None, band)
-    ts(C("pf", 0, 1), C("pc", 2, 3), 96.0, None, mul)
-    ts(C("pf", 2, 3), C("pc", 4, 5), 16.0, None, mul)
-    ts(C("pf", 4, 5), C("pc", 4, 5), 7.0, 0.5, eq, mul)
-    cp(C("pf", 6, 7), C("pc", 4, 5))
-    ts(C("rpf", 0, CW), C("rpf", 0, CW), C("pf", 6, 7), None, plus)
-    ts(C("rpf", CW, 2 * CW), C("rpf", 0, CW), 24.0, -24.0, ge, mul)
-    tt(C("rpf", 0, CW), C("rpf", 0, CW), C("rpf", CW, 2 * CW), plus)
-    cp(A("rep"), C("rpf", 0, CW))
-    ms(C("msk", 0, 96), 1.0)
-    ts(C("msk", 96, 192), A("mv"), C("pf", 0, 1), float(GH), plus, lt)
-    ts(A("nat"), A("pmi"), C("pf", 2, 3), None, plus)
-    ms(A("Wp"), 1.0)
-    ts(A("Wp"), A("Wp"), C("pf", 4, 5), None, mul)
+    iota(A("iv"), [[0, 8], [1, 16]], -40, 0)
+    for name, w in (("p15", 2.0 ** 15), ("n15", -2.0 ** 15), ("n11", -2048.0), ("n12", -4096.0), ("neg", -1.0), ("m7", 7.0)):
+        aff("mat", "act", mat(name), eye, w)
+    aff("mat", "act", f1, eye)
+    aff("mat", "act", mat("nblk"), mat("blk"), -1.0)
+    aff("mat", "act", mat("tri"), mat("blk"), -4096.0)
+    sel(mat("tri"), mat("tri"), [[-1, 128]], ge, 0.0, 0, 1)
+    sel(mat("tri"), mat("tri"), [[-1, 128]], ne, 4096.0, 0, 1)
+    sel(A("m8", P8, 2, AL), A("ones", P8, slice(0, 128)), [[1, 128]], ge, 0.0, 0, -16)
+    sel(A("m8", P8, 2, AL), A("m8", P8, 2, AL), [[-1, 128]], ge, 0.0, 15, 16)
+    aff("mat", "act", A("m8", P8, 3, AL), A("m8", P8, 2, AL), -1.0)
+    aff("mat", "act", A("b8"), mat("blk"), 256.0)
+    for s in range(16):
+        sel(A("Sel", AL, s, AL), A("b8"), [[0, 8], [1, 16]], eq, 0.0, -s, 0)
+    ms(A("mb", AL, slice(MATS.index("w1"), MATS.index("w2") + 1), AL), 0.0)
+    for name, r, w in (("w1", 0, -1.0), ("w1", 4, 1.0), ("w1", 8, -1.0), ("w2", 8, 1.0)):
+        aff("mat", "act", mat(name, AL, slice(r, 128, 16)), A("gs"), w)
+    act(A("p2"), A("iv"), ACTF.Sigmoid, LN2)
+    act(row("m1", 32), A("p2", slice(32, 33), AL), ACTF.Copy, 2.0 ** 23)
+    tt(A("p2"), A("p2"), mat("blk"), mul)
+    aff("mat", "act", mat("y"), A("p2"), 2.0 ** 51)
+    aff("mat", "act", mat("ny"), A("p2"), -2.0 ** 51)
+    ts(C("pc", 2, 3), C("pc", 0, 1), 15, None, band)
+    act(C("pb", 0, 1), C("pc", 2, 3), ACTF.Sigmoid, LN2, -40 * LN2)
+    ts(C("pf", 0, 1), C("pc", 2, 3), 15.0, -2.0 ** 68, eq, mul)
+    ts(C("pf", 2, 3), C("pf", 0, 1), 2.0 ** 67, C("pb", 0, 1), plus, mul)
+    ts(mat("wb"), mat("blk"), C("pf", 2, 3), None, mul)
+    ts(C("pf", 4, 5), C("pc", 2, 3), 0.0, 2.0 ** -13, eq, mul)
+    ts(mat("r0"), mat("blk"), C("pf", 4, 5), 2.0 ** 12, mul, mul)
+    for w in range(0, BL, 32):
+        sel(Wd("msk", w, 32), A("ones"), [[0, 32], [1, 16]], gt, 0.0, 0, 0)
+    if OPT["cs"][0]:
+        iota(A("c7"), [[0, 16 * UN]], 128, 0)
     for w in Wn:
         ms(C(w, 0, PAD), 0.0)
-    ms(A("ones"), 1.0)
-    ts(A("ga"), A("gv"), 0.0, 2.0 ** 25, ge, mul)
-    ts(A("gv"), A("gv"), 15.5, None, lt)
-    tt(A("gb"), A("ga"), A("gv"), mul)
-    ms(A("Sel"), 0.0)
-    for i in range(16):
-        act(A("Sel", AL, i, slice(i, 128, 16)), A("gb"), ACTF.Copy)
-    ts(A("idb"), A("idv"), 0.0, None, eq)
-    for j, w in enumerate([2.0 ** k for k in range(16)] + [-2.0 ** 15, 1152.0, 9 * 2.0 ** 25, 2.0 ** -9, 576.0, -576.0, -1.0]):
-        act(A("mb", AL, j, AL), A("idb"), ACTF.Copy, w)
-    for j, w in enumerate([8.0, -7.0, 1.0, -1.0]):
-        act(A("mf", AL, j, AL), A("idb"), ACTF.Copy, w)
-    LOFF = -float(512 * 4096 + 1144)
-    for ch in range(NCH):
-        cs = slice(ch * CW, (ch + 1) * CW)
-        ts(A("lT0", AL, AL, cs), A("nbT", AL, AL, cs), LOFF, None, plus)
-    if OPT["c0"]:
-        act(A("lN0"), A("nbN"), ACTF.Identity, 1.0, LOFF)
-    else:
-        ts(A("lN0"), A("nbN"), LOFF, None, plus)
-    ts(A("rbi"), A("rbi"), 512.0, None, plus)
+    ms(C("lw", V, V + 8), 0.0)
+    aff("p0", "dve", A("RD", P8, AL), A("Z", P8, AL))
+    aff("fad", "dve", A("fad"), A("fad"), 0.125)
+    for c, (a, z) in enumerate(CH):
+        ts(C("Z", a, z), C("nbi", a, z), 4095, None, band)
+        ts(PS(2 + c, z - a), C("Z", a, z), 1280.0, 768.0, ge, mul)
+        tt(C("ls", a, z), C("nbi", a, z), PS(2 + c, z - a), plus)
+    dma("sp", A("nbi", P8, AL), A("rb"))
+    aff("rb", "act", A("rbh", P8, AL), A("nbi", P8, AL))
+    for w in ("W0", "Wp", "W1", "W2"):
+        dma("sp", C(w, GCOL[0] + GH, GCOL[1]), A("fade" if SCRATCH[w][2] == bf else "ls"), kb=2)
 
-    def mat(j):
-        return A("mb", AL, j, AL)
+    def times(t, c, a, z, srcs):
+        p, last = PS(4 + c, z - a), t == RO
+        const(p, "cf" if last else "cp", start=True)
+        for j in range(2):
+            use = srcs if j == 0 else srcs[::-1]
+            for i, (x, few) in enumerate(use):
+                m = A("m8", P8, 3 - j if last else j, AL) if few else mat((("w1", "w2"), ("nblk", "blk"))[last][j])
+                mm(p, m, x, False, j == 1 and i == len(use) - 1)
+            if j == 0:
+                grid(p, "g10" if last else "gp")
+        if last:
+            aff("yp", "act", C("Dp", a, z), p)
+            dma("sp", A("yp", AL, slice(a, z)), A("Dp", slice(0, 128, 16), slice(a, z)))
+            return
+        aff("wp", "act", C("Wp", PAD + a, PAD + z), p)
+        if z == GH and t > 0:
+            for q in range(4):
+                mm(PS(4 + c, BL), C("II", 16 - q, 144 - q), C("Wp", PAD + BL * q, PAD + BL * (q + 1)), q == 0, q == 3)
+            aff("yb", "act", A("Yb", AL, t, AL), PS(4 + c, BL))
+            exchange(A("Yb", AL, t, AL), [A("land", AL, 3 * t + d, AL) for d in range(3)], 3.0)
+            bt = newb()
+            for d in range(3):
+                landed.append(dma("sp", A("Wp", slice(0, 128, 4), slice(GCOL[d], GCOL[d] + GH)), A("land", AL, 3 * t + d, AL), bt))
 
     def ghosts(w):
-        return [C(w, PAD + V + d * GH, PAD + V + (d + 1) * GH) for d in range(3)]
-
-    def times_out(t):
-        ts(A("ti"), A("ph"), 31, None, band)
-        cp(C("phb", 48, 96), A("ti"))
-        tt(C("phb", 0, 48), A("ph"), A("ti"), sub)
-        for sh in (1, 0):
-            for il in range(2):
-                for pt in range(2):
-                    o = 96 * sh + 48 * il
-                    mm(C("pX", o, o + 48), A("Ys", AL, 4 * sh + 2 * il + pt, AL), C("phb", 48 * pt, 48 * pt + 48), pt == 0, pt == 1)
-        tt(A("Yb", AL, t, AL), C("pX", 0, 192), A("msk"), mul)
-        exchange(A("Yb", AL, t, slice(96, 192)), [A("land", AL, 3 * t + d, AL) for d in range(3)], 3.0)
-        bt = newb()
-        dma("sp", A("Wp", slice(0, 128, 8), slice(PAD, PAD + V)), A("Yb", AL, t, slice(0, 96)), bt)
-        for d in range(3):
-            o = PAD + V + d * GH
-            dma("sp", A("Wp", slice(d + 1, 128, 8), slice(o, o + V)), A("land", AL, 3 * t + d, AL), bt)
-        tt(A("pr"), A("ph"), A("rbi"), plus)
+        return [C(w, x, x + GH) for x in GCOL]
 
     first, steps = sort_steps()
-    slot = {"G": 0, "xw": 0, "sg": 0, "xb": 0}
+    slot = [0]
 
-    def roll(name):
-        slot[name] = (slot[name] + 1) % 3
-        return slot[name] * 4 * U
+    def ring():
+        slot[0] = (slot[0] + 1) % NS
+        return slot[0] * BL
 
-    def rint(out, a, c, onact):
-        if onact:
-            act(out, a, ACTF.Identity, 1.0, c)
-            act(out, out, ACTF.Identity, 1.0, -c)
-        else:
-            ts(out, a, c, c, plus, sub)
+    def names(t, c):
+        a, z = CH[c]
+        lst, p = C("ls", a, z), PS(2 + c, z - a)
+        if t < RO - 1:
+            dma("sp", C("lw", a, z), lst, kb=2)
+        aff("dH", "act", C("dH", a, z), lst, 2.0 ** -12, 1024.5625)
+        mm(p, mat("n12"), C("dH", a, z), True, False)
+        const(p, "cn")
+        mm(p, f1, lst, False, True)
+        aff("nmS", "act", C("nmS", a, z), p)
+        aff("off1", "dve", C("off1", a, z), C("nmS", a, z), 1.0, 2048.0)
+        aff("hi", "dve", C("hi", a, z), C("nmS", a, z), 64.0, 32.0, "sign")
 
-    def names(t, ch):
-        lT = "lT%d" % (t % 2)
-        cs, o = slice(ch * CW, (ch + 1) * CW), ch * U
-        P2 = C(("pT", "pX")[ch], 0, U)
-        rint(P2, A(lT, AL, AL, cs), 1.5 * 2.0 ** 35, OPT["dl"])
-        tt(C("nmc", o, o + U), A(lT, AL, AL, cs), P2, sub)
-        if OPT["u1"]:
-            act(C("off1", o, o + U), C("nmc", o, o + U), ACTF.Identity, 1.0, 1152.0)
-        else:
-            ts(C("off1", o, o + U), C("nmc", o, o + U), 1152.0, None, plus)
-        act(C("hi2", o, o + U), C("nmc", o, o + U), ACTF.Sign, 1.0, -7.5)
-        for h in range(2):
-            ph_, a, z = A("pP", AL, slice(8 * h, 8 * h + 8), cs), h * U // 2, (h + 1) * U // 2
-            mm(ph_, A("mf", AL, 1, AL), C("nmc", o + a, o + z), True, False)
-            mm(ph_, mat(0), C("kc", a, z), False, False)
-            mm(ph_, mat(21), C("hi2", o + a, o + z), False, True)
-        f = U + ch * CW
-        for k in range(16):
-            mm(C("pX", f, f + CW), mat(k), C("hi2", o + k * CW, o + (k + 1) * CW), k == 0, k == 15)
-        ts(C("Bs", ch * CW, (ch + 1) * CW), C("pX", f, f + CW), -65535.5, -2.0 ** 10, plus, mul)
+    def arrival(t, c, a, z):
+        for v in range(a, z, BL):
+            s = ring()
+            tag[0] = "a%d%d" % (t, v // BL)
+            for w in range(0, BL, OPT["tu"]):
+                aff("tg", "act", Wd("rg", s + w, OPT["tu"]), IND(A("Wp"), C("off1", v + w, v + w + OPT["tu"])))
+            o = 512 * c + v - a
+            mm(C("pa", o, o + BL), C("dH", v, v + BL), eye, True, False)
+            mm(C("pa", o, o + BL), C("Wp", PAD + v, PAD + v + BL), mat("nblk"), False, False)
+            for k in range(16):
+                mm(C("pa", o + k, o + BL, 16), Wd("rg", s, BL, k), A("gs"), False, k == 15)
+        nh, p = B3("nH", a // 16, z // 16), PS(4 + c, z - a)
+        aff("nH", "act", nh, PS(c, z - a), 1.0, -1537.0)
+        mm(p, mat("n15"), nh, True, False)
+        const(p, "c1")
+        grid(p, "g25")
+        mm(p, mat("p15"), nh, False, False)
+        mm(p, eye, C("kc", 0, z - a), False, False)
+        for v in range(a, z, BL):
+            mm(PS(4 + c, BL, v - a), C("hi", v, v + BL), mat("n11"), False, False)
+            mm(PS(4 + c, BL, v - a), C("nmS", v, v + BL), eye, False, v + BL == z)
 
-    def arrival(t, ch):
-        lT = "lT%d" % (t % 2)
-        cs, o, pc = slice(ch * CW, (ch + 1) * CW), ch * U, ch * 512
-        mm(C("pC", pc, pc + U), mat(20), A("ones"), True, False)
-        for k in range(16):
-            for pt in range(2):
-                mm(C("pC", pc + k * CW, pc + (k + 1) * CW), mat(16), C("phb", 48 * pt + ch * CW, 48 * pt + (ch + 1) * CW), False, False)
-        mm(C("pC", pc, pc + U), A("mf", AL, 0, AL), A(lT, AL, AL, cs), False, False)
-        for j in range(4):
-            s = roll("G")
-            src = IND(C("Wp", 0, WW), C("off1", o + 4 * j * CW, o + 4 * (j + 1) * CW))
-            if 4 * ch + j in OPT["g0" if t == 0 else "g1"]:
-                ts(C("G", s, s + 4 * U), src, 2.0 ** -10, None, mul)
-            else:
-                act(C("G", s, s + 4 * U), src, ACTF.Copy, 2.0 ** -10)
-            for i in range(16):
-                mm(C("pC", pc + 4 * j * CW, pc + 4 * (j + 1) * CW), A("Sel", AL, i, AL), C("G", s + i, s + 4 * U, 16), False, j == 3 and i == 15)
-
-    def keys(t, ch):
-        pc, cs = ch * 512, slice(ch * CW, (ch + 1) * CW)
-        rr = C("Rr", ch * U, (ch + 1) * U)
-        rint(rr, C("pC", pc, pc + U), 1.5 * 2.0 ** 48, OPT["R"])
-        tt(A("a15", AL, AL, cs), C("pC", pc, pc + U), rr, sub)
-
-    def sort(cs):
+    def sort(a, z, r0):
+        def at(sp, w):
+            return B3("ps", r0, r0 + z - a, w) if sp == "P" else B3(sp, a, z, w)
         for sp, r in first:
-            w, z = prog([x[0] for x in r]), prog([x[1] for x in r])
-            tt(A("pP" if sp == "P" else "S", AL, z, cs), A("pP", AL, w, cs), A("a15", AL, w, cs), plus)
+            if sp == "S":
+                aff("s0", "act", at("S", prog([x[1] for x in r])), at("P", prog([x[0] for x in r])))
         for ismin, sp, r in steps:
             pw, sw, ow = [prog([x[j] for x in r]) for j in range(3)]
-            tt(A("pP" if sp == "P" else sp, AL, ow, cs), A("pP", AL, pw, cs), A("S", AL, sw, cs), mn if ismin else mx)
+            tt(at(sp, ow), at("P", pw), at("S", sw), mn if ismin else mx)
 
-    def places(t, ch):
-        o = ch * U
-        Kc = A("K", AL, AL, slice(ch * CW, (ch + 1) * CW))
-        ts(A("kk"), Kc, 11, 15, shr, band)
-        if not OPT["ki"]:
-            cp(A("kf"), A("kk"))
-        act(C("pw", o, o + U), A("kk" if OPT["ki"] else "kf"), ACTF.Sigmoid, -math.log(2.0), -12 * math.log(2.0))
-        ts(A("lo"), Kc, 2047, None, band)
-        tt(A("yy"), IND(C("Bs", ch * CW, (ch + 1) * CW), A("rep")), C("pw", o, o + U), mul)
-        rint(C("pT", 0, U), A("yy"), 1.5 * 2.0 ** 23, OPT["r"])
-        tt(A("bit"), C("pT", 0, U), A("yy"), lt)
-        if OPT["n8"]:
-            act(A("kf"), A("lo"), ACTF.Copy)
-            mm(C("pX", 0, U), A("mf", AL, 2, AL), A("kf"), True, False)
-            mm(C("pX", 0, U), mat(17), A("bit"), False, True)
-            if OPT["u0"]:
-                act(C("off", o, o + U), C("pX", 0, U), ACTF.Copy)
-            else:
-                cp(C("off", o, o + U), C("pX", 0, U))
-            act(C("nm8", o, o + U), C("pX", 0, U), ACTF.Copy)
-        else:
-            mm(C("pX", 0, U), mat(17), A("bit"), True, True)
-            tt(C("nm8", o, o + U), A("lo"), C("pX", 0, U), plus)
-            if OPT["u0"]:
-                act(C("off", o, o + U), C("nm8", o, o + U), ACTF.Copy)
-            else:
-                cp(C("off", o, o + U), C("nm8", o, o + U))
-        if t < RO - 1:
-            act(C("pwb", o, o + U), C("pw", o, o + U), ACTF.Copy, 2.0 ** 36)
-            ts(C("fo", ch * CW, (ch + 1) * CW), C("nm8", o, o + CW), float(PAD + V - 1), -float(PAD), mn, plus)
-            ts(C("Fc", ch * CW, (ch + 1) * CW), C("nm8", o, o + CW), float(PAD + V), 65535.0, ge, mul)
+    def places(a, z, banks):
+        bR, bB, bV = banks if OPT["bv"] or a == 0 else (6, 7, 3)
+        aff("aH", "act", B3("aH", a // 16, z // 16), B3("K", a // 16, z // 16), 2.0 ** -15, 1536.5)
 
-    def masking(t, ch):
-        o, dd, pc = ch * U, ch * 16 * U, ch * 512
-        win = C(Wn[t], 0, WW)
-        mm(C("pC", pc, pc + U), mat(18), A("ones"), True, False)
-        short = t == 0 and OPT["d0"]
-        for j in range(4 if short else 0):
-            xs, ss = roll("xb"), roll("sg")
-            act(C("xb", xs, xs + 4 * U), IND(win, C("off", o + 4 * j * CW, o + 4 * (j + 1) * CW)), ACTF.Copy)
-            for s in range(4 * j, 4 * j + 4):
-                x = C("xb", xs + (s % 4) * U, xs + (s % 4 + 1) * U)
-                if s == 0:
-                    act(C("dw", dd, dd + U), x, ACTF.Sigmoid)
-                    M = x
-                    continue
-                M2 = C("Mb", (s % 4) * U, (s % 4 + 1) * U) if s < 15 else C("Xp", o, o + U)
-                tt(M2, x, M, mx)
-                pd = C("pM", 512 * (s % 2), 512 * (s % 2) + U)
-                mm(pd, mat(0), x, True, False)
-                mm(pd, mat(22), M, False, True)
-                sgn = C("sg", ss + (s % 4) * U, ss + (s % 4 + 1) * U)
-                if s in OPT["gt"]:
-                    tt(A("tb"), x, M, ALU.is_gt)
-                    ts(sgn, A("tb"), 2.0, -1.0, mul, plus)
+        def low(bk, stop):
+            for v in range(a, z, BL):
+                p, r = PS(bk, BL, v - a), v // 16
+                mm(p, B3("aH", r, r + 8), mat("n15"), True, False)
+                const(p, "ca")
+                mm(p, B3("K", r, r + 8), f1, False, stop)
+                if not stop:
+                    const(p, "cb")
+                    mm(p, mat("n11"), C("kH", v, v + BL), False, True)
+        low(bR, True)
+        aff("kH", "act", C("kH", a, z), PS(bR, z - a), 2.0 ** -11, 128.5)
+        act(C("pw", a, z), C("kH", a, z), ACTF.Sigmoid, -LN2, 117 * LN2)
+        mm(PS(bB, z - a), mat("wb"), C("hi", a, z), True, True)
+        low(bV, False)
+        tt(C("Z", a, z), C("pw", a, z), PS(bB, z - a), mul)
+        ts(C("Z", a, z), C("Z", a, z), 4, HI, shr, band)
+        tt(C("nmH", a, z), C("Z", a, z), PS(bV, z - a), plus)
+        aff("off", "dve", C("off", a, z), C("nmH", a, z), 1.0, 2048.0)
+
+    def fetch(t, c):
+        a, z = CH[c]
+        n = (z - a) // 16
+        ts(C("c0", a, z), C("nmH", a, z), -1264.0, C("pf", 4, 5), mn, mul)
+        aff("own", "act", C("nmS", a, z), C("nmH", a, z), -64.0, -64 * 1264.5, "sign")
+        p = PS(7 - c, n)
+        for i in range(16):
+            mm(p, A("Sel", AL, i, AL), C("c0", a + i, z, 16), i == 0, i == 15)
+        aff("fo", "act", C("fo", a // 16, z // 16), p, 32.0, 2032.0)
+        tt(C("Dp", a, z), IND(A("lw"), C("fo", a // 16, z // 16)), C("ls", a, z), sub)
+
+    unit, signs = [0], {}
+
+    def masking(t, c, a, z):
+        X, win, cnt = "X%d" % min(t, 1), A(Wn[t]), 4 + c
+        tag[0] = "m%d%d" % (t, a // BL)
+        turn = OPT["tc"][t]
+        if not turn:
+            const(PS(cnt, z - a), "co", start=True)
+
+        def sign(s, v, n, src):
+            signs[t] = aff("sg", "act", Wd("rg", s, n), src, 2.0 ** 40, -2.0 ** 13, "sign")
+            for k in range(1, 16 * (not turn)):
+                mm(PS(cnt, n, v - a), A("Sel", AL, k, AL), Wd("rg", s, n, k), False, False)
+        for v in range(a, z, BL):
+            tag[0] = "m%d%d" % (t, v // BL)
+            src = IND(win, C("off", v, v + BL))
+            cast = v // BL in OPT["cs"][t]
+            if t == 0:
+                j = v // BL
+                x, top, s = BL * (3 + 2 * j % 3), BL * (3 + (2 * j + 1) % 3), BL * (j % 3)
+                aff("lg", "act", Wd("rg", x, BL), src)
+                if j in OPT["rv"]:
+                    for w in range(0, BL, UN):
+                        unit[0] ^= 1
+                        r = UN * unit[0]
+                        scan(Wd("pa", r, UN, head=1), Wd("msk", 0, UN, head=1), Wd("rg", x + w, UN, tail=1))
+                        ms(C("pa", 16 * r, 16 * r + 1), 0.0)
+                        tt(C("Xb", v + w, v + w + UN), Wd("rg", x + w, UN, 15), Wd("pa", r, UN, 15), mx)
+                        tt(Wd(X, v + w, UN), Wd("rg", x + w, UN), Wd("pa", r, UN), sub)
+                        sign(s + w, v + w, UN, Wd(X, v + w, UN))
                 else:
-                    act(sgn, pd, ACTF.Sign, 1.0, -2.0 ** -26)
-                act(C("dw", dd + s * U, dd + (s + 1) * U), pd, ACTF.Sigmoid)
-                M = M2
-            s0 = max(1, 4 * j)
-            for i in range(16):
-                mm(C("pC", pc + s0 * CW, pc + (4 * j + 4) * CW), A("Sel", AL, i, AL), C("sg", ss + (s0 % 4) * U + i, ss + 4 * U, 16), False, j == 3 and i == 15)
-        if not short:
-            act(C("dw", dd, dd + U), IND(win, C("off", o, o + CW)), ACTF.Copy)
-        M = C("dw", dd, dd + U)
-        for s0, s1 in () if short else ((1, 4), (4, 8), (8, 12), (12, 16)):
-            n = s1 - s0
-            xs = roll("xw")
-            act(C("xw", xs, xs + n * U), IND(win, C("off", o + s0 * CW, o + s1 * CW)), ACTF.Copy)
-            for s in range(s0, s1):
-                x = C("xw", xs + (s - s0) * U, xs + (s - s0 + 1) * U)
-                M2 = None
-                if s < 15:
-                    M2 = C("pM", 512 * (s % 2), 512 * (s % 2) + U)
-                elif t < RO - 1:
-                    M2 = C("Xp", o, o + U)
-                if M2 is not None:
-                    tt(M2, x, M, mx)
-                tt(C("dw", dd + s * U, dd + (s + 1) * U), x, M, sub)
-                M = M2
-            ss = roll("sg")
-            act(C("sg", ss, ss + n * U), C("dw", dd + s0 * U, dd + s1 * U), ACTF.Sign, 1.0, -2.0 ** -26)
-            for i in range(16):
-                mm(C("pC", pc + s0 * CW, pc + s1 * CW), A("Sel", AL, i, AL), C("sg", ss + i, ss + n * U, 16), False, s1 == 16 and i == 15)
-        cnt = C("pC", pc, pc + U)
-        tt(A("km"), A("K", AL, AL, slice(ch * CW, (ch + 1) * CW)), cnt, mn)
-        tt(C("km2", 0, 192), C("km", 0, 192), C("km", 192, 384), mx)
-        tt(C("km2", 192, 288), C("km2", 0, 96), C("km2", 96, 192), mx)
-        tt(C("km2", 288, 336), C("km2", 192, 240), C("km2", 240, 288), mx)
-        tt(C("kmx", ch * CW, (ch + 1) * CW), C("km2", 288, 312), C("km2", 312, 336), mx)
-        if t < RO - 1:
-            tt(A("qq"), C("pwb", o, o + U), cnt, mn)
-            f = 432 + ch * CW
-            for s in range(16):
-                mm(C("pX", f, f + CW), mat(19), C("qq", s * CW, (s + 1) * CW), s == 0, s == 15)
-            cp(C("Fi", ch * CW, (ch + 1) * CW), C("pX", f, f + CW))
-        if OPT["o2"]:
-            act(A("ng"), cnt, ACTF.Relu, -2.0 ** -10)
-            mm(C("pT", 0, U), A("mf", AL, 2, AL), C("nm8", o, o + U), True, False)
-            mm(C("pT", 0, U), mat(16), A("ng"), False, True)
-            src = C("pT", 0, U)
+                    scan(Wd("rg", top, BL, head=1), Wd("msk", 0, BL, head=1), Wd("rg", x, BL, tail=1))
+                    tt(C("Xb", v, v + BL), Wd("rg", top, BL, 15), Wd("rg", x, BL, 15), mx)
+            else:
+                s = ring()
+                for w in range(v, v + BL, OPT["lu"]):
+                    aff("lg", "act", Wd(X, w, OPT["lu"]), IND(win, C("off", w, w + OPT["lu"])))
+            whole = t > 0 and v // BL in OPT["un"]
+            if whole:
+                scan(Wd("pa", 0, BL, head=1), Wd("msk", 0, BL, head=1), Wd(X, v, BL, tail=1))
+                if t < RO - 1:
+                    tt(C("t1", v, v + BL), Wd(X, v, BL, 15), Wd("pa", 0, BL, 15), mx)
+                tt(Wd(X, v, BL, head=1), Wd(X, v, BL, head=1), Wd("pa", 0, BL, head=1), sub)
+            for w in range(0, BL * (not whole and (t > 0 or j not in OPT["rv"])), UN):
+                unit[0] ^= 1
+                r = UN * unit[0]
+                if t == 0:
+                    for h in range(0, UN, 32):
+                        mm(Wd("pa", r + h, 32), eye, Wd("rg", x + w + h, 32), True, False)
+                        mm(Wd("pa", r + h, 32, head=1), mat("neg"), Wd("rg", top + w + h, 32, head=1), False, True)
+                    if not cast:
+                        sign(s + w, v + w, UN, Wd("pa", r, UN))
+                    act(Wd(X, v + w, UN), Wd("pa", r, UN), ACTF.Sigmoid)
+                else:
+                    scan(Wd("pa", r, UN, head=1), Wd("msk", 0, UN, head=1), Wd(X, v + w, UN, tail=1))
+                    if t < RO - 1:
+                        tt(C("t1", v + w, v + w + UN), Wd(X, v + w, UN, 15), Wd("pa", r, UN, 15), mx)
+                    d = Wd(X, v + w, UN, head=1)
+                    tt(d, d, Wd("pa", r, UN, head=1), sub)
+                    if v // BL in OPT["su"]:
+                        sign(s + w, v + w, UN, Wd(X, v + w, UN))
+            if cast and t == 0:
+                for w in range(0, BL, UN):
+                    dma("sp", Wd("rg", s + w, UN), A("c7"), kb=2)
+                dma("pool", Wd("rg", s, BL), Wd(X, v, BL), acc=True, kb=6)
+            elif cast:
+                dma("pool", Wd("rg", s, BL), Wd(X, v, BL), kb=8)
+                sign(s, v, BL, Wd("rg", s, BL))
+            elif t > 0 and v // BL not in OPT["su"]:
+                sign(s, v, BL, Wd(X, v, BL))
+            if turn:
+                r = 32 * c + (v - a) // 16
+                mm(B3("ps", r, r + 8), A("ones", slice(0, 1), slice(0, BL)), row("cr" if cast and t == 0 else "ct"), True, False)
+                for k in range(1, 16):
+                    mm(B3("ps", r, r + 8, k), Wd("rg", s, BL, k), A("gs"), False, k == 15)
+        tag[0] = "t%d%d" % (t, a // BL)
+        p = PS(cnt, z - a)
+        if turn:
+            aff("mk", "act", B3("nH", a // 16, z // 16), p, -64.0, 224.0, "sign")
+            mm(p, eye, C("nmH", a, z), True, False)
+            for v in range(a, z, BL):
+                mm(PS(cnt, BL, v - a), B3("nH", v // 16, v // 16 + 8), mat("n12"), False, v + BL == z)
         else:
-            tt(A("tt"), C("nm8", o, o + U), cnt, mn)
-            src = A("tt")
-        if OPT["u2"]:
-            act(C("off2", o, o + U), src, ACTF.Relu)
+            grid(p, "g12")
+            mm(p, eye, C("nmH", a, z), False, True)
+        soon, un = t < RO - 1 and OPT["soon"], "RD" if OPT["qa"] else "kH"
+        if soon:
+            aff("u", "act", C(un, a, z), p, 8.0, 16320.0, "sign")
+        aff("off2", "act", C("off2", a, z), p, 1.0, 2048.0, "relu")
+        if not soon:
+            aff("u", "dve", C(un, a, z), C("off2", a, z), 2.0, -16.0, "sign")
+        bD = 6 if soon else cnt
+        p = PS(bD, z - a)
+        for v in range(a, z, BL):
+            mm(PS(bD, BL, v - a), B3("aH", v // 16, v // 16 + 8), eye, True, False)
+            mm(PS(bD, BL, v - a), mat("tri"), C(un, v, v + BL), False, True)
+        aff("RD", "act", C("RD", a, z), p, 1.0, -5121.0, "relu")
+        times(t + 1, 3 if soon else c, a, z, [(A("rbh", P8, slice(a, z)), True), (C("Wp", PAD + a, PAD + z), False), (C("RD", a, z), False)])
+
+    def lists(t, c):
+        a, z = CH[c]
+        p = PS(7 - c, z - a)
+        if OPT["qa"]:
+            mm(p, eye, C("kH", a, z), True, False)
+            for v in range(a, z, BL):
+                mm(PS(7 - c, BL, v - a), B3("nH", v // 16, v // 16 + 8), mat("p15"), False, v + BL == z)
+            act(C("hi", a, z), p, ACTF.Sigmoid, -LN2, 117 * LN2)
         else:
-            cp(C("off2", o, o + U), src)
-
-    def hearing(t, ch):
-        o, dd = ch * U, ch * 16 * U
-        n = OPT["z"]
-        for j in range(4):
-            z = C("dw", dd + 4 * j * U, dd + 4 * (j + 1) * U)
-            win = C(Wn[t], 0, WW)
-            if 4 * ch + j in OPT["f"][t]:
-                xs = roll("xw")
-                act(C("xw", xs, xs + 4 * U), IND(win, C("off2", o + 4 * j * CW, o + 4 * (j + 1) * CW)), ACTF.Copy)
-                for s in range(4 * j, 4 * j + 4):
-                    zs, pd = C("dw", dd + s * U, dd + (s + 1) * U), C("pM", 512 * (s % 2), 512 * (s % 2) + U)
-                    act(pd, zs, ACTF.Sigmoid)
-                    tt(zs, pd, C("xw", xs + (s % 4) * U, xs + (s % 4 + 1) * U), mul)
-            else:
-                if t > 0 or not OPT["d0"]:
-                    act(z, z, ACTF.Sigmoid)
-                for s in range(4 * j, 4 * j + 4, n):
-                    zs = C("dw", dd + s * U, dd + (s + n) * U)
-                    tt(zs, IND(win, C("off2", o + s * CW, o + (s + n) * CW)), zs, mul)
-            e = ch * 4 * U
-            if t == 0 and j == 0:
-                dma("sp", C("Ea", e, e + 4 * U), z, kb=6)
-            elif t == RO - 1 and j >= 4 - OPT["np"][ch]:
-                for s in range(4 * j, 4 * j + 4):
-                    mm(C(("pT", "pX")[ch], 0, U), A("mf", AL, 2, AL), C("dw", dd + s * U, dd + (s + 1) * U), s == 16 - 4 * OPT["np"][ch], s == 15)
-            else:
-                dma("pool", C("Ea", e, e + 4 * U), z, acc=True, kb=6)
-
-    def fetch(t):
-        act(A("gp"), IND(A("lN%d" % t), A("fo")), ACTF.Copy)
-        act(A("gn"), IND(A("gp"), A("nat")), ACTF.Copy)
-        bt = newb()
-        for k in range(16):
-            dma("sp", A("gT", AL, k, AL), A("gn", slice(k, 128, 16), AL), bt)
-
-    def loudness(t):
-        own, new = Wn[t], Wn[t + 1]
-        if OPT["la"]:
-            act(A("t1"), IND(A("Xp"), A("nat")), ACTF.Copy, 0.125)
+            tt(C("hi", a, z), C("kH", a, z), C("pw", a, z), mul)
+        const(p, "m1", start=True)
+        mm(p, mat("y"), C("hi", a, z), False, False)
+        grid(p, "g0")
+        mm(p, mat("ny"), C("hi", a, z), False, False)
+        const(p, "m2")
+        mm(p, mat("r0"), C("nmS", a, z), False, False)
+        grid(p, "g0", True)
+        if c in OPT["ja"]:
+            tt(C("Dp", a, z), C("Dp", a, z), p, mul)
+            dma("pool", C("ls", a, z), C("Dp", a, z), acc=True, kb=(z - a) / 256)
         else:
-            tt(A("t1"), IND(A("Xp"), A("nat")), C(own, PAD, PAD + V), sub)
-        for h in range(2):
-            a, z = h * U, (h + 1) * U
-            tmp = C("pM", 512 * h, 512 * h + U)
-            if OPT["la"]:
-                act(tmp, C(own, PAD + a, PAD + z), ACTF.Copy, 0.125)
-                tt(tmp, C("t1", a, z), tmp, sub)
-            else:
-                ts(tmp, C("t1", a, z), 0.125, None, mul)
-            tt(tmp, tmp, C(own, PAD + a, PAD + z), plus)
-            tt(C(new, PAD + a, PAD + z), tmp, C("fad", a, z), mul)
-        ls = "Ls%d" % (t + 1)
-        bt = newb()
-        dma("sp", A(ls, slice(0, 112), AL), A(new, slice(16, 128), slice(PAD, PAD + GH)), bt, kb=2)
-        dma("sp", A(ls, slice(112, 128), AL), A(new, slice(0, 16), slice(PAD, PAD + GH)), bt, kb=2)
+            tt(p, C("Dp", a, z), p, mul)
+            tt(C("ls", a, z), C("ls", a, z), p, plus)
 
-    def lists(t):
-        old, new = "lT%d" % (t % 2), "lT%d" % ((t + 1) % 2)
-        ts(A("Fi"), A("Fi"), 65535, None, band)
-        tt(A("Fi"), A("Fi"), A("Fc"), mx)
-        for k in range(16):
-            ts(A("keep", AL, k, AL), A("Fi"), 15 - k, 1, shr, band)
-        for ch in range(NCH):
-            cs = slice(ch * CW, (ch + 1) * CW)
-            tmp = A("pP", AL, AL, cs)
-            if OPT["df"]:
-                for h in range(2):
-                    w = slice(8 * h, 8 * h + 8)
-                    mm(A("pP", AL, w, cs), A("mf", AL, 2, AL), A(old, AL, w, cs), True, False)
-                    mm(A("pP", AL, w, cs), A("mf", AL, 3, AL), A("gT", AL, w, cs), False, True)
-            else:
-                tt(tmp, A(old, AL, AL, cs), A("gT", AL, AL, cs), sub)
-            tt(tmp, tmp, A("keep", AL, AL, cs), mul)
-            tt(A(new, AL, AL, cs), tmp, A("gT", AL, AL, cs), plus)
-        if t + 2 < RO:
+    def loudness(t, c):
+        a, z = CH[c]
+        p, own, new = PS(6 + c, z - a), C(Wn[t], PAD + a, PAD + z), Wn[t + 1]
+        if t == 0:
+            mm(p, eye, C("Xb", a, z), True, False)
+            mm(p, mat("m7"), own, False, True)
+        else:
+            aff("l8", "act", p, own)
+            tt(C("t1", a, z), C("t1", a, z), p, sub)
+            aff("l8", "act", p, own, 8.0)
+            tt(p, C("t1", a, z), p, plus)
+        tt(C(new, PAD + a, PAD + z), p, C("fad", a, z), mul)
+        if c == 0:
             bt = newb()
-            for k in range(16):
-                dma("sp", A("lN%d" % (t + 1), slice(k, 128, 16), AL), A(new, AL, k, AL), bt)
+            dma("sp", A("Ls1", slice(0, 112), AL), A(new, slice(16, 128), slice(PAD, PAD + GH)), bt, kb=2)
+            dma("sp", A("Ls1", slice(112, 128), AL), A(new, slice(0, 16), slice(PAD, PAD + GH)), bt, kb=2)
+            exchange(A("Ls1"), ghosts(new), 8.0)
 
-    times_out(0)
+    def hearing(t, c):
+        a, z = CH[c]
+        X = "X%d" % min(t, 1)
+        sums, scans = [], []
+        for v in range(a, z, BL):
+            tag[0] = "h%d%d" % (t, v // BL)
+            x = Wd(X, v, BL)
+            how = OPT["em"][v // BL]
+            direct = t == RO - 1 and how in "ps"
+            step = OPT["lastu"] if direct and v + BL == V else OPT["hu"]
+            for w in range(v, v + BL, step):
+                y = Wd(X, w, step)
+                if t == RO - 1 and v // BL in OPT["fa"]:
+                    unit[0] ^= 1
+                    p = Wd("pa", UN * unit[0], step)
+                    act(p, y, ACTF.Sigmoid)
+                    aff("xg", "act", y, IND(A(Wn[t]), C("off2", w, w + step)))
+                    tt(y, y, p, mul)
+                    continue
+                if t > 0 or v // BL in OPT["rv"]:
+                    act(y, y, ACTF.Sigmoid)
+                n = tt(y, IND(A(Wn[t]), C("off2", w, w + step)), y, mul)
+                if v // BL >= OPT["hw"][t]:
+                    ops[n]["deps"].add(signs[t])
+            if t > 0 and not direct:
+                dma("pool", Wd("X0", v, BL), x, acc=True, kb=8, after=landed[-1:] if t < RO - 1 else ())
+            if t == RO - 1:
+                if how == "v":
+                    scan(x, A("msk"), Wd("X0", v, BL), True)
+                    aff("ye", "act", C("t1", v, v + BL), Wd(X, v, BL, 15))
+                    continue
+                sums.insert(len(sums) if not direct else 0, ("X0", v, BL))
+                if direct:
+                    (sums if how == "p" else scans).extend((X, w, step) for w in range(v, v + BL, step))
+        if t == RO - 1:
+            tag[0] = "e%d%d" % (t, c)
+            if sums:
+                const(PS(6 + c, z - a), "c0", start=True)
+            for i, (Y, w, n) in enumerate(sums):
+                for k in range(16):
+                    mm(PS(6 + c, n, w - a), f1, Wd(Y, w, n, k), False, i == len(sums) - 1 and k == 15)
+            for v in range(a, z, BL):
+                if OPT["em"][v // BL] in "dp":
+                    aff("ye", "act", C("t1", v, v + BL), PS(6 + c, BL, v - a))
+            for Y, w, n in scans:
+                tag[0] = "h%d%d" % (t, w // BL)
+                scan(Wd("X0", w, n), Wd("msk", 0, n), Wd(Y, w, n), True)
+                tt(C("t1", w, w + n), Wd("X0", w, n, 15), PS(6 + c, n, w - a), plus)
+            dma("sp", A("ye", AL, slice(a, z)), C("t1", a, z), kb=2)
+
+    def do(step, t, c):
+        tag[0] = "%s%d%d" % (step[0], t, c)
+        step[1](t, c)
+
+    def cuts(at, a, z):
+        at = [a] + [x for x in at if a < x < z] + [z]
+        return list(zip(at, at[1:]))
+
+    for c in range(2):
+        times(0, c, CH[c][0], CH[c][1], [(A("RD", P8, slice(*CH[c])), True)])
     exchange(A("Ls0"), ghosts("W0"), 4.0)
     for t in range(RO):
-        for step in (names, arrival, keys):
-            for ch in range(NCH):
-                step(t, ch)
-        if OPT["w"][t]:
-            sort(slice(0, NCH * CW))
-        for ch in range(NCH):
-            if not OPT["w"][t]:
-                sort(slice(ch * CW, (ch + 1) * CW))
-            places(t, ch)
-        if t < RO - 1:
-            fetch(t)
-        for ch in range(NCH):
-            masking(t, ch)
-        ts(A("tj"), A("kmx"), 15, None, shr)
-        tt(A("tj"), A("tj"), A("pr"), plus)
-        ts(A("ph"), A("tj"), 1023, None, band)
-        if t < RO - 1:
-            times_out(t + 1)
-            lists(t)
-            loudness(t)
-            exchange(A("Ls%d" % (t + 1)), ghosts(Wn[t + 1]), 8.0)
-        else:
-            cp(A("phf"), A("ph"))
-            dma("sp", A("yp"), A("phf"))
-        for ch in range(NCH):
-            hearing(t, ch)
-    for ch in range(NCH):
-        e = ch * 4 * U
-        pm, acc = C("pM", 512 * ch, 512 * ch + U), C(("pT", "pX")[ch], 0, U)
-        tt(pm, C("Ea", e, e + U), C("Ea", e + U, e + 2 * U), plus)
-        tt(pm, pm, C("Ea", e + 2 * U, e + 3 * U), plus)
-        tt(C("t1", ch * U, (ch + 1) * U), pm, C("Ea", e + 3 * U, e + 4 * U), plus)
-        tt(C("gp", ch * U, (ch + 1) * U), acc, C("t1", ch * U, (ch + 1) * U), plus)
-    cp(A("gn"), IND(A("gp"), A("nat")))
-    dma("sp", A("ye"), A("gn"), kb=3)
-    return ops
-
-
-def order(ops, fixed=None):
-    n = len(ops)
+        for c in range(2):
+            do(("n", names), t, c)
+        halves = cuts((OPT["ac"][t] or GH,), 0, V)
+        for c, (a, z) in enumerate(halves):
+            arrival(t, c, a, z)
+        for c, (a0, z0) in enumerate(halves):
+            tag[0] = "s%d%d" % (t, c)
+            if OPT["ac"][t]:
+                sort(a0 // 16, z0 // 16, 32 * c)
+            elif c == 0:
+                sort(0, V // 16, 0)
+            for a, z in cuts(OPT["pc"][t], a0, z0):
+                tag[0] = "p%d%d" % (t, a // BL)
+                places(a, z, (2, 3, 0) if a == 0 else (6, 7, 6 if OPT["ac"][t] else 5))
+        for c in range(2):
+            if t < RO - 1:
+                do(("f", fetch), t, c)
+        j = 0
+        for c in range(2):
+            for a, z in cuts(OPT["mc"][t], *CH[c]):
+                masking(t, j % 2, a, z)
+                j += 1
+            if t < RO - 1:
+                do(("v", loudness), t, c)
+                do(("l", lists), t, c)
+        for c in range(2):
+            do(("h", hearing), t, c)
     members = {}
     for i, o in enumerate(ops):
         if o["batch"] is not None:
             members.setdefault(o["batch"], []).append(i)
     for o in ops:
-        for key in ("raw", "war"):
-            for d in list(o[key]):
-                if ops[d]["batch"] is not None:
-                    o[key].update(members[ops[d]["batch"]])
-        o["deps"] = o["raw"] | o["war"]
+        for d in list(o["deps"]):
+            if ops[d]["batch"] is not None:
+                o["deps"].update(members[ops[d]["batch"]])
+    return ops, members
+
+
+def price(o, e, par):
+    n, w = o["cyc"]
+    if w == "c":
+        c = n * CY
+    elif w == "q":
+        c = n * CY * par["f"]
+    elif w == "p":
+        c = 0.01 + n * CY * par["pe"] * par["f"]
+    else:
+        k = {"g": par["G"], "h": 0.5 if e == "dve" else 1, "1": 1, "2": 2, "b": par["b2"]}[w]
+        c = ((1.3 if e == "act" else 1) * par["ov"] + max(64, n * k) * CY) * par["f"]
+    lat = o["lat"]
+    if lat:
+        lat = {"d": par["dma"] + par["kb"] * lat[1], "f": lat[1] * par["far"], "c": lat[1]}[lat[0]]
+    return c, lat
+
+
+def queue_of(o):
+    return ASG.get(o["key"] + o["tag"], ASG.get(o["key"], o["eng"])) if o["key"] else o["eng"]
+
+
+def rank(o, path, e):
+    tag = o["tag"]
+    bias = BIAS.get(tag, 0.0) + BIAS.get(tag[:2], 0.0) + BIAS.get((o["key"] or o["kind"]) + tag, 0.0)
+    if e not in ("act", "dve", "any") or o["cyc"][0] < 900 and tag[:1] != "s" or not tag:
+        return 1000.0 + path + bias
+    step, t, b = (o["key"] or tag[0]), int(tag[1]), int(tag[2])
+    at, pace, late = STEP.get(step + tag[1], STEP[step])
+    return -(OPT["round"] * (t + late) + at + pace * b) + bias + 1e-3 * path
+
+
+def order(ops, par, fixed=None):
+    n = len(ops)
+    eng = [queue_of(o) for o in ops]
+    if fixed is not None:
+        for e in ENGS:
+            for i in fixed[e]:
+                eng[i] = e
+    cost = [{e: price(o, e, par) for e in (("act", "dve") if eng[i] == "any" else (eng[i],))} for i, o in enumerate(ops)]
     succ = [[] for _ in ops]
     for i, o in enumerate(ops):
         for d in o["deps"]:
             succ[d].append(i)
 
-    def gap(d, i):
-        if ops[d]["eng"] == ops[i]["eng"] and ops[d]["batch"] is None:
-            return 0.0 if ops[i]["eng"] == "pe" else PAR["same"]
-        return PAR["hop"]
+    def gap(d, j):
+        if eng[d] == eng[j] != "any" and ops[d]["batch"] is None:
+            return 0.0 if eng[d] == "pe" else par["same"]
+        return par["hop"]
     left = [len(o["deps"]) for o in ops]
-    topo = [i for i in range(n) if left[i] == 0]
-    for i in topo:
-        for j in succ[i]:
-            left[j] -= 1
-            if left[j] == 0:
-                topo.append(j)
-    assert len(topo) == n
     pr = [0.0] * n
-    for i in reversed(topo):
-        pr[i] = ops[i]["cost"] + ops[i]["lat"] + max([pr[j] + gap(i, j) for j in succ[i]] + [0.0])
-    kinds = sorted(set((o["eng"], o["kind"], str(o["args"][0][0])) for o in ops if o["args"]))
-    shift = dict(zip(kinds, OPT["amp"] * np.random.default_rng(OPT["seed"]).standard_normal(len(kinds))))
-    for i, o in enumerate(ops):
-        if o["args"]:
-            pr[i] += float(shift[(o["eng"], o["kind"], str(o["args"][0][0]))])
-    left = [len(o["deps"]) for o in ops]
+    if fixed is None:
+        topo = [i for i in range(n) if left[i] == 0]
+        for i in topo:
+            for j in succ[i]:
+                left[j] -= 1
+                if left[j] == 0:
+                    topo.append(j)
+        for i in reversed(topo):
+            pr[i] = sum(min(cost[i].values())) + max([pr[j] + gap(i, j) for j in succ[i]] + [0.0])
+        for i, o in enumerate(ops):
+            pr[i] = rank(o, pr[i], eng[i])
+        left = [len(o["deps"]) for o in ops]
     ready = {e: [] for e in ENGS + (None,)}
-    rt, fin, free = [0.0] * n, [0.0] * n, {e: 0.0 for e in ENGS}
+    rt, free, end = [0.0] * n, {e: 0.0 for e in ENGS}, 0.0
     queue = {e: [] for e in ENGS}
+
+    def offer(j):
+        for e in cost[j]:
+            ready[e].append(j)
     for i in range(n):
         if left[i] == 0:
-            ready[ops[i]["eng"]].append(i)
-    done = 0
-    while done < n:
+            offer(i)
+    look, fill, lines = OPT["look"], OPT["fill"], 0.0
+    for step in range(n):
         if ready[None]:
-            i = ready[None].pop()
+            i, e = ready[None].pop(), None
             start = rt[i]
         else:
             best = None
             for e in ENGS:
-                can = ready[e] if fixed is None else [j for j in fixed[e][len(queue[e]):len(queue[e]) + 1] if left[j] == 0]
+                can = ready[e]
+                if fixed is not None:
+                    k = len(queue[e])
+                    can = [fixed[e][k]] if k < len(fixed[e]) and left[fixed[e][k]] == 0 else []
                 if can:
                     t0 = max(free[e], min(rt[j] for j in can))
                     if best is None or t0 < best[0]:
                         best = (t0, e, can)
             t0, e, can = best
-            i = max((j for j in can if rt[j] <= t0 + OPT["look"]), key=lambda j: (pr[j], -j))
-            if rt[i] > t0 + 1e-6:
-                now = [j for j in can if rt[j] <= t0 + 1e-6 and ops[j]["cost"] <= OPT["fill"] and pr[j] >= pr[i] - OPT["near"]]
-                if now:
-                    i = max(now, key=lambda j: (pr[j], -j))
-            ready[e].remove(i)
+            i = can[0]
+            if fixed is None:
+                i = max((j for j in can if rt[j] <= t0 + look), key=lambda j: (pr[j], -j))
+                if rt[i] > t0 + 1e-6:
+                    now = [j for j in can if rt[j] <= t0 + 1e-6 and cost[j][e][0] <= fill]
+                    if now:
+                        i = max(now, key=lambda j: (pr[j], -j))
+                for x in cost[i]:
+                    ready[x].remove(i)
             start = max(t0, rt[i])
-            free[e] = start + ops[i]["cost"]
+            free[e] = start + cost[i][e][0]
             queue[e].append(i)
-        ops[i]["start"] = start
-        fin[i] = start + ops[i]["cost"] + ops[i]["lat"]
-        done += 1
+            eng[i] = e
+        ops[i]["start"], ops[i]["use"] = start, e
+        fin = start + sum(cost[i][e])
+        if ops[i]["kind"] in ("dma", "send"):
+            wait = max(0.0, lines - start - cost[i][e][0] - 1.0)
+            fin += wait
+            lines = start + cost[i][e][0] + 1.0 + wait + par["kb"] * (ops[i]["lat"][1] if ops[i]["kind"] == "dma" else 1.0)
+        end = max(end, fin)
         for j in succ[i]:
-            rt[j] = max(rt[j], fin[i] + gap(i, j))
+            rt[j] = max(rt[j], fin + gap(i, j))
             left[j] -= 1
-            if left[j] == 0:
-                ready[ops[j]["eng"]].append(j)
+            if left[j] == 0 and (fixed is None or eng[j] is None):
+                offer(j)
+    return queue, end
+
+
+def waits(ops, members, queue):
     pos = {}
     for e in ENGS:
         for p, i in enumerate(queue[e]):
@@ -754,15 +892,15 @@ def order(ops, fixed=None):
             o = ops[i]
             need, o["wb"] = {}, []
             for d in sorted(o["deps"]):
-                od = ops[d]
-                if od["batch"] is not None:
-                    if od["batch"] not in seen:
-                        seen.add(od["batch"])
-                        waited.add(od["batch"])
-                        o["wb"].append(od["batch"])
-                elif od["eng"] != e or e != "pe":
-                    if pos[d] > known.get(od["eng"], -1) and pos[d] > pos.get(need.get(od["eng"]), -1):
-                        need[od["eng"]] = d
+                bt, x = ops[d]["batch"], ops[d]["use"]
+                if bt is not None:
+                    if bt not in seen:
+                        seen.add(bt)
+                        waited.add(bt)
+                        o["wb"].append(bt)
+                elif x != e or e != "pe":
+                    if pos[d] > known.get(x, -1) and pos[d] > pos.get(need.get(x), -1):
+                        need[x] = d
             for x, d in need.items():
                 known[x] = pos[d]
                 marked.add(d)
@@ -774,10 +912,318 @@ def order(ops, fixed=None):
             if i in marked:
                 c += 1
                 count[i] = c
-    return dict(ops=ops, queue=queue, count=count, members=members, tail=[x for x in members if x not in waited], end=max(fin))
+    return count, [x for x in members if x not in waited]
 
 
 PLAN = {}
+
+
+def place(ops, par, key, back):
+    n = len(ops)
+    pre, suc = [list(o["deps"]) for o in ops], [[] for _ in ops]
+    for i, o in enumerate(ops):
+        for d in o["deps"]:
+            suc[d].append(i)
+    if back:
+        pre, suc = suc, pre
+    left = [len(x) for x in pre]
+    can = sorted(((key[i], i) for i in range(n) if left[i] == 0), reverse=True)
+    busy = {e: [] for e in ENGS}
+    start, fin, use = [0.0] * n, [0.0] * n, [None] * n
+    while can:
+        i = can.pop()[1]
+        eng, best = queue_of(ops[i]), None
+        for e in (("act", "dve") if eng == "any" else (eng,)):
+            c, lat = price(ops[i], e, par)
+            r = 0.0
+            for d in pre[i]:
+                same = use[d] == e and ops[i if back else d]["batch"] is None
+                r = max(r, fin[d] + ((0.0 if e == "pe" else par["same"]) if same else par["hop"]))
+            r += lat if back else 0.0
+            k = 0
+            if e is not None:
+                line = busy[e]
+                k = len(line)
+                while k > 0 and line[k - 1][1] > r:
+                    k -= 1
+                while k < len(line) and line[k][0] < r + c - 1e-9:
+                    r = max(r, line[k][1])
+                    k += 1
+            if best is None or r + c < best[0]:
+                best = (r + c, r, e, k, lat)
+        z, r, e, k, lat = best
+        if e is not None:
+            busy[e].insert(k, (r, z))
+        start[i], use[i], fin[i] = r, e, z + (0.0 if back else lat)
+        new = []
+        for j in suc[i]:
+            left[j] -= 1
+            if left[j] == 0:
+                new.append((key[j], j))
+        if new:
+            can = sorted(can + new, reverse=True)
+    return start, fin, use
+
+
+def refine(ops, turns, seed):
+    rng = np.random.default_rng(seed)
+    group = [(o["key"] or o["kind"]) + o["tag"] + str(o["eng"]) for o in ops]
+    names = sorted(set(group))
+
+    def judge(start, fin, use):
+        queue = {e: [] for e in ENGS}
+        for i in sorted(range(len(ops)), key=lambda i: (start[i], i)):
+            if use[i] is not None:
+                queue[use[i]].append(i)
+        v = [order(ops, dict(PAR, **m), queue)[1] / w for m, w in CASES]
+        return sum(v) / len(v) + 0.5 * max(v), fin, queue
+    order(ops, PAR)
+    best = judge(*place(ops, PAR, [o["start"] for o in ops], False))
+    for turn in range(turns):
+        late = place(ops, PAR, [-x for x in best[1]], True)[1]
+        shift = dict(zip(names, 3.0 * rng.standard_normal(len(names)) * (rng.random(len(names)) < 0.05)))
+        now = judge(*place(ops, PAR, [float(shift[group[i]]) - x for i, x in enumerate(late)], False))
+        if now[0] < best[0]:
+            best = now
+    order(ops, PAR, best[2])
+    return best[2]
+
+
+def graph(ops):
+    n = len(ops)
+    left, suc = [len(o["deps"]) for o in ops], [[] for _ in ops]
+    for i, o in enumerate(ops):
+        for d in o["deps"]:
+            suc[d].append(i)
+    topo = [i for i in range(n) if left[i] == 0]
+    for i in topo:
+        for j in suc[i]:
+            left[j] -= 1
+            if left[j] == 0:
+                topo.append(j)
+    before, pre, suc = [0] * n, [None] * n, [[] for _ in ops]
+    for i in topo:
+        far = 0
+        for d in ops[i]["deps"]:
+            far |= before[d]
+        pre[i] = [d for d in sorted(ops[i]["deps"]) if not far >> d & 1]
+        before[i] = far | sum(1 << d for d in pre[i])
+        for d in pre[i]:
+            suc[d].append(i)
+    return pre, suc
+
+
+def prices(ops, par):
+    return [{e: price(o, e, par) for e in (("act", "dve") if o["key"] else (o["eng"],))} for o in ops]
+
+
+def place(ops, links, cost, par, key, back):
+    n = len(ops)
+    pre, suc = links[::-1] if back else links
+    left = [len(x) for x in pre]
+    todo = sorted(range(n), key=lambda i: (key[i], i))
+    held = [False] * n
+    busy = {e: [] for e in ENGS}
+    start, fin, use = [0.0] * n, [0.0] * n, [None] * n
+    near, hop = {e: par["same"] for e in ENGS + (None,)}, par["hop"]
+    near["pe"] = 0.0
+    for first in todo:
+        if left[first]:
+            held[first] = True
+            continue
+        now = [first]
+        while now:
+            i = now.pop()
+            eng, best = queue_of(ops[i]), None
+            for e in (("act", "dve") if eng == "any" else (eng,)):
+                c, lat = cost[i][e]
+                r = 0.0
+                for d in pre[i]:
+                    x = fin[d] + (near[e] if use[d] == e and ops[i if back else d]["batch"] is None else hop)
+                    if x > r:
+                        r = x
+                if back:
+                    r += lat
+                k = 0
+                if e is not None:
+                    line = busy[e]
+                    k = len(line)
+                    while k > 0 and line[k - 1][1] > r:
+                        k -= 1
+                    while k < len(line) and line[k][0] < r + c - 1e-9:
+                        r = max(r, line[k][1])
+                        k += 1
+                if best is None or r + c < best[0]:
+                    best = (r + c, r, e, k, lat)
+            z, r, e, k, lat = best
+            if e is not None:
+                busy[e].insert(k, (r, z))
+            start[i], use[i], fin[i] = r, e, z + (0.0 if back else lat)
+            for j in suc[i]:
+                left[j] -= 1
+                if left[j] == 0 and held[j]:
+                    now.append(j)
+            now.sort(key=lambda j: -key[j])
+    return start, fin, use
+
+
+def replay(ops, pre, cost, par, seq, use):
+    fin, free, lines = [0.0] * len(ops), {e: 0.0 for e in ENGS + (None,)}, 0.0
+    near, hop = {e: par["same"] for e in free}, par["hop"]
+    near["pe"] = 0.0
+    for i in seq:
+        e = use[i]
+        r = free[e]
+        for d in pre[i]:
+            x = fin[d] + (near[e] if use[d] == e and ops[d]["batch"] is None else hop)
+            if x > r:
+                r = x
+        c, lat = cost[i][e]
+        if e is not None:
+            free[e] = r + c
+        fin[i] = r + c + lat
+        if lat and e is not None:
+            wait = max(0.0, lines - r - c - 1.0)
+            fin[i] += wait
+            lines = r + c + 1.0 + wait + par["kb"] * (ops[i]["lat"][1] if ops[i]["kind"] == "dma" else 1.0)
+    return max(fin)
+
+
+def refine(ops, turns, seed, move=None):
+    rng = np.random.default_rng(seed)
+    group = [(o["key"] or o["kind"]) + o["tag"] + str(o["eng"]) for o in ops]
+    names = sorted(set(group))
+    links, cost = graph(ops), prices(ops, PAR)
+    cases = [(dict(PAR, **m), prices(ops, dict(PAR, **m)), w) for m, w in CASES]
+
+    def judge(start, fin, use):
+        seq = sorted(range(len(ops)), key=lambda i: (start[i], i))
+        v = [replay(ops, links[0], c, par, seq, use) / w for par, c, w in cases]
+        return sum(v) / len(v) + 0.5 * max(v), fin, seq, use
+    order(ops, PAR)
+    best = cur = judge(*place(ops, links, cost, PAR, [o["start"] for o in ops], False))
+    for turn in range(turns):
+        undo = move(rng) if move else None
+        late = place(ops, links, cost, PAR, [-x for x in cur[1]], True)[1]
+        shift = dict(zip(names, OPT["amp"] * rng.standard_normal(len(names)) * (rng.random(len(names)) < OPT["part"])))
+        now = judge(*place(ops, links, cost, PAR, [float(shift[group[i]]) - x for i, x in enumerate(late)], False))
+        if now[0] < cur[0] + OPT["heat"] * (1.0 - turn / turns) * rng.random():
+            cur = now
+            best = min(best, cur, key=lambda x: x[0])
+        elif undo:
+            undo()
+    queue = {e: [i for i in best[2] if best[3][i] == e] for e in ENGS}
+    order(ops, PAR, queue)
+    return queue
+
+
+def polish(ops, queue, moves, seed):
+    rng = np.random.default_rng(seed)
+    n = len(ops)
+    pre, suc = graph(ops)
+    cases = [(dict(PAR, **m), prices(ops, dict(PAR, **m)), w) for m, w in CASES]
+    plain = [o["batch"] is None for o in ops]
+    load = [o["lat"][1] if o["kind"] == "dma" else 1.0 for o in ops]
+
+    def run(case, seq, use, at, old):
+        par, cost, w = case
+        free, last, lines = {e: 0.0 for e in ENGS + (None,)}, {}, 0.0
+        fin, why, off, lin = [list(x) for x in old[1:]] if old else ([0.0] * n, [-1] * n, [0.0] * n, [0.0] * n)
+        if at:
+            lines = lin[seq[at - 1]]
+            for i in seq[at - 1::-1]:
+                if use[i] not in last and use[i] is not None:
+                    last[use[i]], free[use[i]] = i, off[i]
+                    if len(last) == len(ENGS):
+                        break
+        hop, same, kb = par["hop"], par["same"], par["kb"]
+        for i in seq[at:]:
+            e = use[i]
+            r, y = free[e], last.get(e, -1)
+            near = 0.0 if e == "pe" else same
+            for d in pre[i]:
+                x = fin[d] + (near if use[d] == e and plain[d] else hop)
+                if x > r:
+                    r, y = x, d
+            c, lat = cost[i][e]
+            why[i] = y
+            r += c
+            if e is not None:
+                free[e], last[e], off[i] = r, i, r
+                if lat:
+                    wait = max(0.0, lines - r - 1.0)
+                    lines = r + 1.0 + wait + kb * load[i]
+                    r += wait
+            fin[i], lin[i] = r + lat, lines
+        return max(fin) / w, fin, why, off, lin
+
+    def judge(seq, use, first=0, old=None, at=0):
+        out = [None] * len(cases)
+        for k in list(range(first, len(cases))) + list(range(first)):
+            out[k] = run(cases[k], seq, use, at, old and old[k])
+            if old and out[k][0] > old[k][0] + OPT["give"]:
+                return 9.0, out
+        v = [x[0] for x in out]
+        return sum(v) / len(v) + 0.5 * max(v), out
+
+    def shift(seq, a, b, back):
+        part = seq[a:b + 1]
+        if back:
+            part = part[::-1]
+        took, link = {part[-1]}, (pre if back else suc)
+        for i in part[-2::-1]:
+            if any(j in took for j in link[i]):
+                took.add(i)
+        if part[0] in took:
+            return None
+        part = [i for i in part if i in took] + [i for i in part if i not in took]
+        return seq[:a] + (part[::-1] if back else part) + seq[b + 1:]
+    seq = sorted(range(n), key=lambda i: (ops[i]["start"], i))
+    use = [o["use"] for o in ops]
+    cur = judge(seq, use)
+    best = (cur[0], seq, use)
+    for move in range(moves):
+        case = int(rng.integers(len(cases)))
+        fin, why = cur[1][case][1:3]
+        i, pairs, sums = fin.index(max(fin)), [], [0.0]
+        while why[i] >= 0:
+            if use[why[i]] == use[i] and why[i] not in pre[i]:
+                pairs.append((why[i], i))
+                sums.append(sums[-1] + OPT["flat"] + cases[0][1][why[i]][use[i]][0])
+            i = why[i]
+        u, v = pairs[int(np.searchsorted(sums, rng.random() * sums[-1], "right")) - 1]
+        new, now, kind = seq, use, rng.random()
+        a, b = seq.index(u), seq.index(v)
+        if kind < 0.1:
+            free = [x for x in (u, v) if ops[x]["key"]]
+            if not free:
+                continue
+            x = free[rng.integers(len(free))]
+            now = list(use)
+            now[x] = "act" if use[x] == "dve" else "dve"
+        else:
+            far = (0, 0, 1, 2, 4, 8)[rng.integers(6)]
+            while far and (b < n - 1 if kind < 0.55 else a > 0):
+                a, b = (a, b + 1) if kind < 0.55 else (a - 1, b)
+                far -= use[seq[b if kind < 0.55 else a]] == use[u]
+            new = shift(seq, a, b, kind < 0.55)
+            if new is None:
+                continue
+        got = judge(new, now, case, cur[1], a)
+        if got[0] <= cur[0] + OPT["heat"] * (1.0 - move / moves) * rng.random():
+            cur, seq, use = got, new, now
+            if cur[0] < best[0]:
+                best = (cur[0], seq, use)
+    queue = {e: [i for i in best[1] if best[2][i] == e] for e in ENGS}
+    order(ops, PAR, queue)
+    return queue
+
+
+def plan():
+    ops, members = build()
+    queue = polish(ops, refine(ops, OPT["turns"], OPT["seed"]), OPT["moves"], OPT["seed"])
+    count, tail = waits(ops, members, queue)
+    return dict(ops=ops, members=members, queue=queue, count=count, tail=tail)
 
 
 def shares(src, cores, topo):
@@ -799,7 +1245,7 @@ def rank_program(g, core, T, topo):
     if T.rank_of(core) is None:
         return
     if not PLAN:
-        PLAN.update(order(build()))
+        PLAN.update(plan())
     ops, cores = PLAN["ops"], list(T.cores)
     mine = shares(core, cores, topo)
     arrive = sum(len(e) for c in cores if c != core for x, e in shares(c, cores, topo) if x == core)
@@ -810,6 +1256,8 @@ def rank_program(g, core, T, topo):
             return a
         if a[0] == "*":
             return R(a[1]).indirect(R(a[2]))
+        if a[0] == "?":
+            return R(a[3] if ops[a[1]]["use"] == "dve" else a[2])
         return T[a[0]][a[1] if len(a[1]) > 1 else a[1][0]]
 
     def total(bt):
@@ -818,12 +1266,32 @@ def rank_program(g, core, T, topo):
             return sum(len(e) for x, e in mine)
         return arrive if kind == "recv" else 16 * len(PLAN["members"][bt])
 
+    def activation(q, out, a, fn, scale, bias):
+        if bias != 0.0:
+            return q.activation(out, a, fn, bias=bias, scale=scale)
+        if scale != 1.0:
+            return q.activation(out, a, fn, scale=scale)
+        return q.activation(out, a, fn)
+
+    def either(q, e, out, a, scale, bias, fn):
+        if e == "act":
+            if fn == "sign":
+                return activation(q, out, a, ACTF.Sigmoid, scale, bias)
+            return activation(q, out, a, ACTF.Relu if fn else (ACTF.Identity if bias != 0.0 else ACTF.Copy), scale, bias)
+        if fn == "sign":
+            return q.tensor_scalar(out, a, -bias / scale, None, ALU.is_gt if scale > 0 else ALU.is_lt)
+        if fn:
+            return q.tensor_scalar(out, a, bias, 0.0, ALU.add, ALU.max)
+        if bias != 0.0:
+            return q.tensor_scalar(out, a, scale, bias, ALU.mult, ALU.add)
+        return q.tensor_scalar(out, a, scale, None, ALU.mult) if scale != 1.0 else q.tensor_copy(out, a)
+
     for e in ENGS:
         q = Q[e]
         for i in PLAN["queue"][e]:
             o = ops[i]
             for d in o["we"]:
-                q.wait_ge(T.sem["e_" + ops[d]["eng"]], PLAN["count"][d])
+                q.wait_ge(T.sem["e_" + ops[d]["use"]], PLAN["count"][d])
             for bt in o["wb"]:
                 q.wait_ge(T.sem["b%d" % bt], total(bt))
             k, a = o["kind"], o["args"]
@@ -846,19 +1314,20 @@ def rank_program(g, core, T, topo):
                     ins = q.tensor_scalar(R(a[0]), R(a[1]), R(a[2]), None, a[4])
                 else:
                     ins = q.tensor_scalar(R(a[0]), R(a[1]), R(a[2]), R(a[3]), a[4], a[5])
-            elif k == "cp":
-                ins = q.tensor_copy(R(a[0]), R(a[1]))
+            elif k == "scan" and a[3]:
+                ins = q.tensor_tensor_scan(R(a[0]), R(a[1]), R(a[2]), 0.0, ALU.mult, ALU.add)
+            elif k == "scan":
+                ins = q.tensor_tensor_scan(R(a[0]), R(a[2]), R(a[1]), 0.0, ALU.max, ALU.mult)
             elif k == "ms":
                 ins = q.memset(R(a[0]), a[1])
             elif k == "act":
-                if a[4] != 0.0:
-                    ins = q.activation(R(a[0]), R(a[1]), a[2], bias=a[4], scale=a[3])
-                elif a[3] != 1.0:
-                    ins = q.activation(R(a[0]), R(a[1]), a[2], scale=a[3])
-                else:
-                    ins = q.activation(R(a[0]), R(a[1]), a[2])
+                ins = activation(q, R(a[0]), R(a[1]), a[2], a[3], a[4])
+            elif k == "aff":
+                ins = either(q, e, R(a[0]), R(a[1]), a[2], a[3], a[4])
             elif k == "mm":
                 ins = q.matmul(R(a[0]), R(a[1]), R(a[2]), a[3], a[4])
+            elif k == "sel":
+                ins = q.affine_select(R(a[0]), R(a[1]), a[2], a[3], a[4], a[5], a[6])
             elif SCRATCH[a[0][0]][2] == i32:
                 ins = q.iota(R(a[0]), a[1], a[2], a[3])
             else:

import math
import numpy as np
from concourse.bass import DstId, RemoteDMATransfer
from concourse.mybir import AluOpType, ActivationFunctionType

ALU, ACTF = AluOpType, ActivationFunctionType
V, GH, NR, RO = 768, 512, 4, 3
PAD = 16
HI = 2048
WW = PAD + HI + 2 * GH
GCOL = (PAD + V, PAD + HI, PAD + HI + GH)
CH = ((0, 512), (512, 768))
BL, UN = 128, 64
NS = 6
f32, bf, i32, u16, f16 = "float32", "bfloat16", "int32", "uint16", "float16"
MATS = ["p15", "n15", "n11", "n12", "neg", "m7", "blk", "nblk", "tri", "w1", "w2", "y", "ny", "wb", "r0"]
ROWS = ["cn", "ca", "cp", "m1", "m2", "cf", "c1", "cb", "co", "ct", "cr", "c0", "g25", "g12", "gp", "g0", "g10"]
TWO = 6


def N(dt, n=V):
    return ("sbuf", [128, n], dt)


SCRATCH = {
    "X0": N(f32, 16 * V), "X1": N(f32, 16 * V), "rg": N(bf, 16 * NS * BL), "Xb": N(bf),
    "W0": N(bf, WW), "W1": N(f32, WW), "W2": N(f32, WW), "Wp": N(bf, WW),
    "Ls0": N(bf, GH), "Ls1": N(f32, GH), "fad": N(bf),
    "Yb": ("sbuf", [128, RO, BL], bf), "land": ("sbuf", [128, 3 * RO, BL], bf),
    "Yi": N(i32, 64), "rbh": N(f16),
    "ls": N(f32), "lw": N(f32, V + 8), "Z": N(i32), "nbi": N(i32),
    "dH": N(f16), "nmS": N(f16), "hi": N(bf), "off1": N(u16), "kH": N(bf), "pw": N(bf), "nmH": N(f16),
    "off": N(u16), "off2": N(u16), "RD": N(f16), "c0": N(f16), "Dp": N(f32), "t1": N(f32),
    "fo": N(u16, 48), "K": ("sbuf", [128, 48, 16], f32), "S": ("sbuf", [128, 48, 32], f32),
    "nH": ("sbuf", [128, 48, 16], f16), "aH": ("sbuf", [128, 48, 16], f16),
    "II": N(bf, 256), "mb": ("sbuf", [128, len(MATS), 128], bf), "Sel": ("sbuf", [128, 16, 128], bf),
    "m8": ("sbuf", [128, 4, 128], bf), "mf": N(f32, 128), "cv": ("sbuf", [128, len(ROWS), 128], bf),
    "ones": N(bf, 512), "nones": N(bf, 512), "kc": N(bf, 512), "msk": N(bf, 16 * BL), "c7": N(bf, 16 * UN),
    "gs": N(bf, 8), "iv": N(f32, 128), "p2": N(bf, 128), "b8": N(bf, 128), "pc": N(i32, 8), "pf": N(f32, 8), "pb": N(bf, 8),
    "pa": ("psum", [128, 2048], f32), "ps": ("psum", [128, 128, 16], f32),
}
EXT = {"loud": [128, V], "fade": [128, V], "ph0": [8, V], "rb": [8, V], "nb": [128, V], "ye": [128, V], "yp": [8, V]}
ENGS = ("pe", "dve", "act", "pool", "sp")
NSEM = 60
SEMAPHORES = ["e_" + e for e in ENGS[:4]] + ["b%d" % i for i in range(NSEM)]
AL = slice(None)
CY = 0.83e-3
PAR = {"G": 1.56, "ov": 0.05, "hop": 0.12, "same": 0.06, "pe": 0.7, "dma": 2.0, "kb": 0.22, "far": 1.0, "b2": 1.0, "f": 1.0}
CASES = (({}, 228.0), ({"pe": 0.85, "G": 1.15}, 210.0), ({"dma": 3.5, "kb": 0.4, "far": 2.0, "hop": 0.25, "same": 0.12}, 250.0),
         ({"G": 2.0, "f": 1.3, "pe": 0.55}, 330.0))
OPT = {"ac": (384, 384, 384), "round": 56.0, "soon": 1, "un": (), "lastu": 32, "flat": 0.2, "rv": (3,), "hw": (6, 6, 6), "give": 0.002, "fa": (), "qa": 0, "ja": (), "bv": 1, "hu": 64, "tu": 128, "lu": 128, "su": (5,), "em": "vddsss",
       "tc": (1, 1, 1), "cs": ((0, 1, 2), (), ()),
       "look": 0.1, "fill": 0.45, "pc": ((128,), (128,), (128,)), "mc": ((640,), (640,), (256, 640)),
       "turns": 40, "moves": 24000, "amp": 3.0, "part": 0.05, "heat": 0.0005, "seed": 10}
ASG = {"tg": "act", "lg": "act", "sg": "act", "lgm01": "dve", "lgm03": "dve", "tga01": "dve", "tga02": "dve", "tga04": "dve",
       "sgm04": "dve", "sgm05": "dve", "nH": "any", "s0": "any", "tga11": "dve", "tga21": "dve",
       "mk": "any", "u": "any", "dH": "dve"}
BIAS = {}
STEP = {"tg": (0.0, 2.7, 0), "s0": (0.0, 0.0, 0), "s": (8.0, 8.0, 0), "lg": (16.0, 5.0, 0), "m": (20.0, 4.4, 0), "sg": (26.0, 4.4, 0),
        "h": (44.0, 4.4, 0), "lg2": (16.0, 6.5, 0), "m2": (20.0, 6.5, 0), "sg2": (24.0, 6.5, 0), "h2": (34.0, 6.5, 0),
        "lg0": (16.0, 4.0, 0), "m0": (20.0, 4.0, 0), "sg0": (21.0, 4.0, 0), "h0": (60.0, 3.0, 0), "h1": (36.0, 4.4, 0),
        "xg": (34.0, 6.5, 0)}

SORT_P = "000000000000000000001111000011110000111100000011111111111111111"
SORT_V = "000000001111111100000000111111110000110000010011110000001111111"


def pairwise(n):
    st, a = [], 1
    while a < n:
        st.append([(i, i + a) for i in range(n) if not i & a])
        a *= 2
    a, e = a // 4, 1
    while a > 0:
        d = e
        while d > 0:
            st.append([(b - d * a, b) for b in range((d + 1) * a, n) if (b // a - d - 1) % 2 == 0])
            d //= 2
        a, e = a // 2, 2 * e + 1
    return st


def runs(items):
    rem, out = sorted(items), []
    while rem:
        best = [rem[0]]
        for x in rem:
            for y in rem:
                if y <= x:
                    continue
                d = tuple(b - a for a, b in zip(x, y))
                if min(d) <= 0:
                    continue
                run = [x, y]
                while tuple(a + b for a, b in zip(run[-1], d)) in rem:
                    run.append(tuple(a + b for a, b in zip(run[-1], d)))
                if len(run) > len(best):
                    best = run
        out.append(best)
        for z in best:
            rem.remove(z)
    return out


def sort_steps():
    comps = [(si, l, h) for si, s in enumerate(pairwise(16)) for l, h in s]
    b, v = [int(x) for x in SORT_P], [int(x) for x in SORT_V]
    nxt, last = {}, {}
    for c in range(len(comps) - 1, -1, -1):
        for w in comps[c][1:]:
            nxt[(c, w)] = last.get(w)
            last[w] = c

    def loc(c, w):
        if c is None:
            return ("K", w)
        return ("P", w) if (w == comps[c][1]) == (b[c] == 0) else ("S", 16 * v[c] + w)
    steps = []
    for si in range(10):
        for phs in (0, 1):
            gr = {}
            for c, (s, l, h) in enumerate(comps):
                if s == si:
                    pw, sw = (l, h) if b[c] == 0 else (h, l)
                    w = sw if phs == 0 else pw
                    o = loc(nxt[(c, w)], w)
                    gr.setdefault((w == l, o[0]), []).append((pw, loc(c, sw)[1], o[1]))
            for key, it in gr.items():
                for r in runs(it):
                    steps.append((key[0], key[1], r))
    init = [loc(last[w], w) for w in range(16)]
    first = [(sp, r) for sp in "PS" for r in runs([(w, x[1]) for w, x in enumerate(init) if x[0] == sp])]
    return first, steps


def prog(vals):
    step = vals[1] - vals[0] if len(vals) > 1 else 1
    return slice(vals[0], vals[-1] + 1, step)


def shape_of(name):
    return SCRATCH[name][1] if name in SCRATCH else EXT[name]


def A(name, *idx):
    return (name, idx if idx else (AL,))


def C(name, a, b, step=1):
    return (name, (AL, slice(a, b, step)))


def B3(name, a, b, last=AL):
    return (name, (AL, slice(a, b), last))


def PS(bank, n, off=0):
    if bank < 4:
        return C("pa", 512 * bank + off, 512 * bank + off + n)
    return B3("ps", 32 * (bank - 4) + off // 16, 32 * (bank - 4) + (off + n) // 16)


def Wd(name, v, n, k=None, head=0, tail=0):
    return C(name, 16 * v + head, 16 * (v + n) - tail) if k is None else C(name, 16 * v + k, 16 * (v + n), 16)


def IND(win, offs):
    return ("*", win, offs)


def cells(ap):
    name, idx = ap
    if name in EXT:
        return np.zeros(1, np.int64)
    sh = shape_of(name)[1:]
    return np.arange(int(np.prod(sh))).reshape(sh)[tuple(idx[1:])].reshape(-1)


def build():
    ops = []
    lastw, readers, bank, pebank = {}, {}, {}, {}

    def add(eng, kind, args, outs, ins, cyc, lat=0.0, batch=None, extra=(), key=None):
        n = len(ops)
        raw, war = set(extra), set()
        rd = []
        for a in ins:
            rd += [a[1], a[2]] if a[0] == "*" else ([a[2], a[3]] if a[0] == "?" else [a])
        for a in rd + list(outs):
            if a[0] not in lastw:
                size = 1 if a[0] in EXT else int(np.prod(shape_of(a[0])[1:]))
                lastw[a[0]] = np.full(size, -1, np.int64)
                readers[a[0]] = {}
        for a in rd:
            raw.update(int(x) for x in np.unique(lastw[a[0]][cells(a)]) if x >= 0)
        for a in outs:
            c = cells(a)
            m = np.zeros(len(lastw[a[0]]), bool)
            m[c] = True
            war.update(int(x) for x in np.unique(lastw[a[0]][c]) if x >= 0)
            for r in list(readers[a[0]]):
                rc = readers[a[0]][r]
                hit = m[rc]
                if hit.any():
                    war.add(r)
                    if hit.all():
                        del readers[a[0]][r]
                    else:
                        readers[a[0]][r] = rc[~hit]
        for a in rd:
            c = cells(a)
            old = readers[a[0]].get(n)
            readers[a[0]][n] = c if old is None else np.concatenate([old, c])
        for a in outs:
            lastw[a[0]][cells(a)] = n
        who = eng if key is None else n
        for bk in set((a[0], int(x)) for a in rd + list(outs) if a[0] in ("pa", "ps") for x in np.unique(cells(a) // 512)):
            cur = bank.get(bk)
            if cur is None or cur[0] != who:
                bank[bk] = [who, [n], cur[1] if cur else []]
            else:
                cur[1].append(n)
            war.update(bank[bk][2])
            if eng == "pe":
                if bk in pebank:
                    war.add(pebank[bk])
                pebank[bk] = n
        if batch is not None:
            for x in raw | war:
                if ops[x]["batch"] == batch:
                    war = war | ops[x]["deps"]
            raw = set(x for x in raw if ops[x]["batch"] != batch)
            war = set(x for x in war if ops[x]["batch"] != batch)
        ops.append(dict(eng=eng, kind=kind, args=args, deps=(raw | war) - {n}, cyc=cyc, lat=lat, batch=batch, key=key, tag=tag[0]))
        return n

    tag = [""]

    def size(ap):
        return len(cells(ap))

    def two(*aps):
        return all(SCRATCH[a[0]][2] in (bf, u16, f16) for a in aps)

    def one(out, a):
        return (size(out), "g" if a[0] == "*" else ("h" if two(out, a) else "1"))

    def tt(out, a, b, op):
        w = "g" if a[0] == "*" else ("1" if {"pa", "ps"} & {a[0], b[0]} else ("b" if two(out, a, b) else "2"))
        return add("dve", "tt", (out, a, b, op), [out], [a, b], (size(out), w))

    def ts(out, a, s1, s2, op0, op1=None):
        return add("dve", "ts", (out, a, s1, s2, op0, op1), [out], [a] + [s for s in (s1, s2) if isinstance(s, tuple)], one(out, a))

    def scan(out, m, x, sums=False):
        return add("dve", "scan", (out, m, x, sums), [out], [m, x], (size(out), "h" if two(out, m, x) else "1"))

    def ms(out, val):
        return add("dve", "ms", (out, val), [out], [], one(out, out))

    def act(out, a, fn, scale=1.0, bias=0.0):
        return add("act", "act", (out, a, fn, scale, bias), [out], [a], one(out, a))

    def aff(key, eng, out, a, scale=1.0, bias=0.0, fn=None):
        return add(eng, "aff", (out, a, scale, bias, fn), [out], [a], one(out, a), key=key)

    def mm(out, l, r, start, stop):
        k = l[2] if l[0] == "?" else l
        n = max(min(64, size(k)), size(r)) * (4 if SCRATCH[r[0]][2] == f32 else 1)
        return add("pe", "mm", (out, l, r, start, stop), [out], [l, r], (n, "p"))

    def iota(out, pat, base, cm):
        return add("pool", "iota", (out, pat, base, cm), [out], [], (2 * size(out) + 160, "q"))

    def sel(out, a, pat, op, fill, base, cm):
        return add("pool", "sel", (out, a, pat, op, fill, base, cm), [out], [a], (2 * size(out) + 200, "q"))

    nb = [0]

    def newb():
        nb[0] += 1
        return nb[0] - 1

    landed = []

    def dma(eng, out, a, batch=None, acc=False, kb=1.0, after=()):
        b = newb() if batch is None else batch
        return add(eng, "dma", (out, a, acc), [out], [a, out] if acc else [a], (1200 if eng == "pool" else 140, "c"),
                   ("d", kb * (2 if acc else 1)), b, after)

    def exchange(src, dsts, lat):
        s = add("pool", "send", (src, dsts, newb()), [], [src], (1200, "c"), ("f", lat), newb())
        return add(None, "recv", (), dsts, [], (0, "c"), ("c", 0.5), ops[s]["args"][2], extra=[s])

    ge, gt, eq, ne = ALU.is_ge, ALU.is_gt, ALU.is_equal, ALU.not_equal
    mul, plus, sub, mx, mn = ALU.mult, ALU.add, ALU.subtract, ALU.max, ALU.min
    band, shr = ALU.bitwise_and, ALU.arith_shift_right
    Wn = ["W0", "W1", "W2"]
    LN2 = math.log(2.0)
    P8 = slice(0, 8)

    def mat(name, rows=AL, cols=AL):
        return A("mb", rows, MATS.index(name), cols)

    def row(name, part=None, cols=AL):
        j = ROWS.index(name)
        return A("cv", (slice(0, 33) if j < TWO else slice(0, 1)) if part is None else slice(part, part + 1), j, cols)

    def const(out, name, start=False, stop=False, neg=False):
        r = row(name)
        mm(out, r, A("nones" if neg else "ones", r[1][0], slice(0, size(out))), start, stop)

    def grid(out, name, stop=False):
        const(out, name)
        const(out, name, stop=stop, neg=True)

    eye, f1 = C("II", 0, 128), A("mf")

    b = newb()
    dma("sp", A("Yi", slice(0, 112), slice(0, 32)), A("ph0", slice(1, 8), slice(0, GH)), b)
    dma("act", A("Yi", slice(112, 128), slice(0, 32)), A("ph0", slice(0, 1), slice(0, GH)), b)
    ms(C("Wp", 0, PAD), 0.0)
    ms(C("Wp", GCOL[0], GCOL[0] + GH), 0.0)
    ms(C("Wp", GCOL[1], WW), 0.0)
    ts(C("Yi", 32, 64), C("Yi", 0, 32), 31, None, band)
    tt(A("Yb", AL, 0, slice(0, 32)), C("Yi", 0, 32), C("Yi", 32, 64), sub)
    aff("p0", "dve", A("Yb", AL, 0, slice(32, 64)), C("Yi", 32, 64))
    exchange(A("Yb", AL, 0, slice(0, 64)), [A("land", AL, d, slice(0, 64)) for d in range(3)], 3.0)
    b = newb()
    for d in range(3):
        for j in range(2):
            dma(("sp", "act")[j], A("Wp", slice(4 * j, 128, 16), slice(GCOL[d], GCOL[d] + GH)), A("land", AL, d, slice(32 * j, 32 * j + 32)), b)
    dma("sp", A("Z", P8, AL), A("ph0"))
    b = newb()
    dma("act", A("Ls0", slice(0, 112), AL), A("loud", slice(16, 128), slice(0, GH)), b)
    dma("act", A("Ls0", slice(112, 128), AL), A("loud", slice(0, 16), slice(0, GH)), b)
    dma("sp", A("nbi"), A("nb"), kb=3)
    dma("sp", C("W0", PAD, PAD + V), A("loud"))
    dma("sp", A("fad"), A("fade"))
    ms(A("ones"), 1.0)
    ms(A("nones", slice(0, 1), AL), -1.0)
    ms(A("cv", slice(0, 64), slice(0, TWO), AL), 0.0)
    ms(A("m8", P8, slice(0, 2), AL), 0.0)
    sel(eye, C("ones", 0, 128), [[-1, 128]], eq, 0.0, 0, 1)
    aff("mat", "act", C("II", 128, 256), eye)
    for j, r, w in ((0, 0, -1.0), (0, 4, 1.0), (0, 8, -1.0), (1, 8, 1.0)):
        aff("mat", "act", A("m8", P8, j, slice(r, 128, 16)), A("II", P8, P8), w)
    for name, parts in (("cp", ((0, 0, 512.0), (32, 0, -0.5))),
                        ("gp", ((0, None, 0.0), (0, 0, 1.5 * 2.0 ** 33), (0, 4, 1.5 * 2.0 ** 28), (0, 8, 1.5 * 2.0 ** 28))),
                        ("cn", ((0, None, 2.0 ** 22), (32, None, 2064.0))), ("c1", ((0, None, -2.0 ** 14),)),
                        ("g25", ((0, None, 1.5 * 2.0 ** 48),)), ("ca", ((0, None, 1536 * 2.0 ** 15), (32, None, 2.0 ** 15))),
                        ("cb", ((0, None, 2.0 ** 18),)), ("co", ((0, None, -2944.0), (0, 0, 0.0))),
                        ("ct", ((0, None, 0.0), (0, 0, 16.0))), ("cr", ((0, None, -2048.0), (0, 0, 16.0))), ("c0", ((0, None, 0.0),)), ("g12", ((0, None, 1.5 * 2.0 ** 35),)),
                        ("m1", ((0, None, -0.5),)), ("m2", ((0, None, 0.5), (32, None, -2.0 ** -17))),
                        ("g0", ((0, None, 1.5 * 2.0 ** 23),)), ("cf", ((0, None, 512.0), (32, None, -0.5))),
                        ("g10", ((0, None, 1.5 * 2.0 ** 33),))):
        for part, col, val in parts:
            ms(row(name, part, AL if col is None else slice(col, 128, 16)), val)
    sel(A("gs"), C("ones", 0, 8), [[-16, 8]], ge, 0.0, 0, 1)
    sel(A("gs"), A("gs"), [[16, 8]], ge, 0.0, 15, -1)
    sel(mat("blk"), C("ones", 0, 128), [[-16, 8], [0, 16]], ge, 0.0, 0, 1)
    sel(mat("blk"), mat("blk"), [[16, 8], [0, 16]], ge, 0.0, 15, -1)
    iota(A("kc"), [[0, 32], [2048, 16]], 2048, 0)
    iota(C("pc", 0, 1), [[0, 1]], 0, 1)
    iota(A("iv"), [[0, 8], [1, 16]], -40, 0)
    for name, w in (("p15", 2.0 ** 15), ("n15", -2.0 ** 15), ("n11", -2048.0), ("n12", -4096.0), ("neg", -1.0), ("m7", 7.0)):
        aff("mat", "act", mat(name), eye, w)
    aff("mat", "act", f1, eye)
    aff("mat", "act", mat("nblk"), mat("blk"), -1.0)
    aff("mat", "act", mat("tri"), mat("blk"), -4096.0)
    sel(mat("tri"), mat("tri"), [[-1, 128]], ge, 0.0, 0, 1)
    sel(mat("tri"), mat("tri"), [[-1, 128]], ne, 4096.0, 0, 1)
    sel(A("m8", P8, 2, AL), A("ones", P8, slice(0, 128)), [[1, 128]], ge, 0.0, 0, -16)
    sel(A("m8", P8, 2, AL), A("m8", P8, 2, AL), [[-1, 128]], ge, 0.0, 15, 16)
    aff("mat", "act", A("m8", P8, 3, AL), A("m8", P8, 2, AL), -1.0)
    aff("mat", "act", A("b8"), mat("blk"), 256.0)
    for s in range(16):
        sel(A("Sel", AL, s, AL), A("b8"), [[0, 8], [1, 16]], eq, 0.0, -s, 0)
    ms(A("mb", AL, slice(MATS.index("w1"), MATS.index("w2") + 1), AL), 0.0)
    for name, r, w in (("w1", 0, -1.0), ("w1", 4, 1.0), ("w1", 8, -1.0), ("w2", 8, 1.0)):
        aff("mat", "act", mat(name, AL, slice(r, 128, 16)), A("gs"), w)
    act(A("p2"), A("iv"), ACTF.Sigmoid, LN2)
    act(row("m1", 32), A("p2", slice(32, 33), AL), ACTF.Copy, 2.0 ** 23)
    tt(A("p2"), A("p2"), mat("blk"), mul)
    aff("mat", "act", mat("y"), A("p2"), 2.0 ** 51)
    aff("mat", "act", mat("ny"), A("p2"), -2.0 ** 51)
    ts(C("pc", 2, 3), C("pc", 0, 1), 15, None, band)
    act(C("pb", 0, 1), C("pc", 2, 3), ACTF.Sigmoid, LN2, -40 * LN2)
    ts(C("pf", 0, 1), C("pc", 2, 3), 15.0, -2.0 ** 68, eq, mul)
    ts(C("pf", 2, 3), C("pf", 0, 1), 2.0 ** 67, C("pb", 0, 1), plus, mul)
    ts(mat("wb"), mat("blk"), C("pf", 2, 3), None, mul)
    ts(C("pf", 4, 5), C("pc", 2, 3), 0.0, 2.0 ** -13, eq, mul)
    ts(mat("r0"), mat("blk"), C("pf", 4, 5), 2.0 ** 12, mul, mul)
    for w in range(0, BL, 32):
        sel(Wd("msk", w, 32), A("ones"), [[0, 32], [1, 16]], gt, 0.0, 0, 0)
    if OPT["cs"][0]:
        iota(A("c7"), [[0, 16 * UN]], 128, 0)
    for w in Wn:
        ms(C(w, 0, PAD), 0.0)
    ms(C("lw", V, V + 8), 0.0)
    aff("p0", "dve", A("RD", P8, AL), A("Z", P8, AL))
    aff("fad", "dve", A("fad"), A("fad"), 0.125)
    for c, (a, z) in enumerate(CH):
        ts(C("Z", a, z), C("nbi", a, z), 4095, None, band)
        ts(PS(2 + c, z - a), C("Z", a, z), 1280.0, 768.0, ge, mul)
        tt(C("ls", a, z), C("nbi", a, z), PS(2 + c, z - a), plus)
    dma("sp", A("nbi", P8, AL), A("rb"))
    aff("rb", "act", A("rbh", P8, AL), A("nbi", P8, AL))
    for w in ("W0", "Wp", "W1", "W2"):
        dma("sp", C(w, GCOL[0] + GH, GCOL[1]), A("fade" if SCRATCH[w][2] == bf else "ls"), kb=2)

    def times(t, c, a, z, srcs):
        p, last = PS(4 + c, z - a), t == RO
        const(p, "cf" if last else "cp", start=True)
        for j in range(2):
            use = srcs if j == 0 else srcs[::-1]
            for i, (x, few) in enumerate(use):
                m = A("m8", P8, 3 - j if last else j, AL) if few else mat((("w1", "w2"), ("nblk", "blk"))[last][j])
                mm(p, m, x, False, j == 1 and i == len(use) - 1)
            if j == 0:
                grid(p, "g10" if last else "gp")
        if last:
            aff("yp", "act", C("Dp", a, z), p)
            dma("sp", A("yp", AL, slice(a, z)), A("Dp", slice(0, 128, 16), slice(a, z)))
            return
        aff("wp", "act", C("Wp", PAD + a, PAD + z), p)
        if z == GH and t > 0:
            for q in range(4):
                mm(PS(4 + c, BL), C("II", 16 - q, 144 - q), C("Wp", PAD + BL * q, PAD + BL * (q + 1)), q == 0, q == 3)
            aff("yb", "act", A("Yb", AL, t, AL), PS(4 + c, BL))
            exchange(A("Yb", AL, t, AL), [A("land", AL, 3 * t + d, AL) for d in range(3)], 3.0)
            bt = newb()
            for d in range(3):
                landed.append(dma("sp", A("Wp", slice(0, 128, 4), slice(GCOL[d], GCOL[d] + GH)), A("land", AL, 3 * t + d, AL), bt))

    def ghosts(w):
        return [C(w, x, x + GH) for x in GCOL]

    first, steps = sort_steps()
    slot = [0]

    def ring():
        slot[0] = (slot[0] + 1) % NS
        return slot[0] * BL

    def names(t, c):
        a, z = CH[c]
        lst, p = C("ls", a, z), PS(2 + c, z - a)
        if t < RO - 1:
            dma("sp", C("lw", a, z), lst, kb=2)
        aff("dH", "act", C("dH", a, z), lst, 2.0 ** -12, 1024.5625)
        mm(p, mat("n12"), C("dH", a, z), True, False)
        const(p, "cn")
        mm(p, f1, lst, False, True)
        aff("nmS", "act", C("nmS", a, z), p)
        aff("off1", "dve", C("off1", a, z), C("nmS", a, z), 1.0, 2048.0)
        aff("hi", "dve", C("hi", a, z), C("nmS", a, z), 64.0, 32.0, "sign")

    def arrival(t, c, a, z):
        for v in range(a, z, BL):
            s = ring()
            tag[0] = "a%d%d" % (t, v // BL)
            for w in range(0, BL, OPT["tu"]):
                aff("tg", "act", Wd("rg", s + w, OPT["tu"]), IND(A("Wp"), C("off1", v + w, v + w + OPT["tu"])))
            o = 512 * c + v - a
            mm(C("pa", o, o + BL), C("dH", v, v + BL), eye, True, False)
            mm(C("pa", o, o + BL), C("Wp", PAD + v, PAD + v + BL), mat("nblk"), False, False)
            for k in range(16):
                mm(C("pa", o + k, o + BL, 16), Wd("rg", s, BL, k), A("gs"), False, k == 15)
        nh, p = B3("nH", a // 16, z // 16), PS(4 + c, z - a)
        aff("nH", "act", nh, PS(c, z - a), 1.0, -1537.0)
        mm(p, mat("n15"), nh, True, False)
        const(p, "c1")
        grid(p, "g25")
        mm(p, mat("p15"), nh, False, False)
        mm(p, eye, C("kc", 0, z - a), False, False)
        for v in range(a, z, BL):
            mm(PS(4 + c, BL, v - a), C("hi", v, v + BL), mat("n11"), False, False)
            mm(PS(4 + c, BL, v - a), C("nmS", v, v + BL), eye, False, v + BL == z)

    def sort(a, z, r0):
        def at(sp, w):
            return B3("ps", r0, r0 + z - a, w) if sp == "P" else B3(sp, a, z, w)
        for sp, r in first:
            if sp == "S":
                aff("s0", "act", at("S", prog([x[1] for x in r])), at("P", prog([x[0] for x in r])))
        for ismin, sp, r in steps:
            pw, sw, ow = [prog([x[j] for x in r]) for j in range(3)]
            tt(at(sp, ow), at("P", pw), at("S", sw), mn if ismin else mx)

    def places(a, z, banks):
        bR, bB, bV = banks if OPT["bv"] or a == 0 else (6, 7, 3)
        aff("aH", "act", B3("aH", a // 16, z // 16), B3("K", a // 16, z // 16), 2.0 ** -15, 1536.5)

        def low(bk, stop):
            for v in range(a, z, BL):
                p, r = PS(bk, BL, v - a), v // 16
                mm(p, B3("aH", r, r + 8), mat("n15"), True, False)
                const(p, "ca")
                mm(p, B3("K", r, r + 8), f1, False, stop)
                if not stop:
                    const(p, "cb")
                    mm(p, mat("n11"), C("kH", v, v + BL), False, True)
        low(bR, True)
        aff("kH", "act", C("kH", a, z), PS(bR, z - a), 2.0 ** -11, 128.5)
        act(C("pw", a, z), C("kH", a, z), ACTF.Sigmoid, -LN2, 117 * LN2)
        mm(PS(bB, z - a), mat("wb"), C("hi", a, z), True, True)
        low(bV, False)
        tt(C("Z", a, z), C("pw", a, z), PS(bB, z - a), mul)
        ts(C("Z", a, z), C("Z", a, z), 4, HI, shr, band)
        tt(C("nmH", a, z), C("Z", a, z), PS(bV, z - a), plus)
        aff("off", "dve", C("off", a, z), C("nmH", a, z), 1.0, 2048.0)

    def fetch(t, c):
        a, z = CH[c]
        n = (z - a) // 16
        ts(C("c0", a, z), C("nmH", a, z), -1264.0, C("pf", 4, 5), mn, mul)
        aff("own", "act", C("nmS", a, z), C("nmH", a, z), -64.0, -64 * 1264.5, "sign")
        p = PS(7 - c, n)
        for i in range(16):
            mm(p, A("Sel", AL, i, AL), C("c0", a + i, z, 16), i == 0, i == 15)
        aff("fo", "act", C("fo", a // 16, z // 16), p, 32.0, 2032.0)
        tt(C("Dp", a, z), IND(A("lw"), C("fo", a // 16, z // 16)), C("ls", a, z), sub)

    unit, signs = [0], {}

    def masking(t, c, a, z):
        X, win, cnt = "X%d" % min(t, 1), A(Wn[t]), 4 + c
        tag[0] = "m%d%d" % (t, a // BL)
        turn = OPT["tc"][t]
        if not turn:
            const(PS(cnt, z - a), "co", start=True)

        def sign(s, v, n, src):
            signs[t] = aff("sg", "act", Wd("rg", s, n), src, 2.0 ** 40, -2.0 ** 13, "sign")
            for k in range(1, 16 * (not turn)):
                mm(PS(cnt, n, v - a), A("Sel", AL, k, AL), Wd("rg", s, n, k), False, False)
        for v in range(a, z, BL):
            tag[0] = "m%d%d" % (t, v // BL)
            src = IND(win, C("off", v, v + BL))
            cast = v // BL in OPT["cs"][t]
            if t == 0:
                j = v // BL
                x, top, s = BL * (3 + 2 * j % 3), BL * (3 + (2 * j + 1) % 3), BL * (j % 3)
                aff("lg", "act", Wd("rg", x, BL), src)
                if j in OPT["rv"]:
                    for w in range(0, BL, UN):
                        unit[0] ^= 1
                        r = UN * unit[0]
                        scan(Wd("pa", r, UN, head=1), Wd("msk", 0, UN, head=1), Wd("rg", x + w, UN, tail=1))
                        ms(C("pa", 16 * r, 16 * r + 1), 0.0)
                        tt(C("Xb", v + w, v + w + UN), Wd("rg", x + w, UN, 15), Wd("pa", r, UN, 15), mx)
                        tt(Wd(X, v + w, UN), Wd("rg", x + w, UN), Wd("pa", r, UN), sub)
                        sign(s + w, v + w, UN, Wd(X, v + w, UN))
                else:
                    scan(Wd("rg", top, BL, head=1), Wd("msk", 0, BL, head=1), Wd("rg", x, BL, tail=1))
                    tt(C("Xb", v, v + BL), Wd("rg", top, BL, 15), Wd("rg", x, BL, 15), mx)
            else:
                s = ring()
                for w in range(v, v + BL, OPT["lu"]):
                    aff("lg", "act", Wd(X, w, OPT["lu"]), IND(win, C("off", w, w + OPT["lu"])))
            whole = t > 0 and v // BL in OPT["un"]
            if whole:
                scan(Wd("pa", 0, BL, head=1), Wd("msk", 0, BL, head=1), Wd(X, v, BL, tail=1))
                if t < RO - 1:
                    tt(C("t1", v, v + BL), Wd(X, v, BL, 15), Wd("pa", 0, BL, 15), mx)
                tt(Wd(X, v, BL, head=1), Wd(X, v, BL, head=1), Wd("pa", 0, BL, head=1), sub)
            for w in range(0, BL * (not whole and (t > 0 or j not in OPT["rv"])), UN):
                unit[0] ^= 1
                r = UN * unit[0]
                if t == 0:
                    for h in range(0, UN, 32):
                        mm(Wd("pa", r + h, 32), eye, Wd("rg", x + w + h, 32), True, False)
                        mm(Wd("pa", r + h, 32, head=1), mat("neg"), Wd("rg", top + w + h, 32, head=1), False, True)
                    if not cast:
                        sign(s + w, v + w, UN, Wd("pa", r, UN))
                    act(Wd(X, v + w, UN), Wd("pa", r, UN), ACTF.Sigmoid)
                else:
                    scan(Wd("pa", r, UN, head=1), Wd("msk", 0, UN, head=1), Wd(X, v + w, UN, tail=1))
                    if t < RO - 1:
                        tt(C("t1", v + w, v + w + UN), Wd(X, v + w, UN, 15), Wd("pa", r, UN, 15), mx)
                    d = Wd(X, v + w, UN, head=1)
                    tt(d, d, Wd("pa", r, UN, head=1), sub)
                    if v // BL in OPT["su"]:
                        sign(s + w, v + w, UN, Wd(X, v + w, UN))
            if cast and t == 0:
                for w in range(0, BL, UN):
                    dma("sp", Wd("rg", s + w, UN), A("c7"), kb=2)
                dma("pool", Wd("rg", s, BL), Wd(X, v, BL), acc=True, kb=6)
            elif cast:
                dma("pool", Wd("rg", s, BL), Wd(X, v, BL), kb=8)
                sign(s, v, BL, Wd("rg", s, BL))
            elif t > 0 and v // BL not in OPT["su"]:
                sign(s, v, BL, Wd(X, v, BL))
            if turn:
                r = 32 * c + (v - a) // 16
                mm(B3("ps", r, r + 8), A("ones", slice(0, 1), slice(0, BL)), row("cr" if cast and t == 0 else "ct"), True, False)
                for k in range(1, 16):
                    mm(B3("ps", r, r + 8, k), Wd("rg", s, BL, k), A("gs"), False, k == 15)
        tag[0] = "t%d%d" % (t, a // BL)
        p = PS(cnt, z - a)
        if turn:
            aff("mk", "act", B3("nH", a // 16, z // 16), p, -64.0, 224.0, "sign")
            mm(p, eye, C("nmH", a, z), True, False)
            for v in range(a, z, BL):
                mm(PS(cnt, BL, v - a), B3("nH", v // 16, v // 16 + 8), mat("n12"), False, v + BL == z)
        else:
            grid(p, "g12")
            mm(p, eye, C("nmH", a, z), False, True)
        soon, un = t < RO - 1 and OPT["soon"], "RD" if OPT["qa"] else "kH"
        if soon:
            aff("u", "act", C(un, a, z), p, 8.0, 16320.0, "sign")
        aff("off2", "act", C("off2", a, z), p, 1.0, 2048.0, "relu")
        if not soon:
            aff("u", "dve", C(un, a, z), C("off2", a, z), 2.0, -16.0, "sign")
        bD = 6 if soon else cnt
        p = PS(bD, z - a)
        for v in range(a, z, BL):
            mm(PS(bD, BL, v - a), B3("aH", v // 16, v // 16 + 8), eye, True, False)
            mm(PS(bD, BL, v - a), mat("tri"), C(un, v, v + BL), False, True)
        aff("RD", "act", C("RD", a, z), p, 1.0, -5121.0, "relu")
        times(t + 1, 3 if soon else c, a, z, [(A("rbh", P8, slice(a, z)), True), (C("Wp", PAD + a, PAD + z), False), (C("RD", a, z), False)])

    def lists(t, c):
        a, z = CH[c]
        p = PS(7 - c, z - a)
        if OPT["qa"]:
            mm(p, eye, C("kH", a, z), True, False)
            for v in range(a, z, BL):
                mm(PS(7 - c, BL, v - a), B3("nH", v // 16, v // 16 + 8), mat("p15"), False, v + BL == z)
            act(C("hi", a, z), p, ACTF.Sigmoid, -LN2, 117 * LN2)
        else:
            tt(C("hi", a, z), C("kH", a, z), C("pw", a, z), mul)
        const(p, "m1", start=True)
        mm(p, mat("y"), C("hi", a, z), False, False)
        grid(p, "g0")
        mm(p, mat("ny"), C("hi", a, z), False, False)
        const(p, "m2")
        mm(p, mat("r0"), C("nmS", a, z), False, False)
        grid(p, "g0", True)
        if c in OPT["ja"]:
            tt(C("Dp", a, z), C("Dp", a, z), p, mul)
            dma("pool", C("ls", a, z), C("Dp", a, z), acc=True, kb=(z - a) / 256)
        else:
            tt(p, C("Dp", a, z), p, mul)
            tt(C("ls", a, z), C("ls", a, z), p, plus)

    def loudness(t, c):
        a, z = CH[c]
        p, own, new = PS(6 + c, z - a), C(Wn[t], PAD + a, PAD + z), Wn[t + 1]
        if t == 0:
            mm(p, eye, C("Xb", a, z), True, False)
            mm(p, mat("m7"), own, False, True)
        else:
            aff("l8", "act", p, own)
            tt(C("t1", a, z), C("t1", a, z), p, sub)
            aff("l8", "act", p, own, 8.0)
            tt(p, C("t1", a, z), p, plus)
        tt(C(new, PAD + a, PAD + z), p, C("fad", a, z), mul)
        if c == 0:
            bt = newb()
            dma("sp", A("Ls1", slice(0, 112), AL), A(new, slice(16, 128), slice(PAD, PAD + GH)), bt, kb=2)
            dma("sp", A("Ls1", slice(112, 128), AL), A(new, slice(0, 16), slice(PAD, PAD + GH)), bt, kb=2)
            exchange(A("Ls1"), ghosts(new), 8.0)

    def hearing(t, c):
        a, z = CH[c]
        X = "X%d" % min(t, 1)
        sums, scans = [], []
        for v in range(a, z, BL):
            tag[0] = "h%d%d" % (t, v // BL)
            x = Wd(X, v, BL)
            how = OPT["em"][v // BL]
            direct = t == RO - 1 and how in "ps"
            step = OPT["lastu"] if direct and v + BL == V else OPT["hu"]
            for w in range(v, v + BL, step):
                y = Wd(X, w, step)
                if t == RO - 1 and v // BL in OPT["fa"]:
                    unit[0] ^= 1
                    p = Wd("pa", UN * unit[0], step)
                    act(p, y, ACTF.Sigmoid)
                    aff("xg", "act", y, IND(A(Wn[t]), C("off2", w, w + step)))
                    tt(y, y, p, mul)
                    continue
                if t > 0 or v // BL in OPT["rv"]:
                    act(y, y, ACTF.Sigmoid)
                n = tt(y, IND(A(Wn[t]), C("off2", w, w + step)), y, mul)
                if v // BL >= OPT["hw"][t]:
                    ops[n]["deps"].add(signs[t])
            if t > 0 and not direct:
                dma("pool", Wd("X0", v, BL), x, acc=True, kb=8, after=landed[-1:] if t < RO - 1 else ())
            if t == RO - 1:
                if how == "v":
                    scan(x, A("msk"), Wd("X0", v, BL), True)
                    aff("ye", "act", C("t1", v, v + BL), Wd(X, v, BL, 15))
                    continue
                sums.insert(len(sums) if not direct else 0, ("X0", v, BL))
                if direct:
                    (sums if how == "p" else scans).extend((X, w, step) for w in range(v, v + BL, step))
        if t == RO - 1:
            tag[0] = "e%d%d" % (t, c)
            if sums:
                const(PS(6 + c, z - a), "c0", start=True)
            for i, (Y, w, n) in enumerate(sums):
                for k in range(16):
                    mm(PS(6 + c, n, w - a), f1, Wd(Y, w, n, k), False, i == len(sums) - 1 and k == 15)
            for v in range(a, z, BL):
                if OPT["em"][v // BL] in "dp":
                    aff("ye", "act", C("t1", v, v + BL), PS(6 + c, BL, v - a))
            for Y, w, n in scans:
                tag[0] = "h%d%d" % (t, w // BL)
                scan(Wd("X0", w, n), Wd("msk", 0, n), Wd(Y, w, n), True)
                tt(C("t1", w, w + n), Wd("X0", w, n, 15), PS(6 + c, n, w - a), plus)
            dma("sp", A("ye", AL, slice(a, z)), C("t1", a, z), kb=2)

    def do(step, t, c):
        tag[0] = "%s%d%d" % (step[0], t, c)
        step[1](t, c)

    def cuts(at, a, z):
        at = [a] + [x for x in at if a < x < z] + [z]
        return list(zip(at, at[1:]))

    for c in range(2):
        times(0, c, CH[c][0], CH[c][1], [(A("RD", P8, slice(*CH[c])), True)])
    exchange(A("Ls0"), ghosts("W0"), 4.0)
    for t in range(RO):
        for c in range(2):
            do(("n", names), t, c)
        halves = cuts((OPT["ac"][t] or GH,), 0, V)
        for c, (a, z) in enumerate(halves):
            arrival(t, c, a, z)
        for c, (a0, z0) in enumerate(halves):
            tag[0] = "s%d%d" % (t, c)
            if OPT["ac"][t]:
                sort(a0 // 16, z0 // 16, 32 * c)
            elif c == 0:
                sort(0, V // 16, 0)
            for a, z in cuts(OPT["pc"][t], a0, z0):
                tag[0] = "p%d%d" % (t, a // BL)
                places(a, z, (2, 3, 0) if a == 0 else (6, 7, 6 if OPT["ac"][t] else 5))
        for c in range(2):
            if t < RO - 1:
                do(("f", fetch), t, c)
        j = 0
        for c in range(2):
            for a, z in cuts(OPT["mc"][t], *CH[c]):
                masking(t, j % 2, a, z)
                j += 1
            if t < RO - 1:
                do(("v", loudness), t, c)
                do(("l", lists), t, c)
        for c in range(2):
            do(("h", hearing), t, c)
    members = {}
    for i, o in enumerate(ops):
        if o["batch"] is not None:
            members.setdefault(o["batch"], []).append(i)
    for o in ops:
        for d in list(o["deps"]):
            if ops[d]["batch"] is not None:
                o["deps"].update(members[ops[d]["batch"]])
    return ops, members


def price(o, e, par):
    n, w = o["cyc"]
    if w == "c":
        c = n * CY
    elif w == "q":
        c = n * CY * par["f"]
    elif w == "p":
        c = 0.01 + n * CY * par["pe"] * par["f"]
    else:
        k = {"g": par["G"], "h": 0.5 if e == "dve" else 1, "1": 1, "2": 2, "b": par["b2"]}[w]
        c = ((1.3 if e == "act" else 1) * par["ov"] + max(64, n * k) * CY) * par["f"]
    lat = o["lat"]
    if lat:
        lat = {"d": par["dma"] + par["kb"] * lat[1], "f": lat[1] * par["far"], "c": lat[1]}[lat[0]]
    return c, lat


def queue_of(o):
    return ASG.get(o["key"] + o["tag"], ASG.get(o["key"], o["eng"])) if o["key"] else o["eng"]


def rank(o, path, e):
    tag = o["tag"]
    bias = BIAS.get(tag, 0.0) + BIAS.get(tag[:2], 0.0) + BIAS.get((o["key"] or o["kind"]) + tag, 0.0)
    if e not in ("act", "dve", "any") or o["cyc"][0] < 900 and tag[:1] != "s" or not tag:
        return 1000.0 + path + bias
    step, t, b = (o["key"] or tag[0]), int(tag[1]), int(tag[2])
    at, pace, late = STEP.get(step + tag[1], STEP[step])
    return -(OPT["round"] * (t + late) + at + pace * b) + bias + 1e-3 * path


def order(ops, par, fixed=None):
    n = len(ops)
    eng = [queue_of(o) for o in ops]
    if fixed is not None:
        for e in ENGS:
            for i in fixed[e]:
                eng[i] = e
    cost = [{e: price(o, e, par) for e in (("act", "dve") if eng[i] == "any" else (eng[i],))} for i, o in enumerate(ops)]
    succ = [[] for _ in ops]
    for i, o in enumerate(ops):
        for d in o["deps"]:
            succ[d].append(i)

    def gap(d, j):
        if eng[d] == eng[j] != "any" and ops[d]["batch"] is None:
            return 0.0 if eng[d] == "pe" else par["same"]
        return par["hop"]
    left = [len(o["deps"]) for o in ops]
    pr = [0.0] * n
    if fixed is None:
        topo = [i for i in range(n) if left[i] == 0]
        for i in topo:
            for j in succ[i]:
                left[j] -= 1
                if left[j] == 0:
                    topo.append(j)
        for i in reversed(topo):
            pr[i] = sum(min(cost[i].values())) + max([pr[j] + gap(i, j) for j in succ[i]] + [0.0])
        for i, o in enumerate(ops):
            pr[i] = rank(o, pr[i], eng[i])
        left = [len(o["deps"]) for o in ops]
    ready = {e: [] for e in ENGS + (None,)}
    rt, free, end = [0.0] * n, {e: 0.0 for e in ENGS}, 0.0
    queue = {e: [] for e in ENGS}

    def offer(j):
        for e in cost[j]:
            ready[e].append(j)
    for i in range(n):
        if left[i] == 0:
            offer(i)
    look, fill, lines = OPT["look"], OPT["fill"], 0.0
    for step in range(n):
        if ready[None]:
            i, e = ready[None].pop(), None
            start = rt[i]
        else:
            best = None
            for e in ENGS:
                can = ready[e]
                if fixed is not None:
                    k = len(queue[e])
                    can = [fixed[e][k]] if k < len(fixed[e]) and left[fixed[e][k]] == 0 else []
                if can:
                    t0 = max(free[e], min(rt[j] for j in can))
                    if best is None or t0 < best[0]:
                        best = (t0, e, can)
            t0, e, can = best
            i = can[0]
            if fixed is None:
                i = max((j for j in can if rt[j] <= t0 + look), key=lambda j: (pr[j], -j))
                if rt[i] > t0 + 1e-6:
                    now = [j for j in can if rt[j] <= t0 + 1e-6 and cost[j][e][0] <= fill]
                    if now:
                        i = max(now, key=lambda j: (pr[j], -j))
                for x in cost[i]:
                    ready[x].remove(i)
            start = max(t0, rt[i])
            free[e] = start + cost[i][e][0]
            queue[e].append(i)
            eng[i] = e
        ops[i]["start"], ops[i]["use"] = start, e
        fin = start + sum(cost[i][e])
        if ops[i]["kind"] in ("dma", "send"):
            wait = max(0.0, lines - start - cost[i][e][0] - 1.0)
            fin += wait
            lines = start + cost[i][e][0] + 1.0 + wait + par["kb"] * (ops[i]["lat"][1] if ops[i]["kind"] == "dma" else 1.0)
        end = max(end, fin)
        for j in succ[i]:
            rt[j] = max(rt[j], fin + gap(i, j))
            left[j] -= 1
            if left[j] == 0 and (fixed is None or eng[j] is None):
                offer(j)
    return queue, end


def waits(ops, members, queue):
    pos = {}
    for e in ENGS:
        for p, i in enumerate(queue[e]):
            pos[i] = p
    marked, waited = set(), set()
    for e in ENGS:
        known, seen = {}, set()
        for i in queue[e]:
            o = ops[i]
            need, o["wb"] = {}, []
            for d in sorted(o["deps"]):
                bt, x = ops[d]["batch"], ops[d]["use"]
                if bt is not None:
                    if bt not in seen:
                        seen.add(bt)
                        waited.add(bt)
                        o["wb"].append(bt)
                elif x != e or e != "pe":
                    if pos[d] > known.get(x, -1) and pos[d] > pos.get(need.get(x), -1):
                        need[x] = d
            for x, d in need.items():
                known[x] = pos[d]
                marked.add(d)
            o["we"] = list(need.values())
    count = {}
    for e in ENGS:
        c = 0
        for i in queue[e]:
            if i in marked:
                c += 1
                count[i] = c
    return count, [x for x in members if x not in waited]


PLAN = {}


def place(ops, par, key, back):
    n = len(ops)
    pre, suc = [list(o["deps"]) for o in ops], [[] for _ in ops]
    for i, o in enumerate(ops):
        for d in o["deps"]:
            suc[d].append(i)
    if back:
        pre, suc = suc, pre
    left = [len(x) for x in pre]
    can = sorted(((key[i], i) for i in range(n) if left[i] == 0), reverse=True)
    busy = {e: [] for e in ENGS}
    start, fin, use = [0.0] * n, [0.0] * n, [None] * n
    while can:
        i = can.pop()[1]
        eng, best = queue_of(ops[i]), None
        for e in (("act", "dve") if eng == "any" else (eng,)):
            c, lat = price(ops[i], e, par)
            r = 0.0
            for d in pre[i]:
                same = use[d] == e and ops[i if back else d]["batch"] is None
                r = max(r, fin[d] + ((0.0 if e == "pe" else par["same"]) if same else par["hop"]))
            r += lat if back else 0.0
            k = 0
            if e is not None:
                line = busy[e]
                k = len(line)
                while k > 0 and line[k - 1][1] > r:
                    k -= 1
                while k < len(line) and line[k][0] < r + c - 1e-9:
                    r = max(r, line[k][1])
                    k += 1
            if best is None or r + c < best[0]:
                best = (r + c, r, e, k, lat)
        z, r, e, k, lat = best
        if e is not None:
            busy[e].insert(k, (r, z))
        start[i], use[i], fin[i] = r, e, z + (0.0 if back else lat)
        new = []
        for j in suc[i]:
            left[j] -= 1
            if left[j] == 0:
                new.append((key[j], j))
        if new:
            can = sorted(can + new, reverse=True)
    return start, fin, use


def refine(ops, turns, seed):
    rng = np.random.default_rng(seed)
    group = [(o["key"] or o["kind"]) + o["tag"] + str(o["eng"]) for o in ops]
    names = sorted(set(group))

    def judge(start, fin, use):
        queue = {e: [] for e in ENGS}
        for i in sorted(range(len(ops)), key=lambda i: (start[i], i)):
            if use[i] is not None:
                queue[use[i]].append(i)
        v = [order(ops, dict(PAR, **m), queue)[1] / w for m, w in CASES]
        return sum(v) / len(v) + 0.5 * max(v), fin, queue
    order(ops, PAR)
    best = judge(*place(ops, PAR, [o["start"] for o in ops], False))
    for turn in range(turns):
        late = place(ops, PAR, [-x for x in best[1]], True)[1]
        shift = dict(zip(names, 3.0 * rng.standard_normal(len(names)) * (rng.random(len(names)) < 0.05)))
        now = judge(*place(ops, PAR, [float(shift[group[i]]) - x for i, x in enumerate(late)], False))
        if now[0] < best[0]:
            best = now
    order(ops, PAR, best[2])
    return best[2]


def graph(ops):
    n = len(ops)
    left, suc = [len(o["deps"]) for o in ops], [[] for _ in ops]
    for i, o in enumerate(ops):
        for d in o["deps"]:
            suc[d].append(i)
    topo = [i for i in range(n) if left[i] == 0]
    for i in topo:
        for j in suc[i]:
            left[j] -= 1
            if left[j] == 0:
                topo.append(j)
    before, pre, suc = [0] * n, [None] * n, [[] for _ in ops]
    for i in topo:
        far = 0
        for d in ops[i]["deps"]:
            far |= before[d]
        pre[i] = [d for d in sorted(ops[i]["deps"]) if not far >> d & 1]
        before[i] = far | sum(1 << d for d in pre[i])
        for d in pre[i]:
            suc[d].append(i)
    return pre, suc


def prices(ops, par):
    return [{e: price(o, e, par) for e in (("act", "dve") if o["key"] else (o["eng"],))} for o in ops]


def place(ops, links, cost, par, key, back):
    n = len(ops)
    pre, suc = links[::-1] if back else links
    left = [len(x) for x in pre]
    todo = sorted(range(n), key=lambda i: (key[i], i))
    held = [False] * n
    busy = {e: [] for e in ENGS}
    start, fin, use = [0.0] * n, [0.0] * n, [None] * n
    near, hop = {e: par["same"] for e in ENGS + (None,)}, par["hop"]
    near["pe"] = 0.0
    for first in todo:
        if left[first]:
            held[first] = True
            continue
        now = [first]
        while now:
            i = now.pop()
            eng, best = queue_of(ops[i]), None
            for e in (("act", "dve") if eng == "any" else (eng,)):
                c, lat = cost[i][e]
                r = 0.0
                for d in pre[i]:
                    x = fin[d] + (near[e] if use[d] == e and ops[i if back else d]["batch"] is None else hop)
                    if x > r:
                        r = x
                if back:
                    r += lat
                k = 0
                if e is not None:
                    line = busy[e]
                    k = len(line)
                    while k > 0 and line[k - 1][1] > r:
                        k -= 1
                    while k < len(line) and line[k][0] < r + c - 1e-9:
                        r = max(r, line[k][1])
                        k += 1
                if best is None or r + c < best[0]:
                    best = (r + c, r, e, k, lat)
            z, r, e, k, lat = best
            if e is not None:
                busy[e].insert(k, (r, z))
            start[i], use[i], fin[i] = r, e, z + (0.0 if back else lat)
            for j in suc[i]:
                left[j] -= 1
                if left[j] == 0 and held[j]:
                    now.append(j)
            now.sort(key=lambda j: -key[j])
    return start, fin, use


def replay(ops, pre, cost, par, seq, use):
    fin, free, lines = [0.0] * len(ops), {e: 0.0 for e in ENGS + (None,)}, 0.0
    near, hop = {e: par["same"] for e in free}, par["hop"]
    near["pe"] = 0.0
    for i in seq:
        e = use[i]
        r = free[e]
        for d in pre[i]:
            x = fin[d] + (near[e] if use[d] == e and ops[d]["batch"] is None else hop)
            if x > r:
                r = x
        c, lat = cost[i][e]
        if e is not None:
            free[e] = r + c
        fin[i] = r + c + lat
        if lat and e is not None:
            wait = max(0.0, lines - r - c - 1.0)
            fin[i] += wait
            lines = r + c + 1.0 + wait + par["kb"] * (ops[i]["lat"][1] if ops[i]["kind"] == "dma" else 1.0)
    return max(fin)


def refine(ops, turns, seed, move=None):
    rng = np.random.default_rng(seed)
    group = [(o["key"] or o["kind"]) + o["tag"] + str(o["eng"]) for o in ops]
    names = sorted(set(group))
    links, cost = graph(ops), prices(ops, PAR)
    cases = [(dict(PAR, **m), prices(ops, dict(PAR, **m)), w) for m, w in CASES]

    def judge(start, fin, use):
        seq = sorted(range(len(ops)), key=lambda i: (start[i], i))
        v = [replay(ops, links[0], c, par, seq, use) / w for par, c, w in cases]
        return sum(v) / len(v) + 0.5 * max(v), fin, seq, use
    order(ops, PAR)
    best = cur = judge(*place(ops, links, cost, PAR, [o["start"] for o in ops], False))
    for turn in range(turns):
        undo = move(rng) if move else None
        late = place(ops, links, cost, PAR, [-x for x in cur[1]], True)[1]
        shift = dict(zip(names, OPT["amp"] * rng.standard_normal(len(names)) * (rng.random(len(names)) < OPT["part"])))
        now = judge(*place(ops, links, cost, PAR, [float(shift[group[i]]) - x for i, x in enumerate(late)], False))
        if now[0] < cur[0] + OPT["heat"] * (1.0 - turn / turns) * rng.random():
            cur = now
            best = min(best, cur, key=lambda x: x[0])
        elif undo:
            undo()
    queue = {e: [i for i in best[2] if best[3][i] == e] for e in ENGS}
    order(ops, PAR, queue)
    return queue


def polish(ops, queue, moves, seed):
    rng = np.random.default_rng(seed)
    n = len(ops)
    pre, suc = graph(ops)
    cases = [(dict(PAR, **m), prices(ops, dict(PAR, **m)), w) for m, w in CASES]
    plain = [o["batch"] is None for o in ops]
    load = [o["lat"][1] if o["kind"] == "dma" else 1.0 for o in ops]

    def run(case, seq, use, at, old):
        par, cost, w = case
        free, last, lines = {e: 0.0 for e in ENGS + (None,)}, {}, 0.0
        fin, why, off, lin = [list(x) for x in old[1:]] if old else ([0.0] * n, [-1] * n, [0.0] * n, [0.0] * n)
        if at:
            lines = lin[seq[at - 1]]
            for i in seq[at - 1::-1]:
                if use[i] not in last and use[i] is not None:
                    last[use[i]], free[use[i]] = i, off[i]
                    if len(last) == len(ENGS):
                        break
        hop, same, kb = par["hop"], par["same"], par["kb"]
        for i in seq[at:]:
            e = use[i]
            r, y = free[e], last.get(e, -1)
            near = 0.0 if e == "pe" else same
            for d in pre[i]:
                x = fin[d] + (near if use[d] == e and plain[d] else hop)
                if x > r:
                    r, y = x, d
            c, lat = cost[i][e]
            why[i] = y
            r += c
            if e is not None:
                free[e], last[e], off[i] = r, i, r
                if lat:
                    wait = max(0.0, lines - r - 1.0)
                    lines = r + 1.0 + wait + kb * load[i]
                    r += wait
            fin[i], lin[i] = r + lat, lines
        return max(fin) / w, fin, why, off, lin

    def judge(seq, use, first=0, old=None, at=0):
        out = [None] * len(cases)
        for k in list(range(first, len(cases))) + list(range(first)):
            out[k] = run(cases[k], seq, use, at, old and old[k])
            if old and out[k][0] > old[k][0] + OPT["give"]:
                return 9.0, out
        v = [x[0] for x in out]
        return sum(v) / len(v) + 0.5 * max(v), out

    def shift(seq, a, b, back):
        part = seq[a:b + 1]
        if back:
            part = part[::-1]
        took, link = {part[-1]}, (pre if back else suc)
        for i in part[-2::-1]:
            if any(j in took for j in link[i]):
                took.add(i)
        if part[0] in took:
            return None
        part = [i for i in part if i in took] + [i for i in part if i not in took]
        return seq[:a] + (part[::-1] if back else part) + seq[b + 1:]
    seq = sorted(range(n), key=lambda i: (ops[i]["start"], i))
    use = [o["use"] for o in ops]
    cur = judge(seq, use)
    best = (cur[0], seq, use)
    for move in range(moves):
        case = int(rng.integers(len(cases)))
        fin, why = cur[1][case][1:3]
        i, pairs, sums = fin.index(max(fin)), [], [0.0]
        while why[i] >= 0:
            if use[why[i]] == use[i] and why[i] not in pre[i]:
                pairs.append((why[i], i))
                sums.append(sums[-1] + OPT["flat"] + cases[0][1][why[i]][use[i]][0])
            i = why[i]
        u, v = pairs[int(np.searchsorted(sums, rng.random() * sums[-1], "right")) - 1]
        new, now, kind = seq, use, rng.random()
        a, b = seq.index(u), seq.index(v)
        if kind < 0.1:
            free = [x for x in (u, v) if ops[x]["key"]]
            if not free:
                continue
            x = free[rng.integers(len(free))]
            now = list(use)
            now[x] = "act" if use[x] == "dve" else "dve"
        else:
            far = (0, 0, 1, 2, 4, 8)[rng.integers(6)]
            while far and (b < n - 1 if kind < 0.55 else a > 0):
                a, b = (a, b + 1) if kind < 0.55 else (a - 1, b)
                far -= use[seq[b if kind < 0.55 else a]] == use[u]
            new = shift(seq, a, b, kind < 0.55)
            if new is None:
                continue
        got = judge(new, now, case, cur[1], a)
        if got[0] <= cur[0] + OPT["heat"] * (1.0 - move / moves) * rng.random():
            cur, seq, use = got, new, now
            if cur[0] < best[0]:
                best = (cur[0], seq, use)
    queue = {e: [i for i in best[1] if best[2][i] == e] for e in ENGS}
    order(ops, PAR, queue)
    return queue


def plan():
    ops, members = build()
    queue = polish(ops, refine(ops, OPT["turns"], OPT["seed"]), OPT["moves"], OPT["seed"])
    count, tail = waits(ops, members, queue)
    return dict(ops=ops, members=members, queue=queue, count=count, tail=tail)


def shares(src, cores, topo):
    r = cores.index(src)
    dst = [cores[(r + d) % NR] for d in range(1, NR)]
    out, used = {}, set()
    for x in sorted(dst, key=lambda c: len(topo.engines(src, c))):
        can = [e for e in topo.engines(src, x) if e not in used]
        alike = [y for y in dst if y not in out and topo.mask(src, y) == topo.mask(src, x)]
        n = 1
        while 2 * n <= len(can) // len(alike):
            n *= 2
        out[x] = can[:n]
        used.update(can[:n])
    return [(x, out[x]) for x in dst]


def rank_program(g, core, T, topo):
    if T.rank_of(core) is None:
        return
    if not PLAN:
        PLAN.update(plan())
    ops, cores = PLAN["ops"], list(T.cores)
    mine = shares(core, cores, topo)
    arrive = sum(len(e) for c in cores if c != core for x, e in shares(c, cores, topo) if x == core)
    Q = {"pe": g.tensor, "dve": g.vector, "act": g.scalar, "pool": g, "sp": g.sync}

    def R(a):
        if not isinstance(a, tuple):
            return a
        if a[0] == "*":
            return R(a[1]).indirect(R(a[2]))
        if a[0] == "?":
            return R(a[3] if ops[a[1]]["use"] == "dve" else a[2])
        return T[a[0]][a[1] if len(a[1]) > 1 else a[1][0]]

    def total(bt):
        kind = ops[PLAN["members"][bt][0]]["kind"]
        if kind == "send":
            return sum(len(e) for x, e in mine)
        return arrive if kind == "recv" else 16 * len(PLAN["members"][bt])

    def activation(q, out, a, fn, scale, bias):
        if bias != 0.0:
            return q.activation(out, a, fn, bias=bias, scale=scale)
        if scale != 1.0:
            return q.activation(out, a, fn, scale=scale)
        return q.activation(out, a, fn)

    def either(q, e, out, a, scale, bias, fn):
        if e == "act":
            if fn == "sign":
                return activation(q, out, a, ACTF.Sigmoid, scale, bias)
            return activation(q, out, a, ACTF.Relu if fn else (ACTF.Identity if bias != 0.0 else ACTF.Copy), scale, bias)
        if fn == "sign":
            return q.tensor_scalar(out, a, -bias / scale, None, ALU.is_gt if scale > 0 else ALU.is_lt)
        if fn:
            return q.tensor_scalar(out, a, bias, 0.0, ALU.add, ALU.max)
        if bias != 0.0:
            return q.tensor_scalar(out, a, scale, bias, ALU.mult, ALU.add)
        return q.tensor_scalar(out, a, scale, None, ALU.mult) if scale != 1.0 else q.tensor_copy(out, a)

    for e in ENGS:
        q = Q[e]
        for i in PLAN["queue"][e]:
            o = ops[i]
            for d in o["we"]:
                q.wait_ge(T.sem["e_" + ops[d]["use"]], PLAN["count"][d])
            for bt in o["wb"]:
                q.wait_ge(T.sem["b%d" % bt], total(bt))
            k, a = o["kind"], o["args"]
            if k == "send":
                tr = []
                for d, (x, eng) in enumerate(mine):
                    rid, pid = topo.addr(x, core)
                    tr.append(RemoteDMATransfer(dst_ids=[DstId(rid=rid, pnc=pid)], dma_engine_mask=sum(1 << y for y in eng),
                                                remote_sem=T.sem["b%d" % a[2]], src=R(a[0]), dst=R(a[1][d])))
                q.remote_dma_fused(tr, local_sem=T.sem["b%d" % o["batch"]])
                continue
            if k == "dma":
                ins = q.dma_start(R(a[0]), R(a[1]), accum_op=ALU.add) if a[2] else q.dma_start(R(a[0]), R(a[1]))
                ins.then_inc(T.sem["b%d" % o["batch"]], 16)
                continue
            if k == "tt":
                ins = q.tensor_tensor(R(a[0]), R(a[1]), R(a[2]), a[3])
            elif k == "ts":
                if a[5] is None:
                    ins = q.tensor_scalar(R(a[0]), R(a[1]), R(a[2]), None, a[4])
                else:
                    ins = q.tensor_scalar(R(a[0]), R(a[1]), R(a[2]), R(a[3]), a[4], a[5])
            elif k == "scan" and a[3]:
                ins = q.tensor_tensor_scan(R(a[0]), R(a[1]), R(a[2]), 0.0, ALU.mult, ALU.add)
            elif k == "scan":
                ins = q.tensor_tensor_scan(R(a[0]), R(a[2]), R(a[1]), 0.0, ALU.max, ALU.mult)
            elif k == "ms":
                ins = q.memset(R(a[0]), a[1])
            elif k == "act":
                ins = activation(q, R(a[0]), R(a[1]), a[2], a[3], a[4])
            elif k == "aff":
                ins = either(q, e, R(a[0]), R(a[1]), a[2], a[3], a[4])
            elif k == "mm":
                ins = q.matmul(R(a[0]), R(a[1]), R(a[2]), a[3], a[4])
            elif k == "sel":
                ins = q.affine_select(R(a[0]), R(a[1]), a[2], a[3], a[4], a[5], a[6])
            elif SCRATCH[a[0][0]][2] == i32:
                ins = q.iota(R(a[0]), a[1], a[2], a[3])
            else:
                ins = q.iota(R(a[0]), a[1], a[2], a[3], allow_small_or_imprecise_dtypes=True)
            if i in PLAN["count"]:
                ins.then_inc(T.sem["e_" + e], 1)
    for bt in PLAN["tail"]:
        g.wait_ge(T.sem["b%d" % bt], total(bt))
